import numpy as np
import ml_dtypes


def mxq(x, axis, fmt="e4m3"):
    dtype, down = {"e4m3": (ml_dtypes.float8_e4m3fn, 7), "e5m2": (ml_dtypes.float8_e5m2, 14)}[fmt]
    v = np.moveaxis(np.asarray(x, np.float32).astype(ml_dtypes.bfloat16).astype(np.float64), axis, -1)
    blocks = v.reshape(v.shape[:-1] + (-1, 32))
    amax = np.abs(blocks).max(-1, keepdims=True)
    byte = np.maximum(np.where(amax > 0, np.frexp(amax)[1] - 1 + 127, 0) - down, 1)
    scale = np.exp2(byte - 127.0)
    codes = (blocks / scale).astype(np.float32).astype(dtype).astype(np.float64)
    return np.moveaxis((codes * scale).reshape(v.shape), -1, axis)


WIDE = False


def mx_kscale(k):
    if not WIDE:
        return np.ones(k)
    levels = np.array([10, -10, 5, -5, 0])
    if k % 512:
        return np.exp2(np.random.permutation(np.resize(levels, k // 32))).repeat(32)
    a = np.empty((k // 512, 16))
    for p in range(k // 512):
        a[p, :8] = np.random.permutation(np.resize(levels, 8))
        for g in range(8):
            far = levels[np.abs(levels - a[p, g]) >= 10]
            a[p, g + 8] = far[np.random.randint(len(far))]
    return np.exp2(a.ravel()).repeat(32)


def f64(x):
    return np.asarray(x).astype(np.float64)


def striped(idx):
    return np.tile(idx.reshape(-1, 16).T, (8, 1)).astype(np.uint16)


def unstriped(offs):
    return offs[:16].T.reshape(-1).astype(np.int64)


E2M1 = np.array([0.0, 0.5, 1.0, 1.5, 2.0, 3.0, 4.0, 6.0, -0.0, -0.5, -1.0, -1.5, -2.0, -3.0, -4.0, -6.0])


def pack_weight(w, fmt):
    k, n = w.shape
    w = f64(np.asarray(w, np.float32).astype(ml_dtypes.bfloat16)).reshape(k // 32, 32, n)
    amax = np.abs(w).max(1)
    if fmt == "e4m3":
        byte = np.frexp(amax)[1] - 1 + 127 - 7
    else:
        mant, ex = np.frexp(amax / 6.0)
        byte = np.where(mant > 0.5, ex, ex - 1) + 127
    byte = np.clip(np.where(amax > 0, byte, 1), 1, 254)
    scaled = (w * np.exp2(127.0 - byte)[:, None, :]).reshape(k, n).astype(np.float32)
    by_word = np.ascontiguousarray(scaled.reshape(k // 512, 128, 4, n).transpose(0, 1, 3, 2))
    if fmt == "e4m3":
        words = by_word.astype(ml_dtypes.float8_e4m3fn).view(np.uint8)
    else:
        c = by_word.astype(ml_dtypes.float4_e2m1fn).view(np.uint8) & 0xF
        words = (c[..., 0::2] | (c[..., 1::2] << 4)).reshape(k // 512, 128, 2 * n)
    return np.ascontiguousarray(words), np.ascontiguousarray(byte.astype(np.uint8).reshape(k // 512, 16, n))


def unpack_weight(words, scales, fmt):
    g, _, n = scales.shape
    words = np.ascontiguousarray(words).reshape(g, 128, n, -1)
    if fmt == "e4m3":
        vals = words.view(ml_dtypes.float8_e4m3fn).astype(np.float64)
    else:
        nib = np.empty((g, 128, n, 4), np.uint8)
        nib[..., 0::2] = words & 0xF
        nib[..., 1::2] = words >> 4
        vals = E2M1[nib]
    vals = vals * np.repeat(np.exp2(scales.astype(np.float64) - 127.0), 8, axis=1)[..., None]
    return vals.transpose(0, 1, 3, 2).reshape(g * 512, n)


def gelu(v):
    return 0.5 * v * (1.0 + np.tanh(np.sqrt(2.0 / np.pi) * (v + 0.044715 * v**3)))


K, T, S, H, T2, N = 1536, 4096, 1024, 512, 2048, 512

def setup_inputs():
    n = np.random.standard_normal
    s = mx_kscale(K)[:, None]
    u = mx_kscale(H)[:, None]
    tab_words, tab_scales = pack_weight(n((K, T)) * s, "e4m3")
    wk_words, wk_scales = pack_weight(n((K, H)) / np.sqrt(K) / s, "e2m1")
    return {
        "tab_words": tab_words, "tab_scales": tab_scales,
        "offs": striped(np.random.permutation(T)[:S]),
        "wk_words": wk_words, "wk_scales": wk_scales,
        "offs2": striped(np.random.permutation(T2)[:S]),
        "wgs": np.exp(0.3 * n((128, S))).astype(np.float32),
        "base": (n((H, T2)) * u).astype(np.float32),
        "wo": (n((H, N)) / np.sqrt(H) / u).astype(np.float32),
    }

def reference(tab_words, tab_scales, offs, wk_words, wk_scales, offs2, wgs, base, wo):
    v = unpack_weight(tab_words, tab_scales, "e4m3")[:, unstriped(offs)]
    wk = unpack_weight(wk_words, wk_scales, "e2m1")
    a = wk.T @ v
    h = np.sqrt(np.abs(a))
    page = np.zeros((H, T2))
    page[:, unstriped(offs2)] = np.tile(f64(wgs), (H // 128, 1)) * h
    z = f64(base) * (1.0 + page)
    zq = mxq(z, 0, "e4m3")
    woq = mxq(f64(wo), 0, "e4m3")
    return woq.T @ zq

@@ -1,0 +1,230 @@
+from contextlib import ExitStack
+
+import concourse.mybir as mybir
+
+K, T, S, H, T2, N = 1536, 4096, 1024, 512, 2048, 512
+FLOPS = 2 * K * H * S + 2 * H * N * T2
+
+F32 = mybir.dt.float32
+BF16 = mybir.dt.bfloat16
+I32 = mybir.dt.int32
+U32 = mybir.dt.uint32
+U16 = mybir.dt.uint16
+U8 = mybir.dt.uint8
+FP8X4 = mybir.dt.float8_e4m3fn_x4
+FP4X4 = mybir.dt.float4_e2m1fn_x4
+ACT = mybir.ActivationFunctionType
+MULT = mybir.AluOpType.mult
+
+P = 128
+PACK = 4
+PASSES = K // (P * PACK)
+HALF = 512
+CHUNK = 256
+
+
+def tile_list_kmer_locus_coverage_kernel(
+    tc, tab_words, tab_scales, offs, wk_words, wk_scales, offs2, wgs, base, wo, out
+):
+    nc = tc.nc
+    with ExitStack() as ctx:
+        keep = ctx.enter_context(tc.tile_pool(name="keep", bufs=1))
+        big = ctx.enter_context(tc.tile_pool(name="big", bufs=3))
+        ring = ctx.enter_context(tc.tile_pool(name="ring", bufs=3))
+        psum = ctx.enter_context(tc.psum_pool(name="psum", bufs=1))
+
+        idx = keep.tile([P, S // 16], U16, name="idx")
+        idx2 = keep.tile([P, S // 16], U16, name="idx2")
+        srows = keep.tile([P, T // 4], I32, name="srows", align_bytes=64)
+        planes = keep.tile([P, 4, S // 4], I32, name="planes", align_bytes=64)
+        wks_raw = keep.tile([P, PASSES, H // 4], I32, name="wks_raw", align_bytes=64)
+        wkw_raw = keep.tile([P, PASSES, H // 2], I32, name="wkw_raw", align_bytes=64)
+        pages = [keep.tile([P, T2], F32, name="page%d" % t, align_bytes=64) for t in range(PACK)]
+        one = keep.tile([P, 1], F32, name="one")
+        floor = keep.tile([P, 1], F32, name="floor")
+
+        nc.vector.memset(srows[:], 0)
+        nc.vector.memset(wks_raw[:], 0)
+        nc.vector.memset(one[:], 1.0)
+        nc.vector.memset(planes[:], 0)
+        for t in range(PACK):
+            nc.vector.memset(pages[t][:], 0.0)
+
+        words = [big.tile([P, T], I32, name="words%d" % a, tag="big", align_bytes=64) for a in range(PASSES)]
+
+        def load_words(a):
+            nc.sync.dma_start(words[a][:], tab_words[a].rearrange("p t i -> p (t i)").bitcast(I32))
+
+        nc.sync.dma_start(idx[:], offs)
+        load_words(0)
+        for a in range(PASSES):
+            nc.scalar.dma_start(srows[2 * a : P : 8, :], tab_scales[a].bitcast(I32))
+        for q in range(4):
+            nc.scalar.dma_start(
+                wks_raw[32 * q : 32 * q + 4, :, :],
+                wk_scales[:, 4 * q : 4 * q + 4, :].bitcast(I32).rearrange("a r c -> r a c"),
+            )
+        nc.scalar.activation(floor[:], one[:], ACT.Sqrt, scale=2.0**-116)
+        nc.sync.dma_start(wkw_raw[:], wk_words.bitcast(I32).rearrange("a p c -> p a c"))
+        load_words(1)
+        load_words(2)
+        nc.sync.dma_start(idx2[:], offs2)
+
+        gathered = [keep.tile([P, S], U32, name="gathered%d" % a, align_bytes=64) for a in range(PASSES)]
+        grows = keep.tile([P, S], U8, name="grows", align_bytes=64)
+        wkw = keep.tile([P, PASSES, 2 * H], U8, name="wkw", align_bytes=64)
+        wks = keep.tile([P, PASSES, H], U8, name="wks", align_bytes=64)
+
+        def gather_words(a, lo, hi):
+            nc.vector.tensor_copy(
+                gathered[a][:, lo:hi], words[a][:].bitcast(U32).indirect(idx[:, lo // 16 : hi // 16])
+            )
+
+        nc.vector.tensor_copy(grows[:], srows[:].bitcast(U8).indirect(idx[:]))
+        for q in range(4):
+            nc.scalar.dma_start(
+                planes[32 * q : 32 * q + 4, :, :], grows[32 * q : 32 * q + 32 : 2, :].bitcast(I32)
+            )
+        gather_words(0, 0, S)
+        nc.vector.tensor_copy(
+            wkw[:].bitcast(U16).rearrange("p a (t m) -> p a t m", t=PACK),
+            wkw_raw[:].bitcast(U16).rearrange("p a (m t) -> p a t m", t=PACK),
+        )
+        nc.vector.tensor_copy(
+            wks[:].rearrange("p a (t m) -> p a t m", t=PACK),
+            wks_raw[:].bitcast(U8).rearrange("p a (m t) -> p a t m", t=PACK),
+        )
+        gather_words(1, 0, S)
+        gather_words(2, 0, HALF)
+        gather_words(2, HALF, S)
+
+        wg = keep.tile([P, PACK, S], F32, name="wg")
+        wgs_by_plane = wgs.rearrange("(m t) j -> m t j", t=PACK)
+        for lo, hi in ((0, 1), (1, 2), (2, 4)):
+            for q in (0, 2, 1, 3):
+                nc.sync.dma_start(wg[32 * q : 32 * q + 32, lo:hi, :], wgs_by_plane[:, lo:hi, :])
+        wo_raw = keep.tile([P, PACK, N], F32, name="wo_raw")
+        nc.sync.dma_start(wo_raw[:], wo.rearrange("(p t) n -> p t n", t=PACK))
+        base_sb = keep.tile([P, PACK, T2], F32, name="base_sb")
+        base_by_plane = base.rearrange("(p t) j -> p t j", t=PACK)
+        for t in range(PACK):
+            nc.sync.dma_start(base_sb[:, t, :], base_by_plane[:, t, :])
+
+        banks = [[psum.tile([P, HALF], F32, name="acc%d%d" % (t, hf), tag="bank%d" % (2 * t + hf)) for hf in range(2)] for t in range(PACK)]
+        planes_u8 = planes[:].bitcast(U8)
+
+        def first_product(a, hf, t):
+            cols = slice(hf * HALF, (hf + 1) * HALF)
+            nc.tensor.matmul_mx(
+                out=banks[t][hf][:],
+                lhsT=wkw[:, a, 2 * P * t : 2 * P * (t + 1)].bitcast(FP4X4),
+                lhsT_scale=wks[:, a, P * t : P * (t + 1)],
+                rhs=gathered[a][:, cols].bitcast(FP8X4),
+                rhs_scale=planes_u8[:, a, cols],
+                start=(a == 0),
+                stop=(a == PASSES - 1),
+            )
+
+        for a in range(PASSES):
+            for hf in range(2):
+                for t in range(PACK):
+                    first_product(a, hf, t)
+
+        hs = keep.tile([P, PACK, S], F32, name="hs")
+        lifted = keep.tile([P, PACK, T2], F32, name="lifted")
+
+        def root(t, lo, hi):
+            hf = lo // HALF
+            mag = ring.tile([P, hi - lo], F32, name="mag")
+            nc.scalar.activation(mag[:], banks[t][hf][:, lo - hf * HALF : hi - hf * HALF], ACT.Abs)
+            nc.scalar.activation(hs[:, t, lo:hi], mag[:], ACT.Sqrt, bias=floor[:])
+
+        def scatter(t, lo, hi):
+            nc.vector.tensor_tensor(
+                pages[t][:].indirect(idx2[:, lo // 16 : hi // 16]), hs[:, t, lo:hi], wg[:, t, lo:hi], MULT
+            )
+
+        def lift(t, lo, hi):
+            nc.scalar.activation(lifted[:, t, lo:hi], pages[t][:, lo:hi], ACT.Copy, bias=1.0)
+
+        first = 256
+        root(0, 0, first)
+        scatter(0, 0, first)
+        root(1, 0, first)
+        scatter(1, 0, first)
+        for t in (0, 1):
+            root(t, first, HALF)
+            root(t, HALF, S)
+            scatter(t, first, S)
+        for t in (2, 3):
+            root(t, 0, HALF)
+            root(t, HALF, S)
+        lift(0, 0, T2)
+        wo_bf = keep.tile([P, N, PACK], BF16, name="wo_bf", align_bytes=64)
+        wo_codes = keep.tile([P, N], U32, name="wo_codes", align_bytes=64)
+        wo_scales = keep.tile([P, N], U8, name="wo_scales", align_bytes=64)
+        nc.scalar.copy(wo_bf[:], wo_raw[:].rearrange("p t n -> p n t"))
+        scatter(2, 0, S)
+        lift(1, 0, T2)
+        nc.vector.quantize_mx(
+            out=wo_codes[:].bitcast(FP8X4), scales=wo_scales[:], in_=wo_bf[:].rearrange("p n t -> p (n t)")
+        )
+        scatter(3, 0, S)
+        lift(2, 0, T2)
+
+        out_view = out.rearrange("(m p) j -> p m j", p=P)
+        chunks = T2 // CHUNK
+        zs = {}
+        zq = {}
+
+        def make_z(c):
+            cols = slice(c * CHUNK, (c + 1) * CHUNK)
+            z = ring.tile([P, CHUNK, PACK], BF16, name="z", align_bytes=64)
+            nc.vector.tensor_tensor(
+                z[:].rearrange("p (c i) t -> p c t i", i=2),
+                lifted[:, :, cols].rearrange("p t (c i) -> p c t i", i=2),
+                base_sb[:, :, cols].rearrange("p t (c i) -> p c t i", i=2),
+                MULT,
+            )
+            zs[c] = z
+
+        def quantise_z(c):
+            codes = ring.tile([P, CHUNK], U32, name="z_codes", align_bytes=64)
+            scales = ring.tile([P, CHUNK], U8, name="z_scales", align_bytes=64)
+            nc.vector.quantize_mx(
+                out=codes[:].bitcast(FP8X4), scales=scales[:], in_=zs[c][:].rearrange("p j t -> p (j t)")
+            )
+            zq[c] = (codes, scales)
+
+        def second_product(c):
+            codes, scales = zq[c]
+            staged = big.tile([P, PACK, CHUNK], F32, name="staged", tag="big", align_bytes=64)
+            for pair in range(2):
+                acc = psum.tile([P, 2, CHUNK], F32, name="track", tag="bank%d" % ((2 * c + pair) % 8))
+                for u in range(2):
+                    m = 2 * pair + u
+                    nc.tensor.matmul_mx(
+                        out=acc[:, u, :],
+                        lhsT=wo_codes[:, P * m : P * (m + 1)].bitcast(FP8X4),
+                        lhsT_scale=wo_scales[:, P * m : P * (m + 1)],
+                        rhs=codes[:].bitcast(FP8X4),
+                        rhs_scale=scales[:],
+                        start=True,
+                        stop=True,
+                    )
+                if c == chunks - 1 and pair == 1:
+                    nc.vector.tensor_copy(staged[:, 2 * pair : 2 * pair + 2, :], acc[:])
+                else:
+                    nc.scalar.copy(staged[:, 2 * pair : 2 * pair + 2, :], acc[:])
+            nc.sync.dma_start(out_view[:, :, c * CHUNK : (c + 1) * CHUNK], staged[:])
+
+        lift(3, 0, CHUNK)
+        lift(3, CHUNK, 2 * CHUNK)
+        make_z(0)
+        for c in range(chunks):
+            if c + 2 < chunks:
+                lift(3, (c + 2) * CHUNK, (c + 3) * CHUNK)
+            if c + 1 < chunks:
+                make_z(c + 1)
+            quantise_z(c)
+            second_product(c)

@@ -29,46 +29,49 @@ def tile_list_kmer_locus_coverage_kernel(
     nc = tc.nc
     with ExitStack() as ctx:
         keep = ctx.enter_context(tc.tile_pool(name="keep", bufs=1))
-        big = ctx.enter_context(tc.tile_pool(name="big", bufs=3))
+        big = ctx.enter_context(tc.tile_pool(name="big", bufs=1))
+        stage = ctx.enter_context(tc.tile_pool(name="stage", bufs=4))
         ring = ctx.enter_context(tc.tile_pool(name="ring", bufs=3))
         psum = ctx.enter_context(tc.psum_pool(name="psum", bufs=1))
 
         idx = keep.tile([P, S // 16], U16, name="idx")
         idx2 = keep.tile([P, S // 16], U16, name="idx2")
-        srows = keep.tile([P, T // 4], I32, name="srows", align_bytes=64)
+        srows = big.tile([P, T // 4], I32, name="srows", tag="a", align_bytes=64)
         planes = keep.tile([P, 4, S // 4], I32, name="planes", align_bytes=64)
         wks_raw = keep.tile([P, PASSES, H // 4], I32, name="wks_raw", align_bytes=64)
-        wkw_raw = keep.tile([P, PASSES, H // 2], I32, name="wkw_raw", align_bytes=64)
+        wkw_raw = big.tile([P, PASSES, H // 2], I32, name="wkw_raw", tag="d", align_bytes=64)
         pages = [keep.tile([P, T2], F32, name="page%d" % t, align_bytes=64) for t in range(PACK)]
-        one = keep.tile([P, 1], F32, name="one")
+        one = big.tile([P, 1], F32, name="one", tag="c", align_bytes=64)
         floor = keep.tile([P, 1], F32, name="floor")
 
-        nc.vector.memset(srows[:], 0)
-        nc.vector.memset(wks_raw[:], 0)
-        nc.vector.memset(one[:], 1.0)
-        nc.vector.memset(planes[:], 0)
-        for t in range(PACK):
-            nc.vector.memset(pages[t][:], 0.0)
-
-        words = [big.tile([P, T], I32, name="words%d" % a, tag="big", align_bytes=64) for a in range(PASSES)]
+        words = [big.tile([P, T], I32, name="words0", tag="b", align_bytes=64)]
 
         def load_words(a):
             nc.sync.dma_start(words[a][:], tab_words[a].rearrange("p t i -> p (t i)").bitcast(I32))
 
         nc.sync.dma_start(idx[:], offs)
+        scale_rows = tab_scales.bitcast(I32).rearrange("a q c -> q a c")
+        for u in range(2):
+            nc.sync.dma_start(srows[32 + u : 96 : 2, :], scale_rows[:, u : u + 2, :])
         load_words(0)
-        for a in range(PASSES):
-            nc.scalar.dma_start(srows[2 * a : P : 8, :], tab_scales[a].bitcast(I32))
+        nc.sync.dma_start(wkw_raw[:], wk_words.bitcast(I32).rearrange("a p c -> p a c"))
+        nc.sync.dma_start(idx2[:], offs2)
+
+        nc.vector.memset(one[:], 1.0)
+        nc.gpsimd.memset(wks_raw[:], 0)
+        nc.gpsimd.memset(srows[0:32, :], 0)
+        nc.gpsimd.memset(srows[96:128, :], 0)
+        nc.gpsimd.memset(planes[:], 0)
+        for t in range(PACK):
+            nc.gpsimd.memset(pages[t][:], 0.0)
         for q in range(4):
             nc.scalar.dma_start(
                 wks_raw[32 * q : 32 * q + 4, :, :],
                 wk_scales[:, 4 * q : 4 * q + 4, :].bitcast(I32).rearrange("a r c -> r a c"),
             )
         nc.scalar.activation(floor[:], one[:], ACT.Sqrt, scale=2.0**-116)
-        nc.sync.dma_start(wkw_raw[:], wk_words.bitcast(I32).rearrange("a p c -> p a c"))
+        words.append(big.tile([P, T], I32, name="words1", tag="c", align_bytes=64))
         load_words(1)
-        load_words(2)
-        nc.sync.dma_start(idx2[:], offs2)
 
         gathered = [keep.tile([P, S], U32, name="gathered%d" % a, align_bytes=64) for a in range(PASSES)]
         grows = keep.tile([P, S], U8, name="grows", align_bytes=64)
@@ -83,8 +86,10 @@ def tile_list_kmer_locus_coverage_kernel(
         nc.vector.tensor_copy(grows[:], srows[:].bitcast(U8).indirect(idx[:]))
         for q in range(4):
             nc.scalar.dma_start(
-                planes[32 * q : 32 * q + 4, :, :], grows[32 * q : 32 * q + 32 : 2, :].bitcast(I32)
+                planes[32 * q : 32 * q + 4, :, :], grows[32 + 16 * q : 48 + 16 * q, :].bitcast(I32)
             )
+        words.append(big.tile([P, T], I32, name="words2", tag="a", align_bytes=64))
+        load_words(2)
         gather_words(0, 0, S)
         nc.vector.tensor_copy(
             wkw[:].bitcast(U16).rearrange("p a (t m) -> p a t m", t=PACK),
@@ -98,17 +103,18 @@ def tile_list_kmer_locus_coverage_kernel(
         gather_words(2, 0, HALF)
         gather_words(2, HALF, S)
 
-        wg = keep.tile([P, PACK, S], F32, name="wg")
+        first = 256
+        wg = big.tile([P, PACK, S], F32, name="wg", tag="b", align_bytes=64)
         wgs_by_plane = wgs.rearrange("(m t) j -> m t j", t=PACK)
-        for lo, hi in ((0, 1), (1, 2), (2, 4)):
+        for ts, js in ((slice(0, 2), slice(0, first)), (slice(0, 2), slice(first, S)), (slice(2, 4), slice(0, S))):
             for q in (0, 2, 1, 3):
-                nc.sync.dma_start(wg[32 * q : 32 * q + 32, lo:hi, :], wgs_by_plane[:, lo:hi, :])
-        wo_raw = keep.tile([P, PACK, N], F32, name="wo_raw")
+                nc.sync.dma_start(wg[32 * q : 32 * q + 32, ts, js], wgs_by_plane[:, ts, js])
+        wo_raw = big.tile([P, PACK, N], F32, name="wo_raw", tag="d", align_bytes=64)
         nc.sync.dma_start(wo_raw[:], wo.rearrange("(p t) n -> p t n", t=PACK))
-        base_sb = keep.tile([P, PACK, T2], F32, name="base_sb")
         base_by_plane = base.rearrange("(p t) j -> p t j", t=PACK)
-        for t in range(PACK):
-            nc.sync.dma_start(base_sb[:, t, :], base_by_plane[:, t, :])
+        base_sb = [big.tile([P, PACK, T2 // 2], F32, name="base%d" % u, tag="ca"[u], align_bytes=64) for u in range(2)]
+        for u in range(2):
+            nc.sync.dma_start(base_sb[u][:], base_by_plane[:, :, u * (T2 // 2) : (u + 1) * (T2 // 2)])
 
         banks = [[psum.tile([P, HALF], F32, name="acc%d%d" % (t, hf), tag="bank%d" % (2 * t + hf)) for hf in range(2)] for t in range(PACK)]
         planes_u8 = planes[:].bitcast(U8)
@@ -120,7 +126,7 @@ def tile_list_kmer_locus_coverage_kernel(
                 lhsT=wkw[:, a, 2 * P * t : 2 * P * (t + 1)].bitcast(FP4X4),
                 lhsT_scale=wks[:, a, P * t : P * (t + 1)],
                 rhs=gathered[a][:, cols].bitcast(FP8X4),
-                rhs_scale=planes_u8[:, a, cols],
+                rhs_scale=planes_u8[:, (0, 2, 3)[a], cols],
                 start=(a == 0),
                 stop=(a == PASSES - 1),
             )
@@ -147,7 +153,6 @@ def tile_list_kmer_locus_coverage_kernel(
         def lift(t, lo, hi):
             nc.scalar.activation(lifted[:, t, lo:hi], pages[t][:, lo:hi], ACT.Copy, bias=1.0)
 
-        first = 256
         root(0, 0, first)
         scatter(0, 0, first)
         root(1, 0, first)
@@ -183,7 +188,7 @@ def tile_list_kmer_locus_coverage_kernel(
             nc.vector.tensor_tensor(
                 z[:].rearrange("p (c i) t -> p c t i", i=2),
                 lifted[:, :, cols].rearrange("p t (c i) -> p c t i", i=2),
-                base_sb[:, :, cols].rearrange("p t (c i) -> p c t i", i=2),
+                base_sb[c * CHUNK // (T2 // 2)][:, :, (c * CHUNK) % (T2 // 2) : (c * CHUNK) % (T2 // 2) + CHUNK].rearrange("p t (c i) -> p c t i", i=2),
                 MULT,
             )
             zs[c] = z
@@ -198,7 +203,7 @@ def tile_list_kmer_locus_coverage_kernel(
 
         def second_product(c):
             codes, scales = zq[c]
-            staged = big.tile([P, PACK, CHUNK], F32, name="staged", tag="big", align_bytes=64)
+            staged = stage.tile([P, PACK, CHUNK], F32, name="staged", align_bytes=64)
             for pair in range(2):
                 acc = psum.tile([P, 2, CHUNK], F32, name="track", tag="bank%d" % ((2 * c + pair) % 8))
                 for u in range(2):

@@ -37,10 +37,10 @@ def tile_list_kmer_locus_coverage_kernel(
         idx = keep.tile([P, S // 16], U16, name="idx")
         idx2 = keep.tile([P, S // 16], U16, name="idx2")
         srows = big.tile([P, T // 4], I32, name="srows", tag="a", align_bytes=64)
-        planes = keep.tile([P, 4, S // 4], I32, name="planes", align_bytes=64)
+        planes = big.tile([P, 4, S // 4], I32, name="planes", tag="e", align_bytes=64)
         wks_raw = keep.tile([P, PASSES, H // 4], I32, name="wks_raw", align_bytes=64)
         wkw_raw = big.tile([P, PASSES, H // 2], I32, name="wkw_raw", tag="d", align_bytes=64)
-        pages = [keep.tile([P, T2], F32, name="page%d" % t, align_bytes=64) for t in range(PACK)]
+        pages = [keep.tile([P, T2], F32, name="page%d" % t, align_bytes=64) for t in range(2)]
         one = big.tile([P, 1], F32, name="one", tag="c", align_bytes=64)
         floor = keep.tile([P, 1], F32, name="floor")
 
@@ -52,18 +52,16 @@ def tile_list_kmer_locus_coverage_kernel(
         nc.sync.dma_start(idx[:], offs)
         scale_rows = tab_scales.bitcast(I32).rearrange("a q c -> q a c")
         for u in range(2):
-            nc.sync.dma_start(srows[32 + u : 96 : 2, :], scale_rows[:, u : u + 2, :])
-        load_words(0)
+            nc.sync.dma_start(srows[32 + u : 96 : 2, :], scale_rows[:, u : 3 : 2 - u, :])
         nc.sync.dma_start(wkw_raw[:], wk_words.bitcast(I32).rearrange("a p c -> p a c"))
+        load_words(0)
         nc.sync.dma_start(idx2[:], offs2)
 
         nc.vector.memset(one[:], 1.0)
-        nc.gpsimd.memset(wks_raw[:], 0)
-        nc.gpsimd.memset(srows[0:32, :], 0)
-        nc.gpsimd.memset(srows[96:128, :], 0)
-        nc.gpsimd.memset(planes[:], 0)
-        for t in range(PACK):
-            nc.gpsimd.memset(pages[t][:], 0.0)
+        nc.vector.memset(wks_raw[:], 0)
+        nc.vector.memset(srows[0:32, :], 0)
+        nc.vector.memset(srows[96:128, :], 0)
+        nc.vector.memset(planes[:, 0:PASSES, :], 0)
         for q in range(4):
             nc.scalar.dma_start(
                 wks_raw[32 * q : 32 * q + 4, :, :],
@@ -73,7 +71,7 @@ def tile_list_kmer_locus_coverage_kernel(
         words.append(big.tile([P, T], I32, name="words1", tag="c", align_bytes=64))
         load_words(1)
 
-        gathered = [keep.tile([P, S], U32, name="gathered%d" % a, align_bytes=64) for a in range(PASSES)]
+        gathered = [big.tile([P, S], U32, name="gathered%d" % a, tag="fgh"[a], align_bytes=64) for a in range(PASSES)]
         grows = keep.tile([P, S], U8, name="grows", align_bytes=64)
         wkw = keep.tile([P, PASSES, 2 * H], U8, name="wkw", align_bytes=64)
         wks = keep.tile([P, PASSES, H], U8, name="wks", align_bytes=64)
@@ -90,7 +88,6 @@ def tile_list_kmer_locus_coverage_kernel(
             )
         words.append(big.tile([P, T], I32, name="words2", tag="a", align_bytes=64))
         load_words(2)
-        gather_words(0, 0, S)
         nc.vector.tensor_copy(
             wkw[:].bitcast(U16).rearrange("p a (t m) -> p a t m", t=PACK),
             wkw_raw[:].bitcast(U16).rearrange("p a (m t) -> p a t m", t=PACK),
@@ -99,6 +96,7 @@ def tile_list_kmer_locus_coverage_kernel(
             wks[:].rearrange("p a (t m) -> p a t m", t=PACK),
             wks_raw[:].bitcast(U8).rearrange("p a (m t) -> p a t m", t=PACK),
         )
+        gather_words(0, 0, S)
         gather_words(1, 0, S)
         gather_words(2, 0, HALF)
         gather_words(2, HALF, S)
@@ -126,15 +124,19 @@ def tile_list_kmer_locus_coverage_kernel(
                 lhsT=wkw[:, a, 2 * P * t : 2 * P * (t + 1)].bitcast(FP4X4),
                 lhsT_scale=wks[:, a, P * t : P * (t + 1)],
                 rhs=gathered[a][:, cols].bitcast(FP8X4),
-                rhs_scale=planes_u8[:, (0, 2, 3)[a], cols],
+                rhs_scale=planes_u8[:, a, cols],
                 start=(a == 0),
                 stop=(a == PASSES - 1),
             )
 
-        for a in range(PASSES):
-            for hf in range(2):
-                for t in range(PACK):
-                    first_product(a, hf, t)
+        for hf in range(2):
+            for t in range(PACK):
+                first_product(0, hf, t)
+        for ts in ((0, 1), (2, 3)):
+            for a in (1, 2):
+                for hf in range(2):
+                    for t in ts:
+                        first_product(a, hf, t)
 
         hs = keep.tile([P, PACK, S], F32, name="hs")
         lifted = keep.tile([P, PACK, T2], F32, name="lifted")
@@ -153,6 +155,11 @@ def tile_list_kmer_locus_coverage_kernel(
         def lift(t, lo, hi):
             nc.scalar.activation(lifted[:, t, lo:hi], pages[t][:, lo:hi], ACT.Copy, bias=1.0)
 
+        for t in range(2):
+            nc.vector.memset(pages[t][:], 0.0)
+        for t in (2, 3):
+            pages.append(big.tile([P, T2], F32, name="page%d" % t, tag="he"[t - 2], align_bytes=64))
+            nc.gpsimd.memset(pages[t][:], 0.0)
         root(0, 0, first)
         scatter(0, 0, first)
         root(1, 0, first)
@@ -171,31 +178,34 @@ def tile_list_kmer_locus_coverage_kernel(
         nc.scalar.copy(wo_bf[:], wo_raw[:].rearrange("p t n -> p n t"))
         scatter(2, 0, S)
         lift(1, 0, T2)
+        scatter(3, 0, S)
         nc.vector.quantize_mx(
             out=wo_codes[:].bitcast(FP8X4), scales=wo_scales[:], in_=wo_bf[:].rearrange("p n t -> p (n t)")
         )
-        scatter(3, 0, S)
         lift(2, 0, T2)
 
         out_view = out.rearrange("(m p) j -> p m j", p=P)
-        chunks = T2 // CHUNK
+        widths = [CHUNK] * 7 + [CHUNK // 2] * 2
+        starts = [sum(widths[:c]) for c in range(len(widths))]
+        chunks = len(widths)
         zs = {}
         zq = {}
 
         def make_z(c):
-            cols = slice(c * CHUNK, (c + 1) * CHUNK)
-            z = ring.tile([P, CHUNK, PACK], BF16, name="z", align_bytes=64)
+            lo, w = starts[c], widths[c]
+            blo = lo % (T2 // 2)
+            z = ring.tile([P, w, PACK], BF16, name="z", align_bytes=64)
             nc.vector.tensor_tensor(
                 z[:].rearrange("p (c i) t -> p c t i", i=2),
-                lifted[:, :, cols].rearrange("p t (c i) -> p c t i", i=2),
-                base_sb[c * CHUNK // (T2 // 2)][:, :, (c * CHUNK) % (T2 // 2) : (c * CHUNK) % (T2 // 2) + CHUNK].rearrange("p t (c i) -> p c t i", i=2),
+                lifted[:, :, lo : lo + w].rearrange("p t (c i) -> p c t i", i=2),
+                base_sb[lo // (T2 // 2)][:, :, blo : blo + w].rearrange("p t (c i) -> p c t i", i=2),
                 MULT,
             )
             zs[c] = z
 
         def quantise_z(c):
-            codes = ring.tile([P, CHUNK], U32, name="z_codes", align_bytes=64)
-            scales = ring.tile([P, CHUNK], U8, name="z_scales", align_bytes=64)
+            codes = ring.tile([P, widths[c]], U32, name="z_codes", align_bytes=64)
+            scales = ring.tile([P, widths[c]], U8, name="z_scales", align_bytes=64)
             nc.vector.quantize_mx(
                 out=codes[:].bitcast(FP8X4), scales=scales[:], in_=zs[c][:].rearrange("p j t -> p (j t)")
             )
@@ -203,9 +213,10 @@ def tile_list_kmer_locus_coverage_kernel(
 
         def second_product(c):
             codes, scales = zq[c]
-            staged = stage.tile([P, PACK, CHUNK], F32, name="staged", align_bytes=64)
+            lo, w = starts[c], widths[c]
+            staged = stage.tile([P, PACK, w], F32, name="staged", align_bytes=64)
             for pair in range(2):
-                acc = psum.tile([P, 2, CHUNK], F32, name="track", tag="bank%d" % ((2 * c + pair) % 8))
+                acc = psum.tile([P, 2, w], F32, name="track", tag="bank%d" % ((2 * c + pair) % 8))
                 for u in range(2):
                     m = 2 * pair + u
                     nc.tensor.matmul_mx(
@@ -221,14 +232,17 @@ def tile_list_kmer_locus_coverage_kernel(
                     nc.vector.tensor_copy(staged[:, 2 * pair : 2 * pair + 2, :], acc[:])
                 else:
                     nc.scalar.copy(staged[:, 2 * pair : 2 * pair + 2, :], acc[:])
-            nc.sync.dma_start(out_view[:, :, c * CHUNK : (c + 1) * CHUNK], staged[:])
+            nc.sync.dma_start(out_view[:, :, lo : lo + w], staged[:])
 
-        lift(3, 0, CHUNK)
-        lift(3, CHUNK, 2 * CHUNK)
+        def lift_last(c):
+            lift(3, starts[c], starts[c] + widths[c])
+
+        lift_last(0)
+        lift_last(1)
         make_z(0)
         for c in range(chunks):
             if c + 2 < chunks:
-                lift(3, (c + 2) * CHUNK, (c + 3) * CHUNK)
+                lift_last(c + 2)
             if c + 1 < chunks:
                 make_z(c + 1)
             quantise_z(c)

@@ -37,10 +37,10 @@ def tile_list_kmer_locus_coverage_kernel(
         idx = keep.tile([P, S // 16], U16, name="idx")
         idx2 = keep.tile([P, S // 16], U16, name="idx2")
         srows = big.tile([P, T // 4], I32, name="srows", tag="a", align_bytes=64)
-        planes = big.tile([P, 4, S // 4], I32, name="planes", tag="e", align_bytes=64)
-        wks_raw = keep.tile([P, PASSES, H // 4], I32, name="wks_raw", align_bytes=64)
+        planes = keep.tile([P, 4, S // 4], I32, name="planes", align_bytes=64)
+        wks_raw = big.tile([P, PASSES, H // 4], I32, name="wks_raw", tag="e", align_bytes=64)
         wkw_raw = big.tile([P, PASSES, H // 2], I32, name="wkw_raw", tag="d", align_bytes=64)
-        pages = [keep.tile([P, T2], F32, name="page%d" % t, align_bytes=64) for t in range(2)]
+        pages = [keep.tile([P, T2], F32, name="page0", align_bytes=64)]
         one = big.tile([P, 1], F32, name="one", tag="c", align_bytes=64)
         floor = keep.tile([P, 1], F32, name="floor")
 
@@ -83,7 +83,7 @@ def tile_list_kmer_locus_coverage_kernel(
 
         nc.vector.tensor_copy(grows[:], srows[:].bitcast(U8).indirect(idx[:]))
         for q in range(4):
-            nc.scalar.dma_start(
+            nc.sync.dma_start(
                 planes[32 * q : 32 * q + 4, :, :], grows[32 + 16 * q : 48 + 16 * q, :].bitcast(I32)
             )
         words.append(big.tile([P, T], I32, name="words2", tag="a", align_bytes=64))
@@ -104,15 +104,16 @@ def tile_list_kmer_locus_coverage_kernel(
         first = 256
         wg = big.tile([P, PACK, S], F32, name="wg", tag="b", align_bytes=64)
         wgs_by_plane = wgs.rearrange("(m t) j -> m t j", t=PACK)
-        for ts, js in ((slice(0, 2), slice(0, first)), (slice(0, 2), slice(first, S)), (slice(2, 4), slice(0, S))):
+        for ts, js in (
+            (slice(0, 2), slice(0, first)),
+            (slice(0, 1), slice(first, S)),
+            (slice(1, 2), slice(first, S)),
+            (slice(2, 4), slice(0, S)),
+        ):
             for q in (0, 2, 1, 3):
                 nc.sync.dma_start(wg[32 * q : 32 * q + 32, ts, js], wgs_by_plane[:, ts, js])
-        wo_raw = big.tile([P, PACK, N], F32, name="wo_raw", tag="d", align_bytes=64)
+        wo_raw = big.tile([P, PACK, N], F32, name="wo_raw", tag="f", align_bytes=64)
         nc.sync.dma_start(wo_raw[:], wo.rearrange("(p t) n -> p t n", t=PACK))
-        base_by_plane = base.rearrange("(p t) j -> p t j", t=PACK)
-        base_sb = [big.tile([P, PACK, T2 // 2], F32, name="base%d" % u, tag="ca"[u], align_bytes=64) for u in range(2)]
-        for u in range(2):
-            nc.sync.dma_start(base_sb[u][:], base_by_plane[:, :, u * (T2 // 2) : (u + 1) * (T2 // 2)])
 
         banks = [[psum.tile([P, HALF], F32, name="acc%d%d" % (t, hf), tag="bank%d" % (2 * t + hf)) for hf in range(2)] for t in range(PACK)]
         planes_u8 = planes[:].bitcast(U8)
@@ -129,11 +130,8 @@ def tile_list_kmer_locus_coverage_kernel(
                 stop=(a == PASSES - 1),
             )
 
-        for hf in range(2):
-            for t in range(PACK):
-                first_product(0, hf, t)
         for ts in ((0, 1), (2, 3)):
-            for a in (1, 2):
+            for a in range(PASSES):
                 for hf in range(2):
                     for t in ts:
                         first_product(a, hf, t)
@@ -155,10 +153,11 @@ def tile_list_kmer_locus_coverage_kernel(
         def lift(t, lo, hi):
             nc.scalar.activation(lifted[:, t, lo:hi], pages[t][:, lo:hi], ACT.Copy, bias=1.0)
 
-        for t in range(2):
-            nc.vector.memset(pages[t][:], 0.0)
+        pages.append(big.tile([P, T2], F32, name="page1", tag="c", align_bytes=64))
+        nc.gpsimd.memset(pages[0][:], 0.0)
+        nc.vector.memset(pages[1][:], 0.0)
         for t in (2, 3):
-            pages.append(big.tile([P, T2], F32, name="page%d" % t, tag="he"[t - 2], align_bytes=64))
+            pages.append(big.tile([P, T2], F32, name="page%d" % t, tag="de"[t - 2], align_bytes=64))
             nc.gpsimd.memset(pages[t][:], 0.0)
         root(0, 0, first)
         scatter(0, 0, first)
@@ -176,6 +175,11 @@ def tile_list_kmer_locus_coverage_kernel(
         wo_codes = keep.tile([P, N], U32, name="wo_codes", align_bytes=64)
         wo_scales = keep.tile([P, N], U8, name="wo_scales", align_bytes=64)
         nc.scalar.copy(wo_bf[:], wo_raw[:].rearrange("p t n -> p n t"))
+        base_by_plane = base.rearrange("(p t) j -> p t j", t=PACK)
+        base_sb = [big.tile([P, PACK, T2 // 2], F32, name="base%d" % u, tag="ga"[u], align_bytes=64) for u in range(2)]
+        for u in range(2):
+            nc.sync.dma_start(base_sb[u][:], base_by_plane[:, :, u * (T2 // 2) : (u + 1) * (T2 // 2)])
+
         scatter(2, 0, S)
         lift(1, 0, T2)
         scatter(3, 0, S)
@@ -185,7 +189,7 @@ def tile_list_kmer_locus_coverage_kernel(
         lift(2, 0, T2)
 
         out_view = out.rearrange("(m p) j -> p m j", p=P)
-        widths = [CHUNK] * 7 + [CHUNK // 2] * 2
+        widths = [CHUNK] * 8
         starts = [sum(widths[:c]) for c in range(len(widths))]
         chunks = len(widths)
         zs = {}
@@ -232,7 +236,12 @@ def tile_list_kmer_locus_coverage_kernel(
                     nc.vector.tensor_copy(staged[:, 2 * pair : 2 * pair + 2, :], acc[:])
                 else:
                     nc.scalar.copy(staged[:, 2 * pair : 2 * pair + 2, :], acc[:])
-            nc.sync.dma_start(out_view[:, :, lo : lo + w], staged[:])
+                if c == chunks - 1:
+                    nc.sync.dma_start(
+                        out_view[:, 2 * pair : 2 * pair + 2, lo : lo + w], staged[:, 2 * pair : 2 * pair + 2, :]
+                    )
+            if c < chunks - 1:
+                nc.sync.dma_start(out_view[:, :, lo : lo + w], staged[:])
 
         def lift_last(c):
             lift(3, starts[c], starts[c] + widths[c])

@@ -38,9 +38,9 @@ def tile_list_kmer_locus_coverage_kernel(
         idx2 = keep.tile([P, S // 16], U16, name="idx2")
         srows = big.tile([P, T // 4], I32, name="srows", tag="a", align_bytes=64)
         planes = keep.tile([P, 4, S // 4], I32, name="planes", align_bytes=64)
-        wks_raw = big.tile([P, PASSES, H // 4], I32, name="wks_raw", tag="e", align_bytes=64)
-        wkw_raw = big.tile([P, PASSES, H // 2], I32, name="wkw_raw", tag="d", align_bytes=64)
-        pages = [keep.tile([P, T2], F32, name="page0", align_bytes=64)]
+        wk_raw = big.tile([P, PASSES * (H // 2 + H // 4)], I32, name="wk_raw", tag="d", align_bytes=64)
+        wkw_raw = wk_raw[:, 0 : PASSES * (H // 2)]
+        wks_raw = wk_raw[:, PASSES * (H // 2) :]
         one = big.tile([P, 1], F32, name="one", tag="c", align_bytes=64)
         floor = keep.tile([P, 1], F32, name="floor")
 
@@ -53,18 +53,18 @@ def tile_list_kmer_locus_coverage_kernel(
         scale_rows = tab_scales.bitcast(I32).rearrange("a q c -> q a c")
         for u in range(2):
             nc.sync.dma_start(srows[32 + u : 96 : 2, :], scale_rows[:, u : 3 : 2 - u, :])
-        nc.sync.dma_start(wkw_raw[:], wk_words.bitcast(I32).rearrange("a p c -> p a c"))
+        nc.sync.dma_start(wkw_raw.rearrange("p (a c) -> p a c", a=PASSES), wk_words.bitcast(I32).rearrange("a p c -> p a c"))
         load_words(0)
         nc.sync.dma_start(idx2[:], offs2)
 
         nc.vector.memset(one[:], 1.0)
-        nc.vector.memset(wks_raw[:], 0)
-        nc.vector.memset(srows[0:32, :], 0)
-        nc.vector.memset(srows[96:128, :], 0)
-        nc.vector.memset(planes[:, 0:PASSES, :], 0)
+        nc.gpsimd.memset(wks_raw, 0)
+        nc.gpsimd.memset(srows[0:32, :], 0)
+        nc.gpsimd.memset(srows[96:128, :], 0)
+        nc.gpsimd.memset(planes[:, 0:PASSES, :], 0)
         for q in range(4):
             nc.scalar.dma_start(
-                wks_raw[32 * q : 32 * q + 4, :, :],
+                wks_raw[32 * q : 32 * q + 4, :].rearrange("p (a c) -> p a c", a=PASSES),
                 wk_scales[:, 4 * q : 4 * q + 4, :].bitcast(I32).rearrange("a r c -> r a c"),
             )
         nc.scalar.activation(floor[:], one[:], ACT.Sqrt, scale=2.0**-116)
@@ -72,9 +72,9 @@ def tile_list_kmer_locus_coverage_kernel(
         load_words(1)
 
         gathered = [big.tile([P, S], U32, name="gathered%d" % a, tag="fgh"[a], align_bytes=64) for a in range(PASSES)]
-        grows = keep.tile([P, S], U8, name="grows", align_bytes=64)
-        wkw = keep.tile([P, PASSES, 2 * H], U8, name="wkw", align_bytes=64)
-        wks = keep.tile([P, PASSES, H], U8, name="wks", align_bytes=64)
+        grows = big.tile([P, S], U8, name="grows", tag="e", align_bytes=64)
+        wkw = keep.tile([P, PACK, PASSES * P // 2], U32, name="wkw", align_bytes=64)
+        wks = keep.tile([P, PACK, PASSES * P // 4], U32, name="wks", align_bytes=64)
 
         def gather_words(a, lo, hi):
             nc.vector.tensor_copy(
@@ -89,13 +89,10 @@ def tile_list_kmer_locus_coverage_kernel(
         words.append(big.tile([P, T], I32, name="words2", tag="a", align_bytes=64))
         load_words(2)
         nc.vector.tensor_copy(
-            wkw[:].bitcast(U16).rearrange("p a (t m) -> p a t m", t=PACK),
-            wkw_raw[:].bitcast(U16).rearrange("p a (m t) -> p a t m", t=PACK),
+            wkw[:].rearrange("p t (g w) -> p t g w", w=2),
+            wkw_raw.bitcast(U32).rearrange("p (g t w) -> p t g w", t=PACK, w=2),
         )
-        nc.vector.tensor_copy(
-            wks[:].rearrange("p a (t m) -> p a t m", t=PACK),
-            wks_raw[:].bitcast(U8).rearrange("p a (m t) -> p a t m", t=PACK),
-        )
+        nc.vector.tensor_copy(wks[:], wks_raw.bitcast(U32).rearrange("p (g t) -> p t g", t=PACK))
         gather_words(0, 0, S)
         gather_words(1, 0, S)
         gather_words(2, 0, HALF)
@@ -103,17 +100,10 @@ def tile_list_kmer_locus_coverage_kernel(
 
         first = 256
         wg = big.tile([P, PACK, S], F32, name="wg", tag="b", align_bytes=64)
-        wgs_by_plane = wgs.rearrange("(m t) j -> m t j", t=PACK)
-        for ts, js in (
-            (slice(0, 2), slice(0, first)),
-            (slice(0, 1), slice(first, S)),
-            (slice(1, 2), slice(first, S)),
-            (slice(2, 4), slice(0, S)),
-        ):
+        wgs_by_plane = wgs.rearrange("(g t i) j -> t g i j", t=PACK, i=4)
+        for t, lo, hi in ((0, 0, first), (1, 0, first), (0, first, S), (1, first, S), (2, 0, S), (3, 0, S)):
             for q in (0, 2, 1, 3):
-                nc.sync.dma_start(wg[32 * q : 32 * q + 32, ts, js], wgs_by_plane[:, ts, js])
-        wo_raw = big.tile([P, PACK, N], F32, name="wo_raw", tag="f", align_bytes=64)
-        nc.sync.dma_start(wo_raw[:], wo.rearrange("(p t) n -> p t n", t=PACK))
+                nc.sync.dma_start(wg[32 * q : 32 * q + 32, t, lo:hi], wgs_by_plane[t, :, :, lo:hi])
 
         banks = [[psum.tile([P, HALF], F32, name="acc%d%d" % (t, hf), tag="bank%d" % (2 * t + hf)) for hf in range(2)] for t in range(PACK)]
         planes_u8 = planes[:].bitcast(U8)
@@ -122,8 +112,8 @@ def tile_list_kmer_locus_coverage_kernel(
             cols = slice(hf * HALF, (hf + 1) * HALF)
             nc.tensor.matmul_mx(
                 out=banks[t][hf][:],
-                lhsT=wkw[:, a, 2 * P * t : 2 * P * (t + 1)].bitcast(FP4X4),
-                lhsT_scale=wks[:, a, P * t : P * (t + 1)],
+                lhsT=wkw[:, t, a * P // 2 : (a + 1) * P // 2].bitcast(U8).bitcast(FP4X4),
+                lhsT_scale=wks[:, t, a * P // 4 : (a + 1) * P // 4].bitcast(U8),
                 rhs=gathered[a][:, cols].bitcast(FP8X4),
                 rhs_scale=planes_u8[:, a, cols],
                 start=(a == 0),
@@ -136,8 +126,11 @@ def tile_list_kmer_locus_coverage_kernel(
                     for t in ts:
                         first_product(a, hf, t)
 
+        wo_raw = big.tile([P, PACK, N], F32, name="wo_raw", tag="a", align_bytes=64)
+        wo_by_plane = wo.rearrange("(g t i) n -> t g i n", t=PACK, i=4)
+        for t in range(PACK):
+            nc.sync.dma_start(wo_raw[:, t, :], wo_by_plane[t])
         hs = keep.tile([P, PACK, S], F32, name="hs")
-        lifted = keep.tile([P, PACK, T2], F32, name="lifted")
 
         def root(t, lo, hi):
             hf = lo // HALF
@@ -153,11 +146,8 @@ def tile_list_kmer_locus_coverage_kernel(
         def lift(t, lo, hi):
             nc.scalar.activation(lifted[:, t, lo:hi], pages[t][:, lo:hi], ACT.Copy, bias=1.0)
 
-        pages.append(big.tile([P, T2], F32, name="page1", tag="c", align_bytes=64))
-        nc.gpsimd.memset(pages[0][:], 0.0)
-        nc.vector.memset(pages[1][:], 0.0)
-        for t in (2, 3):
-            pages.append(big.tile([P, T2], F32, name="page%d" % t, tag="de"[t - 2], align_bytes=64))
+        pages = [big.tile([P, T2], F32, name="page%d" % t, tag="pdec"[t], align_bytes=64) for t in range(PACK)]
+        for t in range(PACK):
             nc.gpsimd.memset(pages[t][:], 0.0)
         root(0, 0, first)
         scatter(0, 0, first)
@@ -170,19 +160,21 @@ def tile_list_kmer_locus_coverage_kernel(
         for t in (2, 3):
             root(t, 0, HALF)
             root(t, HALF, S)
-        lift(0, 0, T2)
         wo_bf = keep.tile([P, N, PACK], BF16, name="wo_bf", align_bytes=64)
-        wo_codes = keep.tile([P, N], U32, name="wo_codes", align_bytes=64)
         wo_scales = keep.tile([P, N], U8, name="wo_scales", align_bytes=64)
         nc.scalar.copy(wo_bf[:], wo_raw[:].rearrange("p t n -> p n t"))
-        base_by_plane = base.rearrange("(p t) j -> p t j", t=PACK)
-        base_sb = [big.tile([P, PACK, T2 // 2], F32, name="base%d" % u, tag="ga"[u], align_bytes=64) for u in range(2)]
+        lifted = big.tile([P, PACK, T2], F32, name="lifted", tag="a", align_bytes=64)
+        lift(0, 0, T2)
+        base_by_plane = base.rearrange("(g t i) j -> t g i j", t=PACK, i=4)
+        base_sb = [big.tile([P, PACK, T2 // 2], F32, name="base%d" % u, tag="gh"[u], align_bytes=64) for u in range(2)]
         for u in range(2):
-            nc.sync.dma_start(base_sb[u][:], base_by_plane[:, :, u * (T2 // 2) : (u + 1) * (T2 // 2)])
+            for t in range(PACK):
+                nc.sync.dma_start(base_sb[u][:, t, :], base_by_plane[t, :, :, u * (T2 // 2) : (u + 1) * (T2 // 2)])
 
         scatter(2, 0, S)
         lift(1, 0, T2)
         scatter(3, 0, S)
+        wo_codes = big.tile([P, N], U32, name="wo_codes", tag="b", align_bytes=64)
         nc.vector.quantize_mx(
             out=wo_codes[:].bitcast(FP8X4), scales=wo_scales[:], in_=wo_bf[:].rearrange("p n t -> p (n t)")
         )

@@ -20,7 +20,10 @@ P = 128
 PACK = 4
 PASSES = K // (P * PACK)
 HALF = 512
+FIRST = 256
 CHUNK = 256
+BANKS = 8
+QUADRANTS = (0, 2, 1, 3)
 
 
 def tile_list_kmer_locus_coverage_kernel(
@@ -30,14 +33,14 @@ def tile_list_kmer_locus_coverage_kernel(
     with ExitStack() as ctx:
         keep = ctx.enter_context(tc.tile_pool(name="keep", bufs=1))
         big = ctx.enter_context(tc.tile_pool(name="big", bufs=1))
-        stage = ctx.enter_context(tc.tile_pool(name="stage", bufs=4))
+        stage = ctx.enter_context(tc.tile_pool(name="stage", bufs=8))
         ring = ctx.enter_context(tc.tile_pool(name="ring", bufs=3))
         psum = ctx.enter_context(tc.psum_pool(name="psum", bufs=1))
 
         idx = keep.tile([P, S // 16], U16, name="idx")
         idx2 = keep.tile([P, S // 16], U16, name="idx2")
-        srows = big.tile([P, T // 4], I32, name="srows", tag="a", align_bytes=64)
-        planes = keep.tile([P, 4, S // 4], I32, name="planes", align_bytes=64)
+        scale_rows = big.tile([P, T // 4], I32, name="scale_rows", tag="a", align_bytes=64)
+        tab_planes = keep.tile([P, 4, S // 4], I32, name="tab_planes", align_bytes=64)
         wk_raw = big.tile([P, PASSES * (H // 2 + H // 4)], I32, name="wk_raw", tag="d", align_bytes=64)
         wkw_raw = wk_raw[:, 0 : PASSES * (H // 2)]
         wks_raw = wk_raw[:, PASSES * (H // 2) :]
@@ -49,20 +52,19 @@ def tile_list_kmer_locus_coverage_kernel(
         def load_words(a):
             nc.sync.dma_start(words[a][:], tab_words[a].rearrange("p t i -> p (t i)").bitcast(I32))
 
+        nc.gpsimd.memset(scale_rows[:], 0)
         nc.sync.dma_start(idx[:], offs)
-        scale_rows = tab_scales.bitcast(I32).rearrange("a q c -> q a c")
-        for u in range(2):
-            nc.sync.dma_start(srows[32 + u : 96 : 2, :], scale_rows[:, u : 3 : 2 - u, :])
+        rows_by_q = tab_scales.bitcast(I32).rearrange("a q c -> q a c")
+        nc.sync.dma_start(scale_rows[32:96:2, :], rows_by_q[:, 0:3:2, :])
+        nc.sync.dma_start(scale_rows[33:96:4, :], rows_by_q[:, 1, :])
         nc.sync.dma_start(wkw_raw.rearrange("p (a c) -> p a c", a=PASSES), wk_words.bitcast(I32).rearrange("a p c -> p a c"))
         load_words(0)
         nc.sync.dma_start(idx2[:], offs2)
 
         nc.vector.memset(one[:], 1.0)
         nc.gpsimd.memset(wks_raw, 0)
-        nc.gpsimd.memset(srows[0:32, :], 0)
-        nc.gpsimd.memset(srows[96:128, :], 0)
-        nc.gpsimd.memset(planes[:, 0:PASSES, :], 0)
-        for q in range(4):
+        nc.gpsimd.memset(tab_planes[:, 0:PASSES, :], 0)
+        for q in QUADRANTS:
             nc.scalar.dma_start(
                 wks_raw[32 * q : 32 * q + 4, :].rearrange("p (a c) -> p a c", a=PASSES),
                 wk_scales[:, 4 * q : 4 * q + 4, :].bitcast(I32).rearrange("a r c -> r a c"),
@@ -72,7 +74,7 @@ def tile_list_kmer_locus_coverage_kernel(
         load_words(1)
 
         gathered = [big.tile([P, S], U32, name="gathered%d" % a, tag="fgh"[a], align_bytes=64) for a in range(PASSES)]
-        grows = big.tile([P, S], U8, name="grows", tag="e", align_bytes=64)
+        picked_rows = big.tile([P, S], U8, name="picked_rows", tag="e", align_bytes=64)
         wkw = keep.tile([P, PACK, PASSES * P // 2], U32, name="wkw", align_bytes=64)
         wks = keep.tile([P, PACK, PASSES * P // 4], U32, name="wks", align_bytes=64)
 
@@ -81,10 +83,10 @@ def tile_list_kmer_locus_coverage_kernel(
                 gathered[a][:, lo:hi], words[a][:].bitcast(U32).indirect(idx[:, lo // 16 : hi // 16])
             )
 
-        nc.vector.tensor_copy(grows[:], srows[:].bitcast(U8).indirect(idx[:]))
-        for q in range(4):
+        nc.vector.tensor_copy(picked_rows[:], scale_rows[:].bitcast(U8).indirect(idx[:]))
+        for q in QUADRANTS:
             nc.sync.dma_start(
-                planes[32 * q : 32 * q + 4, :, :], grows[32 + 16 * q : 48 + 16 * q, :].bitcast(I32)
+                tab_planes[32 * q : 32 * q + 4, :, :], picked_rows[32 + 16 * q : 48 + 16 * q, :].bitcast(I32)
             )
         words.append(big.tile([P, T], I32, name="words2", tag="a", align_bytes=64))
         load_words(2)
@@ -98,15 +100,17 @@ def tile_list_kmer_locus_coverage_kernel(
         gather_words(2, 0, HALF)
         gather_words(2, HALF, S)
 
-        first = 256
         wg = big.tile([P, PACK, S], F32, name="wg", tag="b", align_bytes=64)
         wgs_by_plane = wgs.rearrange("(g t i) j -> t g i j", t=PACK, i=4)
-        for t, lo, hi in ((0, 0, first), (1, 0, first), (0, first, S), (1, first, S), (2, 0, S), (3, 0, S)):
-            for q in (0, 2, 1, 3):
+        for t, lo, hi in ((0, 0, FIRST), (1, 0, FIRST), (0, FIRST, S), (1, FIRST, S), (2, 0, S), (3, 0, S)):
+            for q in QUADRANTS:
                 nc.sync.dma_start(wg[32 * q : 32 * q + 32, t, lo:hi], wgs_by_plane[t, :, :, lo:hi])
 
-        banks = [[psum.tile([P, HALF], F32, name="acc%d%d" % (t, hf), tag="bank%d" % (2 * t + hf)) for hf in range(2)] for t in range(PACK)]
-        planes_u8 = planes[:].bitcast(U8)
+        banks = [
+            [psum.tile([P, HALF], F32, name="acc%d%d" % (t, hf), tag="bank%d" % (2 * t + hf)) for hf in range(2)]
+            for t in range(PACK)
+        ]
+        tab_planes_u8 = tab_planes[:].bitcast(U8)
 
         def first_product(a, hf, t):
             cols = slice(hf * HALF, (hf + 1) * HALF)
@@ -115,7 +119,7 @@ def tile_list_kmer_locus_coverage_kernel(
                 lhsT=wkw[:, t, a * P // 2 : (a + 1) * P // 2].bitcast(U8).bitcast(FP4X4),
                 lhsT_scale=wks[:, t, a * P // 4 : (a + 1) * P // 4].bitcast(U8),
                 rhs=gathered[a][:, cols].bitcast(FP8X4),
-                rhs_scale=planes_u8[:, a, cols],
+                rhs_scale=tab_planes_u8[:, a, cols],
                 start=(a == 0),
                 stop=(a == PASSES - 1),
             )
@@ -146,17 +150,16 @@ def tile_list_kmer_locus_coverage_kernel(
         def lift(t, lo, hi):
             nc.scalar.activation(lifted[:, t, lo:hi], pages[t][:, lo:hi], ACT.Copy, bias=1.0)
 
-        pages = [big.tile([P, T2], F32, name="page%d" % t, tag="pdec"[t], align_bytes=64) for t in range(PACK)]
+        pages = [big.tile([P, T2], F32, name="page%d" % t, tag="pdeq"[t], align_bytes=64) for t in range(PACK)]
         for t in range(PACK):
             nc.gpsimd.memset(pages[t][:], 0.0)
-        root(0, 0, first)
-        scatter(0, 0, first)
-        root(1, 0, first)
-        scatter(1, 0, first)
         for t in (0, 1):
-            root(t, first, HALF)
+            root(t, 0, FIRST)
+            scatter(t, 0, FIRST)
+        for t in (0, 1):
+            root(t, FIRST, HALF)
             root(t, HALF, S)
-            scatter(t, first, S)
+            scatter(t, FIRST, S)
         for t in (2, 3):
             root(t, 0, HALF)
             root(t, HALF, S)
@@ -181,7 +184,7 @@ def tile_list_kmer_locus_coverage_kernel(
         lift(2, 0, T2)
 
         out_view = out.rearrange("(m p) j -> p m j", p=P)
-        widths = [CHUNK] * 8
+        widths = [CHUNK] * (T2 // CHUNK - 1) + [CHUNK // 2] * 2
         starts = [sum(widths[:c]) for c in range(len(widths))]
         chunks = len(widths)
         zs = {}
@@ -212,7 +215,7 @@ def tile_list_kmer_locus_coverage_kernel(
             lo, w = starts[c], widths[c]
             staged = stage.tile([P, PACK, w], F32, name="staged", align_bytes=64)
             for pair in range(2):
-                acc = psum.tile([P, 2, w], F32, name="track", tag="bank%d" % ((2 * c + pair) % 8))
+                acc = psum.tile([P, 2, w], F32, name="track", tag="bank%d" % ((2 * c + pair) % BANKS))
                 for u in range(2):
                     m = 2 * pair + u
                     nc.tensor.matmul_mx(
@@ -224,26 +227,18 @@ def tile_list_kmer_locus_coverage_kernel(
                         start=True,
                         stop=True,
                     )
-                if c == chunks - 1 and pair == 1:
+                if c >= chunks - 2 and pair == 1:
                     nc.vector.tensor_copy(staged[:, 2 * pair : 2 * pair + 2, :], acc[:])
                 else:
                     nc.scalar.copy(staged[:, 2 * pair : 2 * pair + 2, :], acc[:])
-                if c == chunks - 1:
-                    nc.sync.dma_start(
-                        out_view[:, 2 * pair : 2 * pair + 2, lo : lo + w], staged[:, 2 * pair : 2 * pair + 2, :]
-                    )
-            if c < chunks - 1:
-                nc.sync.dma_start(out_view[:, :, lo : lo + w], staged[:])
+                nc.sync.dma_start(
+                    out_view[:, 2 * pair : 2 * pair + 2, lo : lo + w], staged[:, 2 * pair : 2 * pair + 2, :]
+                )
 
-        def lift_last(c):
-            lift(3, starts[c], starts[c] + widths[c])
-
-        lift_last(0)
-        lift_last(1)
+        for lo, hi in ((0, CHUNK), (CHUNK, 2 * CHUNK), (2 * CHUNK, 4 * CHUNK), (4 * CHUNK, T2)):
+            lift(3, lo, hi)
         make_z(0)
         for c in range(chunks):
-            if c + 2 < chunks:
-                lift_last(c + 2)
             if c + 1 < chunks:
                 make_z(c + 1)
             quantise_z(c)

@@ -39,11 +39,10 @@ def tile_list_kmer_locus_coverage_kernel(
 
         idx = keep.tile([P, S // 16], U16, name="idx")
         idx2 = keep.tile([P, S // 16], U16, name="idx2")
-        scale_rows = big.tile([P, T // 4], I32, name="scale_rows", tag="a", align_bytes=64)
+        scale_rows = big.tile([P, T // 4], I32, name="scale_rows", tag="f", align_bytes=64)
         tab_planes = keep.tile([P, 4, S // 4], I32, name="tab_planes", align_bytes=64)
-        wk_raw = big.tile([P, PASSES * (H // 2 + H // 4)], I32, name="wk_raw", tag="d", align_bytes=64)
-        wkw_raw = wk_raw[:, 0 : PASSES * (H // 2)]
-        wks_raw = wk_raw[:, PASSES * (H // 2) :]
+        wkw_raw = big.tile([P, PASSES * (H // 2)], I32, name="wkw_raw", tag="a", align_bytes=64)
+        wks_raw = keep.tile([P, PASSES * (H // 4)], I32, name="wks_raw", align_bytes=64)
         one = big.tile([P, 1], F32, name="one", tag="c", align_bytes=64)
         floor = keep.tile([P, 1], F32, name="floor")
 
@@ -52,20 +51,22 @@ def tile_list_kmer_locus_coverage_kernel(
         def load_words(a):
             nc.sync.dma_start(words[a][:], tab_words[a].rearrange("p t i -> p (t i)").bitcast(I32))
 
-        nc.gpsimd.memset(scale_rows[:], 0)
-        nc.sync.dma_start(idx[:], offs)
+        nc.vector.memset(scale_rows[:], 0)
         rows_by_q = tab_scales.bitcast(I32).rearrange("a q c -> q a c")
-        nc.sync.dma_start(scale_rows[32:96:2, :], rows_by_q[:, 0:3:2, :])
-        nc.sync.dma_start(scale_rows[33:96:4, :], rows_by_q[:, 1, :])
-        nc.sync.dma_start(wkw_raw.rearrange("p (a c) -> p a c", a=PASSES), wk_words.bitcast(I32).rearrange("a p c -> p a c"))
-        load_words(0)
+        nc.scalar.dma_start(scale_rows[32:96:2, :], rows_by_q[:, 0:3:2, :])
+        nc.scalar.dma_start(scale_rows[33:96:4, :], rows_by_q[:, 1, :])
+        nc.sync.dma_start(idx[:], offs)
         nc.sync.dma_start(idx2[:], offs2)
+        load_words(0)
+        nc.sync.dma_start(
+            wkw_raw[:].rearrange("p (a c) -> p a c", a=PASSES), wk_words.bitcast(I32).rearrange("a p c -> p a c")
+        )
 
         nc.vector.memset(one[:], 1.0)
-        nc.gpsimd.memset(wks_raw, 0)
-        nc.gpsimd.memset(tab_planes[:, 0:PASSES, :], 0)
+        nc.gpsimd.memset(wks_raw[:], 0)
+        nc.vector.memset(tab_planes[:, 0:PASSES, :], 0)
         for q in QUADRANTS:
-            nc.scalar.dma_start(
+            nc.gpsimd.dma_start(
                 wks_raw[32 * q : 32 * q + 4, :].rearrange("p (a c) -> p a c", a=PASSES),
                 wk_scales[:, 4 * q : 4 * q + 4, :].bitcast(I32).rearrange("a r c -> r a c"),
             )
@@ -75,8 +76,7 @@ def tile_list_kmer_locus_coverage_kernel(
 
         gathered = [big.tile([P, S], U32, name="gathered%d" % a, tag="fgh"[a], align_bytes=64) for a in range(PASSES)]
         picked_rows = big.tile([P, S], U8, name="picked_rows", tag="e", align_bytes=64)
-        wkw = keep.tile([P, PACK, PASSES * P // 2], U32, name="wkw", align_bytes=64)
-        wks = keep.tile([P, PACK, PASSES * P // 4], U32, name="wks", align_bytes=64)
+        wkw = keep.tile([P, PACK, PASSES * P], U16, name="wkw", align_bytes=64)
 
         def gather_words(a, lo, hi):
             nc.vector.tensor_copy(
@@ -85,55 +85,55 @@ def tile_list_kmer_locus_coverage_kernel(
 
         nc.vector.tensor_copy(picked_rows[:], scale_rows[:].bitcast(U8).indirect(idx[:]))
         for q in QUADRANTS:
-            nc.sync.dma_start(
+            nc.scalar.dma_start(
                 tab_planes[32 * q : 32 * q + 4, :, :], picked_rows[32 + 16 * q : 48 + 16 * q, :].bitcast(I32)
             )
+        nc.vector.tensor_copy(wkw[:], wkw_raw[:].bitcast(U16).rearrange("p (m t) -> p t m", t=PACK))
+        wks = big.tile([P, PACK, PASSES * P], U8, name="wks", tag="e", align_bytes=64)
+        nc.vector.tensor_copy(wks[:], wks_raw[:].bitcast(U8).rearrange("p (m t) -> p t m", t=PACK))
         words.append(big.tile([P, T], I32, name="words2", tag="a", align_bytes=64))
         load_words(2)
-        nc.vector.tensor_copy(
-            wkw[:].rearrange("p t (g w) -> p t g w", w=2),
-            wkw_raw.bitcast(U32).rearrange("p (g t w) -> p t g w", t=PACK, w=2),
-        )
-        nc.vector.tensor_copy(wks[:], wks_raw.bitcast(U32).rearrange("p (g t) -> p t g", t=PACK))
         gather_words(0, 0, S)
         gather_words(1, 0, S)
         gather_words(2, 0, HALF)
         gather_words(2, HALF, S)
 
         wg = big.tile([P, PACK, S], F32, name="wg", tag="b", align_bytes=64)
-        wgs_by_plane = wgs.rearrange("(g t i) j -> t g i j", t=PACK, i=4)
-        for t, lo, hi in ((0, 0, FIRST), (1, 0, FIRST), (0, FIRST, S), (1, FIRST, S), (2, 0, S), (3, 0, S)):
+        wgs_by_plane = wgs.rearrange("(g t) j -> g t j", t=PACK)
+        for t, lo, hi in ((0, 0, FIRST), (0, FIRST, S), (2, 0, S)):
             for q in QUADRANTS:
-                nc.sync.dma_start(wg[32 * q : 32 * q + 32, t, lo:hi], wgs_by_plane[t, :, :, lo:hi])
+                nc.sync.dma_start(wg[32 * q : 32 * q + 32, t : t + 2, lo:hi], wgs_by_plane[:, t : t + 2, lo:hi])
 
-        banks = [
-            [psum.tile([P, HALF], F32, name="acc%d%d" % (t, hf), tag="bank%d" % (2 * t + hf)) for hf in range(2)]
-            for t in range(PACK)
-        ]
+        banks = {}
         tab_planes_u8 = tab_planes[:].bitcast(U8)
 
         def first_product(a, hf, t):
             cols = slice(hf * HALF, (hf + 1) * HALF)
             nc.tensor.matmul_mx(
                 out=banks[t][hf][:],
-                lhsT=wkw[:, t, a * P // 2 : (a + 1) * P // 2].bitcast(U8).bitcast(FP4X4),
-                lhsT_scale=wks[:, t, a * P // 4 : (a + 1) * P // 4].bitcast(U8),
+                lhsT=wkw[:, t, a * P : (a + 1) * P].bitcast(U8).bitcast(FP4X4),
+                lhsT_scale=wks[:, t, a * P : (a + 1) * P],
                 rhs=gathered[a][:, cols].bitcast(FP8X4),
                 rhs_scale=tab_planes_u8[:, a, cols],
                 start=(a == 0),
                 stop=(a == PASSES - 1),
             )
 
-        for ts in ((0, 1), (2, 3)):
+        def first_products(ts):
+            for t in ts:
+                banks[t] = [
+                    psum.tile([P, HALF], F32, name="acc%d%d" % (t, hf), tag="bank%d" % (2 * (t % 2) + hf))
+                    for hf in range(2)
+                ]
             for a in range(PASSES):
                 for hf in range(2):
                     for t in ts:
                         first_product(a, hf, t)
 
+        first_products((0, 1))
+
         wo_raw = big.tile([P, PACK, N], F32, name="wo_raw", tag="a", align_bytes=64)
-        wo_by_plane = wo.rearrange("(g t i) n -> t g i n", t=PACK, i=4)
-        for t in range(PACK):
-            nc.sync.dma_start(wo_raw[:, t, :], wo_by_plane[t])
+        nc.sync.dma_start(wo_raw[:], wo.rearrange("(p t) n -> p t n", t=PACK))
         hs = keep.tile([P, PACK, S], F32, name="hs")
 
         def root(t, lo, hi):
@@ -150,9 +150,14 @@ def tile_list_kmer_locus_coverage_kernel(
         def lift(t, lo, hi):
             nc.scalar.activation(lifted[:, t, lo:hi], pages[t][:, lo:hi], ACT.Copy, bias=1.0)
 
-        pages = [big.tile([P, T2], F32, name="page%d" % t, tag="pdeq"[t], align_bytes=64) for t in range(PACK)]
-        for t in range(PACK):
+        pages = {}
+
+        def clear_page(t):
+            pages[t] = big.tile([P, T2], F32, name="page%d" % t, tag="pdec"[t], align_bytes=64)
             nc.gpsimd.memset(pages[t][:], 0.0)
+
+        for t in (0, 1, 3):
+            clear_page(t)
         for t in (0, 1):
             root(t, 0, FIRST)
             scatter(t, 0, FIRST)
@@ -160,6 +165,8 @@ def tile_list_kmer_locus_coverage_kernel(
             root(t, FIRST, HALF)
             root(t, HALF, S)
             scatter(t, FIRST, S)
+        first_products((2, 3))
+        clear_page(2)
         for t in (2, 3):
             root(t, 0, HALF)
             root(t, HALF, S)
@@ -168,11 +175,10 @@ def tile_list_kmer_locus_coverage_kernel(
         nc.scalar.copy(wo_bf[:], wo_raw[:].rearrange("p t n -> p n t"))
         lifted = big.tile([P, PACK, T2], F32, name="lifted", tag="a", align_bytes=64)
         lift(0, 0, T2)
-        base_by_plane = base.rearrange("(g t i) j -> t g i j", t=PACK, i=4)
+        base_by_plane = base.rearrange("(p t) j -> p t j", t=PACK)
         base_sb = [big.tile([P, PACK, T2 // 2], F32, name="base%d" % u, tag="gh"[u], align_bytes=64) for u in range(2)]
         for u in range(2):
-            for t in range(PACK):
-                nc.sync.dma_start(base_sb[u][:, t, :], base_by_plane[t, :, :, u * (T2 // 2) : (u + 1) * (T2 // 2)])
+            nc.sync.dma_start(base_sb[u][:], base_by_plane[:, :, u * (T2 // 2) : (u + 1) * (T2 // 2)])
 
         scatter(2, 0, S)
         lift(1, 0, T2)

@@ -23,6 +23,7 @@ HALF = 512
 FIRST = 256
 CHUNK = 256
 BANKS = 8
+KIB = 1024
 QUADRANTS = (0, 2, 1, 3)
 
 
@@ -33,45 +34,46 @@ def tile_list_kmer_locus_coverage_kernel(
     with ExitStack() as ctx:
         keep = ctx.enter_context(tc.tile_pool(name="keep", bufs=1))
         big = ctx.enter_context(tc.tile_pool(name="big", bufs=1))
+        shared = ctx.enter_context(tc.tile_pool(name="shared", bufs=1))
         stage = ctx.enter_context(tc.tile_pool(name="stage", bufs=8))
         ring = ctx.enter_context(tc.tile_pool(name="ring", bufs=3))
         psum = ctx.enter_context(tc.psum_pool(name="psum", bufs=1))
 
         idx = keep.tile([P, S // 16], U16, name="idx")
         idx2 = keep.tile([P, S // 16], U16, name="idx2")
-        scale_rows = big.tile([P, T // 4], I32, name="scale_rows", tag="f", align_bytes=64)
-        tab_planes = keep.tile([P, 4, S // 4], I32, name="tab_planes", align_bytes=64)
-        wkw_raw = big.tile([P, PASSES * (H // 2)], I32, name="wkw_raw", tag="a", align_bytes=64)
+        scale_rows = big.tile([P, T // 4], I32, name="scale_rows", tag="a", align_bytes=64)
+        tab_planes = [keep.tile([P, 4, HALF // 4], I32, name="tab_planes0", align_bytes=64)]
+        wkw_raw = big.tile([P, PASSES * (H // 2)], I32, name="wkw_raw", tag="d", align_bytes=64)
         wks_raw = keep.tile([P, PASSES * (H // 4)], I32, name="wks_raw", align_bytes=64)
-        one = big.tile([P, 1], F32, name="one", tag="c", align_bytes=64)
+        one = shared.tile([P, 1], F32, name="one", offset=16 * KIB, align_bytes=64)
         floor = keep.tile([P, 1], F32, name="floor")
 
-        words = [big.tile([P, T], I32, name="words0", tag="b", align_bytes=64)]
+        words = [shared.tile([P, T], I32, name="words0", offset=0, align_bytes=64)]
 
         def load_words(a):
             nc.sync.dma_start(words[a][:], tab_words[a].rearrange("p t i -> p (t i)").bitcast(I32))
 
-        nc.vector.memset(scale_rows[:], 0)
-        rows_by_q = tab_scales.bitcast(I32).rearrange("a q c -> q a c")
-        nc.scalar.dma_start(scale_rows[32:96:2, :], rows_by_q[:, 0:3:2, :])
-        nc.scalar.dma_start(scale_rows[33:96:4, :], rows_by_q[:, 1, :])
+        nc.gpsimd.memset(scale_rows[:], 0)
         nc.sync.dma_start(idx[:], offs)
-        nc.sync.dma_start(idx2[:], offs2)
-        load_words(0)
+        rows_by_q = tab_scales.bitcast(I32).rearrange("a q c -> q a c")
+        nc.sync.dma_start(scale_rows[32:96:2, :], rows_by_q[:, 0:3:2, :])
+        nc.sync.dma_start(scale_rows[33:96:4, :], rows_by_q[:, 1, :])
         nc.sync.dma_start(
             wkw_raw[:].rearrange("p (a c) -> p a c", a=PASSES), wk_words.bitcast(I32).rearrange("a p c -> p a c")
         )
+        load_words(0)
+        nc.sync.dma_start(idx2[:], offs2)
 
         nc.vector.memset(one[:], 1.0)
         nc.gpsimd.memset(wks_raw[:], 0)
-        nc.vector.memset(tab_planes[:, 0:PASSES, :], 0)
+        nc.gpsimd.memset(tab_planes[0][:, 0:PASSES, :], 0)
         for q in QUADRANTS:
-            nc.gpsimd.dma_start(
+            nc.scalar.dma_start(
                 wks_raw[32 * q : 32 * q + 4, :].rearrange("p (a c) -> p a c", a=PASSES),
                 wk_scales[:, 4 * q : 4 * q + 4, :].bitcast(I32).rearrange("a r c -> r a c"),
             )
         nc.scalar.activation(floor[:], one[:], ACT.Sqrt, scale=2.0**-116)
-        words.append(big.tile([P, T], I32, name="words1", tag="c", align_bytes=64))
+        words.append(shared.tile([P, T], I32, name="words1", offset=16 * KIB, align_bytes=64))
         load_words(1)
 
         gathered = [big.tile([P, S], U32, name="gathered%d" % a, tag="fgh"[a], align_bytes=64) for a in range(PASSES)]
@@ -84,67 +86,81 @@ def tile_list_kmer_locus_coverage_kernel(
             )
 
         nc.vector.tensor_copy(picked_rows[:], scale_rows[:].bitcast(U8).indirect(idx[:]))
-        for q in QUADRANTS:
-            nc.scalar.dma_start(
-                tab_planes[32 * q : 32 * q + 4, :, :], picked_rows[32 + 16 * q : 48 + 16 * q, :].bitcast(I32)
-            )
-        nc.vector.tensor_copy(wkw[:], wkw_raw[:].bitcast(U16).rearrange("p (m t) -> p t m", t=PACK))
-        wks = big.tile([P, PACK, PASSES * P], U8, name="wks", tag="e", align_bytes=64)
-        nc.vector.tensor_copy(wks[:], wks_raw[:].bitcast(U8).rearrange("p (m t) -> p t m", t=PACK))
+
+        def move_scales(hf):
+            for q in QUADRANTS:
+                nc.sync.dma_start(
+                    tab_planes[hf][32 * q : 32 * q + 4, :, :],
+                    picked_rows[32 + 16 * q : 48 + 16 * q, hf * HALF : (hf + 1) * HALF].bitcast(I32),
+                )
+
+        move_scales(0)
         words.append(big.tile([P, T], I32, name="words2", tag="a", align_bytes=64))
         load_words(2)
+        nc.vector.tensor_copy(wkw[:], wkw_raw[:].bitcast(U16).rearrange("p (m t) -> p t m", t=PACK))
+        wks = keep.tile([P, PACK, PASSES * P], U8, name="wks", align_bytes=64)
+        nc.vector.tensor_copy(wks[:], wks_raw[:].bitcast(U8).rearrange("p (m t) -> p t m", t=PACK))
         gather_words(0, 0, S)
+        tab_planes.append(shared.tile([P, 4, HALF // 4], I32, name="tab_planes1", offset=0, align_bytes=64))
+        nc.gpsimd.memset(tab_planes[1][:, 0:PASSES, :], 0)
         gather_words(1, 0, S)
         gather_words(2, 0, HALF)
         gather_words(2, HALF, S)
 
-        wg = big.tile([P, PACK, S], F32, name="wg", tag="b", align_bytes=64)
         wgs_by_plane = wgs.rearrange("(g t) j -> g t j", t=PACK)
-        for t, lo, hi in ((0, 0, FIRST), (0, FIRST, S), (2, 0, S)):
+        wg = {}
+        for t, lo, hi, offset in ((0, 0, FIRST, 2 * KIB), (0, FIRST, S, 16 * KIB), (2, 0, S, 22 * KIB)):
+            piece = shared.tile([P, 2, hi - lo], F32, name="wg%d_%d" % (t, lo), offset=offset, align_bytes=64)
             for q in QUADRANTS:
-                nc.sync.dma_start(wg[32 * q : 32 * q + 32, t : t + 2, lo:hi], wgs_by_plane[:, t : t + 2, lo:hi])
+                nc.sync.dma_start(piece[32 * q : 32 * q + 32], wgs_by_plane[:, t : t + 2, lo:hi])
+            for u in range(2):
+                wg[t + u, lo] = piece[:, u, :]
+            if hi == FIRST:
+                move_scales(1)
 
-        banks = {}
-        tab_planes_u8 = tab_planes[:].bitcast(U8)
+        sums = {}
 
-        def first_product(a, hf, t):
-            cols = slice(hf * HALF, (hf + 1) * HALF)
-            nc.tensor.matmul_mx(
-                out=banks[t][hf][:],
-                lhsT=wkw[:, t, a * P : (a + 1) * P].bitcast(U8).bitcast(FP4X4),
-                lhsT_scale=wks[:, t, a * P : (a + 1) * P],
-                rhs=gathered[a][:, cols].bitcast(FP8X4),
-                rhs_scale=tab_planes_u8[:, a, cols],
-                start=(a == 0),
-                stop=(a == PASSES - 1),
-            )
+        def open_piece(t, lo, hi, bank):
+            sums[t, lo] = psum.tile([P, hi - lo], F32, name="acc%d_%d" % (t, lo), tag="bank%d" % bank)
 
-        def first_products(ts):
-            for t in ts:
-                banks[t] = [
-                    psum.tile([P, HALF], F32, name="acc%d%d" % (t, hf), tag="bank%d" % (2 * (t % 2) + hf))
-                    for hf in range(2)
-                ]
+        def first_product(a, t, lo, hi):
+            hf = lo // HALF
+            n = HALF if hi - lo == HALF else P
+            for c in range(lo, hi, n):
+                nc.tensor.matmul_mx(
+                    out=sums[t, lo][:, c - lo : c - lo + n],
+                    lhsT=wkw[:, t, a * P : (a + 1) * P].bitcast(U8).bitcast(FP4X4),
+                    lhsT_scale=wks[:, t, a * P : (a + 1) * P],
+                    rhs=gathered[a][:, c : c + n].bitcast(FP8X4),
+                    rhs_scale=tab_planes[hf][:, a, :].bitcast(U8)[:, c - hf * HALF : c - hf * HALF + n],
+                    start=(a == 0 and c == lo),
+                    stop=(a == PASSES - 1 and c + n == hi),
+                )
+
+        def first_products(pieces):
+            for t, lo, hi, bank in pieces:
+                open_piece(t, lo, hi, bank)
             for a in range(PASSES):
-                for hf in range(2):
-                    for t in ts:
-                        first_product(a, hf, t)
+                for t, lo, hi, bank in pieces:
+                    first_product(a, t, lo, hi)
 
-        first_products((0, 1))
+        first_products(((0, 0, FIRST, 0), (1, 0, HALF, 1), (0, FIRST, HALF, 2)))
+        first_products(((0, HALF, S, 3), (1, HALF, S, 4)))
+        first_products(((2, 0, HALF, 5), (3, 0, HALF, 6)))
 
         wo_raw = big.tile([P, PACK, N], F32, name="wo_raw", tag="a", align_bytes=64)
         nc.sync.dma_start(wo_raw[:], wo.rearrange("(p t) n -> p t n", t=PACK))
         hs = keep.tile([P, PACK, S], F32, name="hs")
 
         def root(t, lo, hi):
-            hf = lo // HALF
+            first = lo if (t, lo) in sums else 0
             mag = ring.tile([P, hi - lo], F32, name="mag")
-            nc.scalar.activation(mag[:], banks[t][hf][:, lo - hf * HALF : hi - hf * HALF], ACT.Abs)
+            nc.scalar.activation(mag[:], sums[t, first][:, lo - first : hi - first], ACT.Abs)
             nc.scalar.activation(hs[:, t, lo:hi], mag[:], ACT.Sqrt, bias=floor[:])
 
         def scatter(t, lo, hi):
             nc.vector.tensor_tensor(
-                pages[t][:].indirect(idx2[:, lo // 16 : hi // 16]), hs[:, t, lo:hi], wg[:, t, lo:hi], MULT
+                pages[t][:].indirect(idx2[:, lo // 16 : hi // 16]), hs[:, t, lo:hi], wg[t, lo], MULT
             )
 
         def lift(t, lo, hi):
@@ -153,10 +169,13 @@ def tile_list_kmer_locus_coverage_kernel(
         pages = {}
 
         def clear_page(t):
-            pages[t] = big.tile([P, T2], F32, name="page%d" % t, tag="pdec"[t], align_bytes=64)
+            if t == 3:
+                pages[t] = shared.tile([P, T2], F32, name="page3", offset=30 * KIB, align_bytes=64)
+            else:
+                pages[t] = big.tile([P, T2], F32, name="page%d" % t, tag="pdq"[t], align_bytes=64)
             nc.gpsimd.memset(pages[t][:], 0.0)
 
-        for t in (0, 1, 3):
+        for t in range(PACK):
             clear_page(t)
         for t in (0, 1):
             root(t, 0, FIRST)
@@ -165,8 +184,7 @@ def tile_list_kmer_locus_coverage_kernel(
             root(t, FIRST, HALF)
             root(t, HALF, S)
             scatter(t, FIRST, S)
-        first_products((2, 3))
-        clear_page(2)
+        first_products(((2, HALF, S, 7), (3, HALF, S, 0)))
         for t in (2, 3):
             root(t, 0, HALF)
             root(t, HALF, S)
@@ -183,7 +201,7 @@ def tile_list_kmer_locus_coverage_kernel(
         scatter(2, 0, S)
         lift(1, 0, T2)
         scatter(3, 0, S)
-        wo_codes = big.tile([P, N], U32, name="wo_codes", tag="b", align_bytes=64)
+        wo_codes = shared.tile([P, N], U32, name="wo_codes", offset=22 * KIB, align_bytes=64)
         nc.vector.quantize_mx(
             out=wo_codes[:].bitcast(FP8X4), scales=wo_scales[:], in_=wo_bf[:].rearrange("p n t -> p (n t)")
         )

@@ -33,124 +33,133 @@ def tile_list_kmer_locus_coverage_kernel(
     nc = tc.nc
     with ExitStack() as ctx:
         keep = ctx.enter_context(tc.tile_pool(name="keep", bufs=1))
-        big = ctx.enter_context(tc.tile_pool(name="big", bufs=1))
-        shared = ctx.enter_context(tc.tile_pool(name="shared", bufs=1))
+        mem = ctx.enter_context(tc.tile_pool(name="mem", bufs=1))
         stage = ctx.enter_context(tc.tile_pool(name="stage", bufs=8))
         ring = ctx.enter_context(tc.tile_pool(name="ring", bufs=3))
         psum = ctx.enter_context(tc.psum_pool(name="psum", bufs=1))
 
+        def placed(shape, dtype, name, kib):
+            return mem.tile(shape, dtype, name=name, offset=int(kib * KIB), align_bytes=64)
+
         idx = keep.tile([P, S // 16], U16, name="idx")
         idx2 = keep.tile([P, S // 16], U16, name="idx2")
-        scale_rows = big.tile([P, T // 4], I32, name="scale_rows", tag="a", align_bytes=64)
-        tab_planes = [keep.tile([P, 4, HALF // 4], I32, name="tab_planes0", align_bytes=64)]
-        wkw_raw = big.tile([P, PASSES * (H // 2)], I32, name="wkw_raw", tag="d", align_bytes=64)
+        words = [placed([P, T], I32, "words0", 12)]
+        scale_rows = placed([P, T // 4], I32, "scale_rows", 59.5)
+        one = placed([P, 1], F32, "one", 30)
+        wkw_raw = keep.tile([P, PASSES * (H // 2)], I32, name="wkw_raw", align_bytes=64)
         wks_raw = keep.tile([P, PASSES * (H // 4)], I32, name="wks_raw", align_bytes=64)
-        one = shared.tile([P, 1], F32, name="one", offset=16 * KIB, align_bytes=64)
+        tab_planes = [keep.tile([P, PASSES, HALF // 4], I32, name="tab_planes0", align_bytes=64)]
         floor = keep.tile([P, 1], F32, name="floor")
 
-        words = [shared.tile([P, T], I32, name="words0", offset=0, align_bytes=64)]
+        def load_words(a, lo, hi):
+            nc.sync.dma_start(words[a][:, lo:hi], tab_words[a].rearrange("p t i -> p (t i)").bitcast(I32)[:, lo:hi])
 
-        def load_words(a):
-            nc.sync.dma_start(words[a][:], tab_words[a].rearrange("p t i -> p (t i)").bitcast(I32))
-
-        nc.gpsimd.memset(scale_rows[:], 0)
+        nc.gpsimd.memset(wks_raw[:], 0)
+        nc.vector.memset(one[:], 1.0)
+        load_words(0, 0, T // 2)
         nc.sync.dma_start(idx[:], offs)
-        rows_by_q = tab_scales.bitcast(I32).rearrange("a q c -> q a c")
-        nc.sync.dma_start(scale_rows[32:96:2, :], rows_by_q[:, 0:3:2, :])
-        nc.sync.dma_start(scale_rows[33:96:4, :], rows_by_q[:, 1, :])
+        nc.sync.dma_start(idx2[:], offs2)
+        rows = tab_scales.bitcast(I32)
+        nc.sync.dma_start(scale_rows[64:96, :], rows.rearrange("a q c -> q a c")[:, 0:2, :])
+        nc.sync.dma_start(scale_rows[48:64, :], rows[2])
+        load_words(0, T // 2, T)
         nc.sync.dma_start(
             wkw_raw[:].rearrange("p (a c) -> p a c", a=PASSES), wk_words.bitcast(I32).rearrange("a p c -> p a c")
         )
-        load_words(0)
-        nc.sync.dma_start(idx2[:], offs2)
-
-        nc.vector.memset(one[:], 1.0)
-        nc.gpsimd.memset(wks_raw[:], 0)
-        nc.gpsimd.memset(tab_planes[0][:, 0:PASSES, :], 0)
         for q in QUADRANTS:
-            nc.scalar.dma_start(
+            nc.sync.dma_start(
                 wks_raw[32 * q : 32 * q + 4, :].rearrange("p (a c) -> p a c", a=PASSES),
                 wk_scales[:, 4 * q : 4 * q + 4, :].bitcast(I32).rearrange("a r c -> r a c"),
             )
         nc.scalar.activation(floor[:], one[:], ACT.Sqrt, scale=2.0**-116)
-        words.append(shared.tile([P, T], I32, name="words1", offset=16 * KIB, align_bytes=64))
-        load_words(1)
+        words.append(placed([P, T], I32, "words1", 28))
+        load_words(1, 0, T)
 
-        gathered = [big.tile([P, S], U32, name="gathered%d" % a, tag="fgh"[a], align_bytes=64) for a in range(PASSES)]
-        picked_rows = big.tile([P, S], U8, name="picked_rows", tag="e", align_bytes=64)
-        wkw = keep.tile([P, PACK, PASSES * P], U16, name="wkw", align_bytes=64)
+        nc.gpsimd.memset(scale_rows[0:48, :], 0)
+        nc.gpsimd.memset(scale_rows[96:128, :], 0)
+        nc.gpsimd.memset(tab_planes[0][:], 0)
+        pages = [placed([P, T2], F32, "page%d" % t, 92 + 8 * t) for t in range(PACK)]
+        for t in range(PACK):
+            nc.gpsimd.memset(pages[t][:], 0.0)
+
+        picked_rows = keep.tile([P, S], U8, name="picked_rows", align_bytes=64)
+        nc.vector.tensor_copy(picked_rows[:], scale_rows[:].bitcast(U8).indirect(idx[:]))
+
+        def move_scales(hf, last):
+            picked = picked_rows[:, hf * HALF : (hf + 1) * HALF].bitcast(I32)
+            for q in QUADRANTS:
+                if last:
+                    nc.sync.dma_start(tab_planes[hf][32 * q : 32 * q + 4, 2, :], picked[48 + 4 * q : 52 + 4 * q, :])
+                else:
+                    nc.sync.dma_start(tab_planes[hf][32 * q : 32 * q + 4, 0:2, :], picked[64 + 8 * q : 72 + 8 * q, :])
+
+        words.append(placed([P, T], I32, "words2", 44))
+        move_scales(0, False)
+        load_words(2, 0, T // 2)
+        move_scales(0, True)
+        load_words(2, T // 2, T)
+
+        gathered = [placed([P, S], U32, "gathered%d" % a, 63 + 4 * a) for a in range(PASSES)]
 
         def gather_words(a, lo, hi):
             nc.vector.tensor_copy(
                 gathered[a][:, lo:hi], words[a][:].bitcast(U32).indirect(idx[:, lo // 16 : hi // 16])
             )
 
-        nc.vector.tensor_copy(picked_rows[:], scale_rows[:].bitcast(U8).indirect(idx[:]))
-
-        def move_scales(hf):
-            for q in QUADRANTS:
-                nc.sync.dma_start(
-                    tab_planes[hf][32 * q : 32 * q + 4, :, :],
-                    picked_rows[32 + 16 * q : 48 + 16 * q, hf * HALF : (hf + 1) * HALF].bitcast(I32),
-                )
-
-        move_scales(0)
-        words.append(big.tile([P, T], I32, name="words2", tag="a", align_bytes=64))
-        load_words(2)
+        gather_words(0, 0, S)
+        wkw = keep.tile([P, PACK, PASSES * P], U16, name="wkw", align_bytes=64)
         nc.vector.tensor_copy(wkw[:], wkw_raw[:].bitcast(U16).rearrange("p (m t) -> p t m", t=PACK))
         wks = keep.tile([P, PACK, PASSES * P], U8, name="wks", align_bytes=64)
         nc.vector.tensor_copy(wks[:], wks_raw[:].bitcast(U8).rearrange("p (m t) -> p t m", t=PACK))
-        gather_words(0, 0, S)
-        tab_planes.append(shared.tile([P, 4, HALF // 4], I32, name="tab_planes1", offset=0, align_bytes=64))
-        nc.gpsimd.memset(tab_planes[1][:, 0:PASSES, :], 0)
         gather_words(1, 0, S)
+        tab_planes.append(placed([P, PASSES, HALF // 4], I32, "tab_planes1", 27.5))
+        nc.gpsimd.memset(tab_planes[1][:], 0)
         gather_words(2, 0, HALF)
         gather_words(2, HALF, S)
 
         wgs_by_plane = wgs.rearrange("(g t) j -> g t j", t=PACK)
         wg = {}
-        for t, lo, hi, offset in ((0, 0, FIRST, 2 * KIB), (0, FIRST, S, 16 * KIB), (2, 0, S, 22 * KIB)):
-            piece = shared.tile([P, 2, hi - lo], F32, name="wg%d_%d" % (t, lo), offset=offset, align_bytes=64)
+
+        def load_wgs(t, lo, hi, kib):
+            piece = placed([P, 2, hi - lo], F32, "wg%d_%d" % (t, lo), kib)
             for q in QUADRANTS:
                 nc.sync.dma_start(piece[32 * q : 32 * q + 32], wgs_by_plane[:, t : t + 2, lo:hi])
             for u in range(2):
                 wg[t + u, lo] = piece[:, u, :]
-            if hi == FIRST:
-                move_scales(1)
+
+        load_wgs(0, 0, FIRST, 16)
+        load_wgs(2, 0, HALF, 12)
+        move_scales(1, False)
+        move_scales(1, True)
+        load_wgs(0, FIRST, S, 45)
+        load_wgs(2, HALF, S, 51)
+        wo_raw = placed([P, PACK, N], F32, "wo_raw", 55)
+        nc.sync.dma_start(wo_raw[:], wo.rearrange("(p t) n -> p t n", t=PACK))
+        base_by_plane = base.rearrange("(p t) j -> p t j", t=PACK)
+        base_sb = [placed([P, PACK, T2 // 2], F32, "base0", 29)]
+        nc.sync.dma_start(base_sb[0][:], base_by_plane[:, :, 0 : T2 // 2])
 
         sums = {}
 
-        def open_piece(t, lo, hi, bank):
-            sums[t, lo] = psum.tile([P, hi - lo], F32, name="acc%d_%d" % (t, lo), tag="bank%d" % bank)
-
-        def first_product(a, t, lo, hi):
-            hf = lo // HALF
-            n = HALF if hi - lo == HALF else P
-            for c in range(lo, hi, n):
-                nc.tensor.matmul_mx(
-                    out=sums[t, lo][:, c - lo : c - lo + n],
-                    lhsT=wkw[:, t, a * P : (a + 1) * P].bitcast(U8).bitcast(FP4X4),
-                    lhsT_scale=wks[:, t, a * P : (a + 1) * P],
-                    rhs=gathered[a][:, c : c + n].bitcast(FP8X4),
-                    rhs_scale=tab_planes[hf][:, a, :].bitcast(U8)[:, c - hf * HALF : c - hf * HALF + n],
-                    start=(a == 0 and c == lo),
-                    stop=(a == PASSES - 1 and c + n == hi),
-                )
-
         def first_products(pieces):
             for t, lo, hi, bank in pieces:
-                open_piece(t, lo, hi, bank)
+                sums[t, lo] = psum.tile([P, hi - lo], F32, name="acc%d_%d" % (t, lo), tag="bank%d" % bank)
             for a in range(PASSES):
                 for t, lo, hi, bank in pieces:
-                    first_product(a, t, lo, hi)
+                    hf = lo // HALF
+                    n = HALF if hi - lo == HALF else P
+                    for c in range(lo, hi, n):
+                        nc.tensor.matmul_mx(
+                            out=sums[t, lo][:, c - lo : c - lo + n],
+                            lhsT=wkw[:, t, a * P : (a + 1) * P].bitcast(U8).bitcast(FP4X4),
+                            lhsT_scale=wks[:, t, a * P : (a + 1) * P],
+                            rhs=gathered[a][:, c : c + n].bitcast(FP8X4),
+                            rhs_scale=tab_planes[hf][:, a, :].bitcast(U8)[:, c - hf * HALF : c - hf * HALF + n],
+                            start=(a == 0 and c == lo),
+                            stop=(a == PASSES - 1 and c + n == hi),
+                        )
 
-        first_products(((0, 0, FIRST, 0), (1, 0, HALF, 1), (0, FIRST, HALF, 2)))
-        first_products(((0, HALF, S, 3), (1, HALF, S, 4)))
-        first_products(((2, 0, HALF, 5), (3, 0, HALF, 6)))
-
-        wo_raw = big.tile([P, PACK, N], F32, name="wo_raw", tag="a", align_bytes=64)
-        nc.sync.dma_start(wo_raw[:], wo.rearrange("(p t) n -> p t n", t=PACK))
-        hs = keep.tile([P, PACK, S], F32, name="hs")
+        hs = placed([P, PACK, S], F32, "hs", 124)
 
         def root(t, lo, hi):
             first = lo if (t, lo) in sums else 0
@@ -166,46 +175,30 @@ def tile_list_kmer_locus_coverage_kernel(
         def lift(t, lo, hi):
             nc.scalar.activation(lifted[:, t, lo:hi], pages[t][:, lo:hi], ACT.Copy, bias=1.0)
 
-        pages = {}
-
-        def clear_page(t):
-            if t == 3:
-                pages[t] = shared.tile([P, T2], F32, name="page3", offset=30 * KIB, align_bytes=64)
-            else:
-                pages[t] = big.tile([P, T2], F32, name="page%d" % t, tag="pdq"[t], align_bytes=64)
-            nc.gpsimd.memset(pages[t][:], 0.0)
-
+        first_products(((0, 0, FIRST, 0), (1, 0, HALF, 1), (2, 0, HALF, 2), (3, 0, HALF, 3), (0, FIRST, HALF, 4)))
         for t in range(PACK):
-            clear_page(t)
-        for t in (0, 1):
-            root(t, 0, FIRST)
-            scatter(t, 0, FIRST)
-        for t in (0, 1):
-            root(t, FIRST, HALF)
-            root(t, HALF, S)
-            scatter(t, FIRST, S)
-        first_products(((2, HALF, S, 7), (3, HALF, S, 0)))
-        for t in (2, 3):
-            root(t, 0, HALF)
+            hi = FIRST if t < 2 else HALF
+            root(t, 0, hi)
+            scatter(t, 0, hi)
+        base_sb.append(placed([P, PACK, T2 // 2], F32, "base1", 0))
+        nc.sync.dma_start(base_sb[1][:], base_by_plane[:, :, T2 // 2 : T2])
+        first_products(((0, HALF, S, 5), (1, HALF, S, 6), (2, HALF, S, 7), (3, HALF, S, 0)))
+        for t in range(PACK):
+            if t < 2:
+                root(t, FIRST, HALF)
             root(t, HALF, S)
         wo_bf = keep.tile([P, N, PACK], BF16, name="wo_bf", align_bytes=64)
         wo_scales = keep.tile([P, N], U8, name="wo_scales", align_bytes=64)
         nc.scalar.copy(wo_bf[:], wo_raw[:].rearrange("p t n -> p n t"))
-        lifted = big.tile([P, PACK, T2], F32, name="lifted", tag="a", align_bytes=64)
-        lift(0, 0, T2)
-        base_by_plane = base.rearrange("(p t) j -> p t j", t=PACK)
-        base_sb = [big.tile([P, PACK, T2 // 2], F32, name="base%d" % u, tag="gh"[u], align_bytes=64) for u in range(2)]
-        for u in range(2):
-            nc.sync.dma_start(base_sb[u][:], base_by_plane[:, :, u * (T2 // 2) : (u + 1) * (T2 // 2)])
-
-        scatter(2, 0, S)
-        lift(1, 0, T2)
-        scatter(3, 0, S)
-        wo_codes = shared.tile([P, N], U32, name="wo_codes", offset=22 * KIB, align_bytes=64)
+        lifted = placed([P, PACK, T2], F32, "lifted", 60)
+        for t in range(PACK):
+            scatter(t, FIRST if t < 2 else HALF, S)
+            if t < PACK - 1:
+                lift(t, 0, T2)
+        wo_codes = placed([P, N], U32, "wo_codes", 51)
         nc.vector.quantize_mx(
             out=wo_codes[:].bitcast(FP8X4), scales=wo_scales[:], in_=wo_bf[:].rearrange("p n t -> p (n t)")
         )
-        lift(2, 0, T2)
 
         out_view = out.rearrange("(m p) j -> p m j", p=P)
         widths = [CHUNK] * (T2 // CHUNK - 1) + [CHUNK // 2] * 2

@@ -43,61 +43,52 @@ def tile_list_kmer_locus_coverage_kernel(
 
         idx = keep.tile([P, S // 16], U16, name="idx")
         idx2 = keep.tile([P, S // 16], U16, name="idx2")
-        words = [placed([P, T], I32, "words0", 12)]
-        scale_rows = placed([P, T // 4], I32, "scale_rows", 59.5)
-        one = placed([P, 1], F32, "one", 30)
+        words = [placed([P, T], I32, "words%d" % a, 12 + 16 * a) for a in range(PASSES)]
+        scale_rows = placed([P, T // 4], I32, "scale_rows", 107.5)
+        one = keep.tile([P, 1], F32, name="one")
         wkw_raw = keep.tile([P, PASSES * (H // 2)], I32, name="wkw_raw", align_bytes=64)
-        wks_raw = keep.tile([P, PASSES * (H // 4)], I32, name="wks_raw", align_bytes=64)
+        wks_raw = placed([P, PASSES * (H // 4)], I32, "wks_raw", 67)
         tab_planes = [keep.tile([P, PASSES, HALF // 4], I32, name="tab_planes0", align_bytes=64)]
         floor = keep.tile([P, 1], F32, name="floor")
 
         def load_words(a, lo, hi):
             nc.sync.dma_start(words[a][:, lo:hi], tab_words[a].rearrange("p t i -> p (t i)").bitcast(I32)[:, lo:hi])
 
-        nc.gpsimd.memset(wks_raw[:], 0)
-        nc.vector.memset(one[:], 1.0)
         load_words(0, 0, T // 2)
         nc.sync.dma_start(idx[:], offs)
+        nc.sync.dma_start(scale_rows[48:96, :], tab_scales.bitcast(I32).rearrange("a q c -> q a c"))
         nc.sync.dma_start(idx2[:], offs2)
-        rows = tab_scales.bitcast(I32)
-        nc.sync.dma_start(scale_rows[64:96, :], rows.rearrange("a q c -> q a c")[:, 0:2, :])
-        nc.sync.dma_start(scale_rows[48:64, :], rows[2])
         load_words(0, T // 2, T)
         nc.sync.dma_start(
             wkw_raw[:].rearrange("p (a c) -> p a c", a=PASSES), wk_words.bitcast(I32).rearrange("a p c -> p a c")
         )
+        load_words(1, 0, T)
+        load_words(2, 0, T)
+        nc.vector.memset(one[:], 1.0)
+        nc.scalar.activation(floor[:], one[:], ACT.Sqrt, scale=2.0**-116)
+
+        nc.gpsimd.memset(wks_raw[:], 0)
         for q in QUADRANTS:
-            nc.sync.dma_start(
+            nc.gpsimd.dma_start(
                 wks_raw[32 * q : 32 * q + 4, :].rearrange("p (a c) -> p a c", a=PASSES),
                 wk_scales[:, 4 * q : 4 * q + 4, :].bitcast(I32).rearrange("a r c -> r a c"),
             )
-        nc.scalar.activation(floor[:], one[:], ACT.Sqrt, scale=2.0**-116)
-        words.append(placed([P, T], I32, "words1", 28))
-        load_words(1, 0, T)
-
-        nc.gpsimd.memset(scale_rows[0:48, :], 0)
-        nc.gpsimd.memset(scale_rows[96:128, :], 0)
-        nc.gpsimd.memset(tab_planes[0][:], 0)
-        pages = [placed([P, T2], F32, "page%d" % t, 92 + 8 * t) for t in range(PACK)]
-        for t in range(PACK):
-            nc.gpsimd.memset(pages[t][:], 0.0)
+        nc.vector.memset(scale_rows[0:48, :], 0)
+        nc.vector.memset(scale_rows[96:128, :], 0)
+        nc.vector.memset(tab_planes[0][:], 0)
 
         picked_rows = keep.tile([P, S], U8, name="picked_rows", align_bytes=64)
         nc.vector.tensor_copy(picked_rows[:], scale_rows[:].bitcast(U8).indirect(idx[:]))
 
-        def move_scales(hf, last):
+        def move_scales(hf, queue):
             picked = picked_rows[:, hf * HALF : (hf + 1) * HALF].bitcast(I32)
             for q in QUADRANTS:
-                if last:
-                    nc.sync.dma_start(tab_planes[hf][32 * q : 32 * q + 4, 2, :], picked[48 + 4 * q : 52 + 4 * q, :])
-                else:
-                    nc.sync.dma_start(tab_planes[hf][32 * q : 32 * q + 4, 0:2, :], picked[64 + 8 * q : 72 + 8 * q, :])
+                queue.dma_start(tab_planes[hf][32 * q : 32 * q + 4], picked[48 + 12 * q : 60 + 12 * q, :])
 
-        words.append(placed([P, T], I32, "words2", 44))
-        move_scales(0, False)
-        load_words(2, 0, T // 2)
-        move_scales(0, True)
-        load_words(2, T // 2, T)
+        move_scales(0, nc.gpsimd)
+        pages = [placed([P, T2], F32, "page%d" % t, (92, 100, 109.5, 18)[t]) for t in range(PACK)]
+        for t in range(PACK):
+            nc.gpsimd.memset(pages[t][:], 0.0)
 
         gathered = [placed([P, S], U32, "gathered%d" % a, 63 + 4 * a) for a in range(PASSES)]
 
@@ -107,13 +98,13 @@ def tile_list_kmer_locus_coverage_kernel(
             )
 
         gather_words(0, 0, S)
-        wkw = keep.tile([P, PACK, PASSES * P], U16, name="wkw", align_bytes=64)
+        wkw = placed([P, PACK, PASSES * P], U16, "wkw", 140)
         nc.vector.tensor_copy(wkw[:], wkw_raw[:].bitcast(U16).rearrange("p (m t) -> p t m", t=PACK))
-        wks = keep.tile([P, PACK, PASSES * P], U8, name="wks", align_bytes=64)
+        wks = placed([P, PACK, PASSES * P], U8, "wks", 108)
         nc.vector.tensor_copy(wks[:], wks_raw[:].bitcast(U8).rearrange("p (m t) -> p t m", t=PACK))
         gather_words(1, 0, S)
         tab_planes.append(placed([P, PASSES, HALF // 4], I32, "tab_planes1", 27.5))
-        nc.gpsimd.memset(tab_planes[1][:], 0)
+        nc.vector.memset(tab_planes[1][:], 0)
         gather_words(2, 0, HALF)
         gather_words(2, HALF, S)
 
@@ -129,8 +120,7 @@ def tile_list_kmer_locus_coverage_kernel(
 
         load_wgs(0, 0, FIRST, 16)
         load_wgs(2, 0, HALF, 12)
-        move_scales(1, False)
-        move_scales(1, True)
+        move_scales(1, nc.sync)
         load_wgs(0, FIRST, S, 45)
         load_wgs(2, HALF, S, 51)
         wo_raw = placed([P, PACK, N], F32, "wo_raw", 55)
@@ -187,7 +177,7 @@ def tile_list_kmer_locus_coverage_kernel(
             if t < 2:
                 root(t, FIRST, HALF)
             root(t, HALF, S)
-        wo_bf = keep.tile([P, N, PACK], BF16, name="wo_bf", align_bytes=64)
+        wo_bf = placed([P, N, PACK], BF16, "wo_bf", 140)
         wo_scales = keep.tile([P, N], U8, name="wo_scales", align_bytes=64)
         nc.scalar.copy(wo_bf[:], wo_raw[:].rearrange("p t n -> p n t"))
         lifted = placed([P, PACK, T2], F32, "lifted", 60)

@@ -44,7 +44,7 @@ def tile_list_kmer_locus_coverage_kernel(
         idx = keep.tile([P, S // 16], U16, name="idx")
         idx2 = keep.tile([P, S // 16], U16, name="idx2")
         words = [placed([P, T], I32, "words%d" % a, 12 + 16 * a) for a in range(PASSES)]
-        scale_rows = placed([P, T // 4], I32, "scale_rows", 107.5)
+        scale_rows = placed([P, T // 4], I32, "scale_rows", 60)
         one = keep.tile([P, 1], F32, name="one")
         wkw_raw = keep.tile([P, PASSES * (H // 2)], I32, name="wkw_raw", align_bytes=64)
         wks_raw = placed([P, PASSES * (H // 4)], I32, "wks_raw", 67)
@@ -54,28 +54,26 @@ def tile_list_kmer_locus_coverage_kernel(
         def load_words(a, lo, hi):
             nc.sync.dma_start(words[a][:, lo:hi], tab_words[a].rearrange("p t i -> p (t i)").bitcast(I32)[:, lo:hi])
 
-        load_words(0, 0, T // 2)
-        nc.sync.dma_start(idx[:], offs)
-        nc.sync.dma_start(scale_rows[48:96, :], tab_scales.bitcast(I32).rearrange("a q c -> q a c"))
-        nc.sync.dma_start(idx2[:], offs2)
-        load_words(0, T // 2, T)
+        nc.gpsimd.memset(wks_raw[:], 0)
         nc.sync.dma_start(
             wkw_raw[:].rearrange("p (a c) -> p a c", a=PASSES), wk_words.bitcast(I32).rearrange("a p c -> p a c")
         )
+        nc.sync.dma_start(idx[:], offs)
+        nc.sync.dma_start(idx2[:], offs2)
+        for q in QUADRANTS:
+            nc.sync.dma_start(
+                wks_raw[32 * q : 32 * q + 4, :].rearrange("p (a c) -> p a c", a=PASSES),
+                wk_scales[:, 4 * q : 4 * q + 4, :].bitcast(I32).rearrange("a r c -> r a c"),
+            )
+        load_words(0, 0, T)
+        nc.sync.dma_start(scale_rows[48:96, :], tab_scales.bitcast(I32).rearrange("a q c -> q a c"))
         load_words(1, 0, T)
         load_words(2, 0, T)
         nc.vector.memset(one[:], 1.0)
         nc.scalar.activation(floor[:], one[:], ACT.Sqrt, scale=2.0**-116)
-
-        nc.gpsimd.memset(wks_raw[:], 0)
-        for q in QUADRANTS:
-            nc.gpsimd.dma_start(
-                wks_raw[32 * q : 32 * q + 4, :].rearrange("p (a c) -> p a c", a=PASSES),
-                wk_scales[:, 4 * q : 4 * q + 4, :].bitcast(I32).rearrange("a r c -> r a c"),
-            )
-        nc.vector.memset(scale_rows[0:48, :], 0)
-        nc.vector.memset(scale_rows[96:128, :], 0)
-        nc.vector.memset(tab_planes[0][:], 0)
+        nc.gpsimd.memset(scale_rows[0:48, :], 0)
+        nc.gpsimd.memset(scale_rows[96:128, :], 0)
+        nc.gpsimd.memset(tab_planes[0][:], 0)
 
         picked_rows = keep.tile([P, S], U8, name="picked_rows", align_bytes=64)
         nc.vector.tensor_copy(picked_rows[:], scale_rows[:].bitcast(U8).indirect(idx[:]))
@@ -85,8 +83,8 @@ def tile_list_kmer_locus_coverage_kernel(
             for q in QUADRANTS:
                 queue.dma_start(tab_planes[hf][32 * q : 32 * q + 4], picked[48 + 12 * q : 60 + 12 * q, :])
 
-        move_scales(0, nc.gpsimd)
-        pages = [placed([P, T2], F32, "page%d" % t, (92, 100, 109.5, 18)[t]) for t in range(PACK)]
+        move_scales(0, nc.sync)
+        pages = [placed([P, T2], F32, "page%d" % t, 92 + 8 * t) for t in range(PACK)]
         for t in range(PACK):
             nc.gpsimd.memset(pages[t][:], 0.0)
 
@@ -100,11 +98,11 @@ def tile_list_kmer_locus_coverage_kernel(
         gather_words(0, 0, S)
         wkw = placed([P, PACK, PASSES * P], U16, "wkw", 140)
         nc.vector.tensor_copy(wkw[:], wkw_raw[:].bitcast(U16).rearrange("p (m t) -> p t m", t=PACK))
-        wks = placed([P, PACK, PASSES * P], U8, "wks", 108)
+        wks = placed([P, PACK, PASSES * P], U8, "wks", 75)
         nc.vector.tensor_copy(wks[:], wks_raw[:].bitcast(U8).rearrange("p (m t) -> p t m", t=PACK))
         gather_words(1, 0, S)
         tab_planes.append(placed([P, PASSES, HALF // 4], I32, "tab_planes1", 27.5))
-        nc.vector.memset(tab_planes[1][:], 0)
+        nc.gpsimd.memset(tab_planes[1][:], 0)
         gather_words(2, 0, HALF)
         gather_words(2, HALF, S)
 
@@ -134,8 +132,8 @@ def tile_list_kmer_locus_coverage_kernel(
         def first_products(pieces):
             for t, lo, hi, bank in pieces:
                 sums[t, lo] = psum.tile([P, hi - lo], F32, name="acc%d_%d" % (t, lo), tag="bank%d" % bank)
-            for a in range(PASSES):
-                for t, lo, hi, bank in pieces:
+            for t, lo, hi, bank in pieces:
+                for a in range(PASSES):
                     hf = lo // HALF
                     n = HALF if hi - lo == HALF else P
                     for c in range(lo, hi, n):

@@ -151,7 +151,8 @@ def tile_list_kmer_locus_coverage_kernel(
 
         def root(t, lo, hi):
             first = lo if (t, lo) in sums else 0
-            mag = ring.tile([P, hi - lo], F32, name="mag")
+            pool = keep if lo == 0 else ring
+            mag = pool.tile([P, hi - lo], F32, name="mag")
             nc.scalar.activation(mag[:], sums[t, first][:, lo - first : hi - first], ACT.Abs)
             nc.scalar.activation(hs[:, t, lo:hi], mag[:], ACT.Sqrt, bias=floor[:])
 
@@ -163,11 +164,17 @@ def tile_list_kmer_locus_coverage_kernel(
         def lift(t, lo, hi):
             nc.scalar.activation(lifted[:, t, lo:hi], pages[t][:, lo:hi], ACT.Copy, bias=1.0)
 
-        first_products(((0, 0, FIRST, 0), (1, 0, HALF, 1), (2, 0, HALF, 2), (3, 0, HALF, 3), (0, FIRST, HALF, 4)))
-        for t in range(PACK):
-            hi = FIRST if t < 2 else HALF
-            root(t, 0, hi)
-            scatter(t, 0, hi)
+        first_products(((0, 0, P, 0), (0, P, FIRST, 1), (1, 0, FIRST, 2)))
+        root(0, 0, P)
+        root(0, P, FIRST)
+        scatter(0, 0, FIRST)
+        root(1, 0, FIRST)
+        scatter(1, 0, FIRST)
+        for t in (2, 3):
+            first_products(((t, 0, HALF, t + 1),))
+            root(t, 0, HALF)
+            scatter(t, 0, HALF)
+        first_products(((0, FIRST, HALF, 3), (1, FIRST, HALF, 4)))
         base_sb.append(placed([P, PACK, T2 // 2], F32, "base1", 0))
         nc.sync.dma_start(base_sb[1][:], base_by_plane[:, :, T2 // 2 : T2])
         first_products(((0, HALF, S, 5), (1, HALF, S, 6), (2, HALF, S, 7), (3, HALF, S, 0)))
@@ -189,7 +196,7 @@ def tile_list_kmer_locus_coverage_kernel(
         )
 
         out_view = out.rearrange("(m p) j -> p m j", p=P)
-        widths = [CHUNK] * (T2 // CHUNK - 1) + [CHUNK // 2] * 2
+        widths = [CHUNK // 2] * 2 + [CHUNK] * (T2 // CHUNK - 3) + [CHUNK // 2] * 4
         starts = [sum(widths[:c]) for c in range(len(widths))]
         chunks = len(widths)
         zs = {}
@@ -219,10 +226,11 @@ def tile_list_kmer_locus_coverage_kernel(
             codes, scales = zq[c]
             lo, w = starts[c], widths[c]
             staged = stage.tile([P, PACK, w], F32, name="staged", align_bytes=64)
-            for pair in range(2):
-                acc = psum.tile([P, 2, w], F32, name="track", tag="bank%d" % ((2 * c + pair) % BANKS))
-                for u in range(2):
-                    m = 2 * pair + u
+            group = PACK if w < CHUNK and c < chunks - 2 else 2
+            for first in range(0, PACK, group):
+                acc = psum.tile([P, group, w], F32, name="track", tag="bank%d" % ((2 * c + first // 2) % BANKS))
+                for u in range(group):
+                    m = first + u
                     nc.tensor.matmul_mx(
                         out=acc[:, u, :],
                         lhsT=wo_codes[:, P * m : P * (m + 1)].bitcast(FP8X4),
@@ -232,15 +240,13 @@ def tile_list_kmer_locus_coverage_kernel(
                         start=True,
                         stop=True,
                     )
-                if c >= chunks - 2 and pair == 1:
-                    nc.vector.tensor_copy(staged[:, 2 * pair : 2 * pair + 2, :], acc[:])
+                if c >= chunks - 2 and first == 2:
+                    nc.vector.tensor_copy(staged[:, first : first + group, :], acc[:])
                 else:
-                    nc.scalar.copy(staged[:, 2 * pair : 2 * pair + 2, :], acc[:])
-                nc.sync.dma_start(
-                    out_view[:, 2 * pair : 2 * pair + 2, lo : lo + w], staged[:, 2 * pair : 2 * pair + 2, :]
-                )
+                    nc.scalar.copy(staged[:, first : first + group, :], acc[:])
+                nc.sync.dma_start(out_view[:, first : first + group, lo : lo + w], staged[:, first : first + group, :])
 
-        for lo, hi in ((0, CHUNK), (CHUNK, 2 * CHUNK), (2 * CHUNK, 4 * CHUNK), (4 * CHUNK, T2)):
+        for lo, hi in ((0, CHUNK // 2), (CHUNK // 2, CHUNK), (CHUNK, 2 * CHUNK), (2 * CHUNK, 4 * CHUNK), (4 * CHUNK, T2)):
             lift(3, lo, hi)
         make_z(0)
         for c in range(chunks):

@@ -196,61 +196,70 @@ def tile_list_kmer_locus_coverage_kernel(
         )
 
         out_view = out.rearrange("(m p) j -> p m j", p=P)
-        widths = [CHUNK // 2] * 2 + [CHUNK] * (T2 // CHUNK - 3) + [CHUNK // 2] * 4
-        starts = [sum(widths[:c]) for c in range(len(widths))]
-        chunks = len(widths)
+        chunks = T2 // CHUNK
         zs = {}
         zq = {}
 
-        def make_z(c):
-            lo, w = starts[c], widths[c]
+        def make_z(c, part):
+            if part == 0:
+                zs[c] = ring.tile([P, CHUNK, PACK], BF16, name="z", align_bytes=64)
+            lo = c * CHUNK + part * P
             blo = lo % (T2 // 2)
-            z = ring.tile([P, w, PACK], BF16, name="z", align_bytes=64)
             nc.vector.tensor_tensor(
-                z[:].rearrange("p (c i) t -> p c t i", i=2),
-                lifted[:, :, lo : lo + w].rearrange("p t (c i) -> p c t i", i=2),
-                base_sb[lo // (T2 // 2)][:, :, blo : blo + w].rearrange("p t (c i) -> p c t i", i=2),
+                zs[c][:, part * P : (part + 1) * P, :].rearrange("p (c i) t -> p c t i", i=2),
+                lifted[:, :, lo : lo + P].rearrange("p t (c i) -> p c t i", i=2),
+                base_sb[lo // (T2 // 2)][:, :, blo : blo + P].rearrange("p t (c i) -> p c t i", i=2),
                 MULT,
             )
-            zs[c] = z
 
-        def quantise_z(c):
-            codes = ring.tile([P, widths[c]], U32, name="z_codes", align_bytes=64)
-            scales = ring.tile([P, widths[c]], U8, name="z_scales", align_bytes=64)
-            nc.vector.quantize_mx(
-                out=codes[:].bitcast(FP8X4), scales=scales[:], in_=zs[c][:].rearrange("p j t -> p (j t)")
-            )
-            zq[c] = (codes, scales)
-
-        def second_product(c):
+        def quantise_z(c, lo, hi):
+            if lo == 0:
+                codes = ring.tile([P, CHUNK], U32, name="z_codes", align_bytes=64)
+                scales = ring.tile([P, CHUNK], U8, name="z_scales", align_bytes=64)
+                zq[c] = (codes, scales)
             codes, scales = zq[c]
-            lo, w = starts[c], widths[c]
-            staged = stage.tile([P, PACK, w], F32, name="staged", align_bytes=64)
-            group = PACK if w < CHUNK and c < chunks - 2 else 2
-            for first in range(0, PACK, group):
-                acc = psum.tile([P, group, w], F32, name="track", tag="bank%d" % ((2 * c + first // 2) % BANKS))
-                for u in range(group):
-                    m = first + u
+            nc.vector.quantize_mx(
+                out=codes[:, lo:hi].bitcast(FP8X4),
+                scales=scales[:, lo:hi],
+                in_=zs[c][:, lo:hi, :].rearrange("p j t -> p (j t)"),
+            )
+
+        def second_product(c, group, n):
+            codes, scales = zq[c]
+            lo = c * CHUNK
+            staged = stage.tile([P, PACK, CHUNK], F32, name="staged", align_bytes=64)
+            accs = [
+                psum.tile([P, group, CHUNK], F32, name="track", tag="bank%d" % ((2 * c + b) % BANKS))
+                for b in range(PACK // group)
+            ]
+            for col in range(0, CHUNK, n):
+                for m in range(PACK):
                     nc.tensor.matmul_mx(
-                        out=acc[:, u, :],
+                        out=accs[m // group][:, m % group, col : col + n],
                         lhsT=wo_codes[:, P * m : P * (m + 1)].bitcast(FP8X4),
                         lhsT_scale=wo_scales[:, P * m : P * (m + 1)],
-                        rhs=codes[:].bitcast(FP8X4),
-                        rhs_scale=scales[:],
+                        rhs=codes[:, col : col + n].bitcast(FP8X4),
+                        rhs_scale=scales[:, col : col + n],
                         start=True,
                         stop=True,
                     )
-                if c >= chunks - 2 and first == 2:
-                    nc.vector.tensor_copy(staged[:, first : first + group, :], acc[:])
+            for b in range(PACK // group):
+                tiles = slice(b * group, (b + 1) * group)
+                if group == 1 and b % 2 == 1:
+                    nc.vector.tensor_copy(staged[:, tiles, :], accs[b][:])
                 else:
-                    nc.scalar.copy(staged[:, first : first + group, :], acc[:])
-                nc.sync.dma_start(out_view[:, first : first + group, lo : lo + w], staged[:, first : first + group, :])
+                    nc.scalar.copy(staged[:, tiles, :], accs[b][:])
+                nc.sync.dma_start(out_view[:, tiles, lo : lo + CHUNK], staged[:, tiles, :])
 
-        for lo, hi in ((0, CHUNK // 2), (CHUNK // 2, CHUNK), (CHUNK, 2 * CHUNK), (2 * CHUNK, 4 * CHUNK), (4 * CHUNK, T2)):
+        for lo, hi in ((0, P), (P, CHUNK), (CHUNK, 2 * CHUNK), (2 * CHUNK, 4 * CHUNK), (4 * CHUNK, T2)):
             lift(3, lo, hi)
-        make_z(0)
-        for c in range(chunks):
-            if c + 1 < chunks:
-                make_z(c + 1)
-            quantise_z(c)
-            second_product(c)
+        make_z(0, 0)
+        make_z(0, 1)
+        for c in range(chunks - 1):
+            make_z(c + 1, 0)
+            quantise_z(c, 0, CHUNK)
+            second_product(c, 2, CHUNK)
+            make_z(c + 1, 1)
+        quantise_z(chunks - 1, 0, P)
+        quantise_z(chunks - 1, P, CHUNK)
+        second_product(chunks - 1, 1, P)

@@ -15,6 +15,7 @@ FP8X4 = mybir.dt.float8_e4m3fn_x4
 FP4X4 = mybir.dt.float4_e2m1fn_x4
 ACT = mybir.ActivationFunctionType
 MULT = mybir.AluOpType.mult
+ADD = mybir.AluOpType.add
 
 P = 128
 PACK = 4
@@ -22,6 +23,7 @@ PASSES = K // (P * PACK)
 HALF = 512
 FIRST = 256
 CHUNK = 256
+SHARED = 6
 BANKS = 8
 KIB = 1024
 QUADRANTS = (0, 2, 1, 3)
@@ -44,10 +46,10 @@ def tile_list_kmer_locus_coverage_kernel(
         idx = keep.tile([P, S // 16], U16, name="idx")
         idx2 = keep.tile([P, S // 16], U16, name="idx2")
         words = [placed([P, T], I32, "words%d" % a, 12 + 16 * a) for a in range(PASSES)]
-        scale_rows = placed([P, T // 4], I32, "scale_rows", 60)
+        scale_rows = placed([P, T // 4], I32, "scale_rows", 64)
         one = keep.tile([P, 1], F32, name="one")
         wkw_raw = keep.tile([P, PASSES * (H // 2)], I32, name="wkw_raw", align_bytes=64)
-        wks_raw = placed([P, PASSES * (H // 4)], I32, "wks_raw", 67)
+        wks_raw = placed([P, PASSES * (H // 4)], I32, "wks_raw", 71)
         tab_planes = [keep.tile([P, PASSES, HALF // 4], I32, name="tab_planes0", align_bytes=64)]
         floor = keep.tile([P, 1], F32, name="floor")
 
@@ -88,7 +90,7 @@ def tile_list_kmer_locus_coverage_kernel(
         for t in range(PACK):
             nc.gpsimd.memset(pages[t][:], 0.0)
 
-        gathered = [placed([P, S], U32, "gathered%d" % a, 63 + 4 * a) for a in range(PASSES)]
+        gathered = [placed([P, S], U32, "gathered%d" % a, 67 + 4 * a) for a in range(PASSES)]
 
         def gather_words(a, lo, hi):
             nc.vector.tensor_copy(
@@ -98,7 +100,7 @@ def tile_list_kmer_locus_coverage_kernel(
         gather_words(0, 0, S)
         wkw = placed([P, PACK, PASSES * P], U16, "wkw", 140)
         nc.vector.tensor_copy(wkw[:], wkw_raw[:].bitcast(U16).rearrange("p (m t) -> p t m", t=PACK))
-        wks = placed([P, PACK, PASSES * P], U8, "wks", 75)
+        wks = placed([P, PACK, PASSES * P], U8, "wks", 79)
         nc.vector.tensor_copy(wks[:], wks_raw[:].bitcast(U8).rearrange("p (m t) -> p t m", t=PACK))
         gather_words(1, 0, S)
         tab_planes.append(placed([P, PASSES, HALF // 4], I32, "tab_planes1", 27.5))
@@ -109,19 +111,21 @@ def tile_list_kmer_locus_coverage_kernel(
         wgs_by_plane = wgs.rearrange("(g t) j -> g t j", t=PACK)
         wg = {}
 
-        def load_wgs(t, lo, hi, kib):
-            piece = placed([P, 2, hi - lo], F32, "wg%d_%d" % (t, lo), kib)
+        def load_wgs(t, planes, lo, hi, kib):
+            piece = placed([P, planes, hi - lo], F32, "wg%d_%d" % (t, lo), kib)
             for q in QUADRANTS:
-                nc.sync.dma_start(piece[32 * q : 32 * q + 32], wgs_by_plane[:, t : t + 2, lo:hi])
-            for u in range(2):
+                nc.sync.dma_start(piece[32 * q : 32 * q + 32], wgs_by_plane[:, t : t + planes, lo:hi])
+            for u in range(planes):
                 wg[t + u, lo] = piece[:, u, :]
 
-        load_wgs(0, 0, FIRST, 16)
-        load_wgs(2, 0, HALF, 12)
+        load_wgs(0, 2, 0, FIRST, 16)
+        load_wgs(0, 2, FIRST, HALF, 14)
+        load_wgs(2, 1, 0, HALF, 12)
         move_scales(1, nc.sync)
-        load_wgs(0, FIRST, S, 45)
-        load_wgs(2, HALF, S, 51)
-        wo_raw = placed([P, PACK, N], F32, "wo_raw", 55)
+        load_wgs(0, 2, HALF, S, 45)
+        load_wgs(2, 1, HALF, S, 49)
+        load_wgs(3, 1, 0, S, 51)
+        wo_raw = placed([P, PACK, N], F32, "wo_raw", 59)
         nc.sync.dma_start(wo_raw[:], wo.rearrange("(p t) n -> p t n", t=PACK))
         base_by_plane = base.rearrange("(p t) j -> p t j", t=PACK)
         base_sb = [placed([P, PACK, T2 // 2], F32, "base0", 29)]
@@ -149,66 +153,107 @@ def tile_list_kmer_locus_coverage_kernel(
 
         hs = placed([P, PACK, S], F32, "hs", 124)
 
-        def root(t, lo, hi):
-            first = lo if (t, lo) in sums else 0
-            pool = keep if lo == 0 else ring
-            mag = pool.tile([P, hi - lo], F32, name="mag")
-            nc.scalar.activation(mag[:], sums[t, first][:, lo - first : hi - first], ACT.Abs)
+        def root(t, lo, hi, pool, tag="mag"):
+            mag = pool.tile([P, hi - lo], F32, name=tag)
+            nc.scalar.activation(mag[:], sums[t, lo][:], ACT.Abs)
             nc.scalar.activation(hs[:, t, lo:hi], mag[:], ACT.Sqrt, bias=floor[:])
 
-        def scatter(t, lo, hi):
+        def scatter_fused(t, lo, hi):
             nc.vector.tensor_tensor(
                 pages[t][:].indirect(idx2[:, lo // 16 : hi // 16]), hs[:, t, lo:hi], wg[t, lo], MULT
             )
 
-        def lift(t, lo, hi):
-            nc.scalar.activation(lifted[:, t, lo:hi], pages[t][:, lo:hi], ACT.Copy, bias=1.0)
+        def weigh(engine, t, lo, hi, weights):
+            engine.tensor_tensor(hs[:, t, lo:hi], hs[:, t, lo:hi], weights, MULT)
+
+        def scatter(t, lo, hi):
+            nc.vector.tensor_copy(pages[t][:].indirect(idx2[:, lo // 16 : hi // 16]), hs[:, t, lo:hi])
 
         first_products(((0, 0, P, 0), (0, P, FIRST, 1), (1, 0, FIRST, 2)))
-        root(0, 0, P)
-        root(0, P, FIRST)
-        scatter(0, 0, FIRST)
-        root(1, 0, FIRST)
-        scatter(1, 0, FIRST)
-        for t in (2, 3):
-            first_products(((t, 0, HALF, t + 1),))
-            root(t, 0, HALF)
-            scatter(t, 0, HALF)
-        first_products(((0, FIRST, HALF, 3), (1, FIRST, HALF, 4)))
+        root(0, 0, P, keep)
+        root(0, P, FIRST, keep, "mag2")
+        scatter_fused(0, 0, FIRST)
+        root(1, 0, FIRST, keep)
+        first_products(((0, FIRST, HALF, 3), (1, FIRST, HALF, 4), (2, 0, HALF, 5)))
+        root(0, FIRST, HALF, keep, "mag2")
+        weigh(nc.vector, 0, FIRST, HALF, wg[0, FIRST])
+        scatter_fused(1, 0, FIRST)
+        scatter(0, FIRST, HALF)
+        for t, lo, hi in ((1, FIRST, HALF), (2, 0, HALF)):
+            root(t, lo, hi, keep)
+            weigh(nc.gpsimd, t, lo, hi, wg[t, lo])
+            scatter(t, lo, hi)
         base_sb.append(placed([P, PACK, T2 // 2], F32, "base1", 0))
         nc.sync.dma_start(base_sb[1][:], base_by_plane[:, :, T2 // 2 : T2])
-        first_products(((0, HALF, S, 5), (1, HALF, S, 6), (2, HALF, S, 7), (3, HALF, S, 0)))
-        for t in range(PACK):
-            if t < 2:
-                root(t, FIRST, HALF)
-            root(t, HALF, S)
+        for t, lo, bank in ((0, HALF, 6), (1, HALF, 7), (2, HALF, 0), (3, 0, 7), (3, HALF, 0)):
+            first_products(((t, lo, lo + HALF, bank),))
+            root(t, lo, lo + HALF, ring)
+            weigh(nc.gpsimd, t, lo, lo + HALF, wg[3, 0][:, lo : lo + HALF] if t == 3 else wg[t, lo])
         wo_bf = placed([P, N, PACK], BF16, "wo_bf", 140)
         wo_scales = keep.tile([P, N], U8, name="wo_scales", align_bytes=64)
         nc.scalar.copy(wo_bf[:], wo_raw[:].rearrange("p t n -> p n t"))
-        lifted = placed([P, PACK, T2], F32, "lifted", 60)
-        for t in range(PACK):
-            scatter(t, FIRST if t < 2 else HALF, S)
-            if t < PACK - 1:
-                lift(t, 0, T2)
-        wo_codes = placed([P, N], U32, "wo_codes", 51)
+
+        base_of = lambda lo: base_sb[lo // (T2 // 2)]
+        GROUP = SHARED // 2 * CHUNK
+        low = [placed([P, 2, GROUP], F32, "low%d" % u, 53.5 + 6 * u) for u in range(2)]
+        high = placed([P, 2, SHARED * CHUNK], F32, "high", 65.5)
+        zs = {}
+        ones = []
+        scatter(0, HALF, S)
+        for u in range(2):
+            nc.scalar.activation(low[u][:, 0, :], pages[0][:, u * GROUP : (u + 1) * GROUP], ACT.Copy, bias=1.0)
+        scatter(1, HALF, S)
+        for c in range(SHARED):
+            u, lo = divmod(c * CHUNK, GROUP)
+            nc.scalar.activation(
+                low[u][:, 1, lo : lo + CHUNK], pages[1][:, c * CHUNK : (c + 1) * CHUNK], ACT.Copy, bias=1.0
+            )
+            zs[c] = placed([P, CHUNK, PACK], BF16, "z%d" % c, 144 + 2 * c)
+            blo = c * CHUNK % (T2 // 2)
+            nc.gpsimd.tensor_tensor(
+                zs[c][:, :, 0:2],
+                low[u][:, :, lo : lo + CHUNK].rearrange("p t j -> p j t"),
+                base_of(c * CHUNK)[:, 0:2, blo : blo + CHUNK].rearrange("p t j -> p j t"),
+                MULT,
+            )
+            if lo + CHUNK == GROUP:
+                ones.append(placed([P, 1], F32, "ones%d" % u, 56 + 5 * u))
+                nc.gpsimd.memset(ones[u][:], 1.0)
+        scatter(2, HALF, S)
+        nc.scalar.copy(high[:, 0, :], pages[2][:, 0 : SHARED * CHUNK])
+        rest = placed([P, PACK, T2 - SHARED * CHUNK], F32, "rest", 46)
+        for t in range(PACK - 1):
+            nc.scalar.activation(rest[:, t, :], pages[t][:, SHARED * CHUNK : T2], ACT.Copy, bias=1.0)
+        scatter(3, 0, S)
+        wo_codes = placed([P, N], U32, "wo_codes", 124)
         nc.vector.quantize_mx(
             out=wo_codes[:].bitcast(FP8X4), scales=wo_scales[:], in_=wo_bf[:].rearrange("p n t -> p (n t)")
         )
 
         out_view = out.rearrange("(m p) j -> p m j", p=P)
         chunks = T2 // CHUNK
-        zs = {}
         zq = {}
 
         def make_z(c, part):
-            if part == 0:
-                zs[c] = ring.tile([P, CHUNK, PACK], BF16, name="z", align_bytes=64)
             lo = c * CHUNK + part * P
             blo = lo % (T2 // 2)
+            if c < SHARED:
+                nc.vector.scalar_tensor_tensor(
+                    zs[c][:, part * P : (part + 1) * P, 2:4],
+                    high[:, :, lo : lo + P].rearrange("p t j -> p j t"),
+                    ones[lo // GROUP][:],
+                    base_of(lo)[:, 2:4, blo : blo + P].rearrange("p t j -> p j t"),
+                    ADD,
+                    MULT,
+                )
+                return
+            if part == 0:
+                zs[c] = ring.tile([P, CHUNK, PACK], BF16, name="z", align_bytes=64)
+            rlo = lo - SHARED * CHUNK
             nc.vector.tensor_tensor(
                 zs[c][:, part * P : (part + 1) * P, :].rearrange("p (c i) t -> p c t i", i=2),
-                lifted[:, :, lo : lo + P].rearrange("p t (c i) -> p c t i", i=2),
-                base_sb[lo // (T2 // 2)][:, :, blo : blo + P].rearrange("p t (c i) -> p c t i", i=2),
+                rest[:, :, rlo : rlo + P].rearrange("p t (c i) -> p c t i", i=2),
+                base_of(lo)[:, :, blo : blo + P].rearrange("p t (c i) -> p c t i", i=2),
                 MULT,
             )
 
@@ -245,17 +290,23 @@ def tile_list_kmer_locus_coverage_kernel(
                     )
             for b in range(PACK // group):
                 tiles = slice(b * group, (b + 1) * group)
-                if group == 1 and b % 2 == 1:
+                if (group == 1 and b % 2 == 1) or (c == chunks - 2 and b == 1):
                     nc.vector.tensor_copy(staged[:, tiles, :], accs[b][:])
                 else:
                     nc.scalar.copy(staged[:, tiles, :], accs[b][:])
                 nc.sync.dma_start(out_view[:, tiles, lo : lo + CHUNK], staged[:, tiles, :])
 
-        for lo, hi in ((0, P), (P, CHUNK), (CHUNK, 2 * CHUNK), (2 * CHUNK, 4 * CHUNK), (4 * CHUNK, T2)):
-            lift(3, lo, hi)
+        for lo, hi in ((0, P), (P, CHUNK), (CHUNK, 2 * CHUNK), (2 * CHUNK, 4 * CHUNK), (4 * CHUNK, SHARED * CHUNK)):
+            nc.scalar.copy(high[:, 1, lo:hi], pages[3][:, lo:hi])
+        nc.scalar.activation(rest[:, 3, :], pages[3][:, SHARED * CHUNK : T2], ACT.Copy, bias=1.0)
         make_z(0, 0)
         make_z(0, 1)
-        for c in range(chunks - 1):
+        quantise_z(0, 0, P)
+        quantise_z(0, P, CHUNK)
+        second_product(0, 2, P)
+        make_z(1, 0)
+        make_z(1, 1)
+        for c in range(1, chunks - 1):
             make_z(c + 1, 0)
             quantise_z(c, 0, CHUNK)
             second_product(c, 2, CHUNK)

@@ -50,7 +50,7 @@ def tile_list_kmer_locus_coverage_kernel(
         one = keep.tile([P, 1], F32, name="one")
         wkw_raw = keep.tile([P, PASSES * (H // 2)], I32, name="wkw_raw", align_bytes=64)
         wks_raw = placed([P, PASSES * (H // 4)], I32, "wks_raw", 71)
-        tab_planes = [keep.tile([P, PASSES, HALF // 4], I32, name="tab_planes0", align_bytes=64)]
+        tab_planes = keep.tile([P, PASSES, S // 4], I32, name="tab_planes", align_bytes=64)
         floor = keep.tile([P, 1], F32, name="floor")
 
         def load_words(a, lo, hi):
@@ -75,17 +75,13 @@ def tile_list_kmer_locus_coverage_kernel(
         nc.scalar.activation(floor[:], one[:], ACT.Sqrt, scale=2.0**-116)
         nc.gpsimd.memset(scale_rows[0:48, :], 0)
         nc.gpsimd.memset(scale_rows[96:128, :], 0)
-        nc.gpsimd.memset(tab_planes[0][:], 0)
+        nc.gpsimd.memset(tab_planes[:], 0)
 
         picked_rows = keep.tile([P, S], U8, name="picked_rows", align_bytes=64)
         nc.vector.tensor_copy(picked_rows[:], scale_rows[:].bitcast(U8).indirect(idx[:]))
 
-        def move_scales(hf, queue):
-            picked = picked_rows[:, hf * HALF : (hf + 1) * HALF].bitcast(I32)
-            for q in QUADRANTS:
-                queue.dma_start(tab_planes[hf][32 * q : 32 * q + 4], picked[48 + 12 * q : 60 + 12 * q, :])
-
-        move_scales(0, nc.sync)
+        for q in QUADRANTS:
+            nc.sync.dma_start(tab_planes[32 * q : 32 * q + 4], picked_rows[48 + 12 * q : 60 + 12 * q, :].bitcast(I32))
         pages = [placed([P, T2], F32, "page%d" % t, 92 + 8 * t) for t in range(PACK)]
         for t in range(PACK):
             nc.gpsimd.memset(pages[t][:], 0.0)
@@ -103,8 +99,6 @@ def tile_list_kmer_locus_coverage_kernel(
         wks = placed([P, PACK, PASSES * P], U8, "wks", 79)
         nc.vector.tensor_copy(wks[:], wks_raw[:].bitcast(U8).rearrange("p (m t) -> p t m", t=PACK))
         gather_words(1, 0, S)
-        tab_planes.append(placed([P, PASSES, HALF // 4], I32, "tab_planes1", 27.5))
-        nc.gpsimd.memset(tab_planes[1][:], 0)
         gather_words(2, 0, HALF)
         gather_words(2, HALF, S)
 
@@ -120,16 +114,14 @@ def tile_list_kmer_locus_coverage_kernel(
 
         load_wgs(0, 2, 0, FIRST, 16)
         load_wgs(0, 2, FIRST, HALF, 14)
-        load_wgs(2, 1, 0, HALF, 12)
-        move_scales(1, nc.sync)
-        load_wgs(0, 2, HALF, S, 45)
-        load_wgs(2, 1, HALF, S, 49)
-        load_wgs(3, 1, 0, S, 51)
-        wo_raw = placed([P, PACK, N], F32, "wo_raw", 59)
-        nc.sync.dma_start(wo_raw[:], wo.rearrange("(p t) n -> p t n", t=PACK))
+        load_wgs(0, 2, HALF, S, 18)
+        load_wgs(2, 1, 0, S, 45)
+        load_wgs(3, 1, 0, S, 49)
         base_by_plane = base.rearrange("(p t) j -> p t j", t=PACK)
         base_sb = [placed([P, PACK, T2 // 2], F32, "base0", 29)]
         nc.sync.dma_start(base_sb[0][:], base_by_plane[:, :, 0 : T2 // 2])
+        wo_raw = placed([P, PACK, N], F32, "wo_raw", 59)
+        nc.sync.dma_start(wo_raw[:], wo.rearrange("(p t) n -> p t n", t=PACK))
 
         sums = {}
 
@@ -138,7 +130,6 @@ def tile_list_kmer_locus_coverage_kernel(
                 sums[t, lo] = psum.tile([P, hi - lo], F32, name="acc%d_%d" % (t, lo), tag="bank%d" % bank)
             for t, lo, hi, bank in pieces:
                 for a in range(PASSES):
-                    hf = lo // HALF
                     n = HALF if hi - lo == HALF else P
                     for c in range(lo, hi, n):
                         nc.tensor.matmul_mx(
@@ -146,7 +137,7 @@ def tile_list_kmer_locus_coverage_kernel(
                             lhsT=wkw[:, t, a * P : (a + 1) * P].bitcast(U8).bitcast(FP4X4),
                             lhsT_scale=wks[:, t, a * P : (a + 1) * P],
                             rhs=gathered[a][:, c : c + n].bitcast(FP8X4),
-                            rhs_scale=tab_planes[hf][:, a, :].bitcast(U8)[:, c - hf * HALF : c - hf * HALF + n],
+                            rhs_scale=tab_planes[:, a, :].bitcast(U8)[:, c : c + n],
                             start=(a == 0 and c == lo),
                             stop=(a == PASSES - 1 and c + n == hi),
                         )
@@ -174,29 +165,24 @@ def tile_list_kmer_locus_coverage_kernel(
         root(0, P, FIRST, keep, "mag2")
         scatter_fused(0, 0, FIRST)
         root(1, 0, FIRST, keep)
-        first_products(((0, FIRST, HALF, 3), (1, FIRST, HALF, 4), (2, 0, HALF, 5)))
+        first_products(((0, FIRST, HALF, 3), (1, FIRST, HALF, 4)))
         root(0, FIRST, HALF, keep, "mag2")
         weigh(nc.vector, 0, FIRST, HALF, wg[0, FIRST])
         scatter_fused(1, 0, FIRST)
         scatter(0, FIRST, HALF)
-        for t, lo, hi in ((1, FIRST, HALF), (2, 0, HALF)):
-            root(t, lo, hi, keep)
-            weigh(nc.gpsimd, t, lo, hi, wg[t, lo])
-            scatter(t, lo, hi)
+        root(1, FIRST, HALF, keep)
+        weigh(nc.gpsimd, 1, FIRST, HALF, wg[1, FIRST])
+        scatter(1, FIRST, HALF)
         base_sb.append(placed([P, PACK, T2 // 2], F32, "base1", 0))
         nc.sync.dma_start(base_sb[1][:], base_by_plane[:, :, T2 // 2 : T2])
-        for t, lo, bank in ((0, HALF, 6), (1, HALF, 7), (2, HALF, 0), (3, 0, 7), (3, HALF, 0)):
+        for t, lo, bank in ((0, HALF, 2), (1, HALF, 3), (2, 0, 4), (2, HALF, 2), (3, 0, 3), (3, HALF, 4)):
             first_products(((t, lo, lo + HALF, bank),))
-            root(t, lo, lo + HALF, ring)
-            weigh(nc.gpsimd, t, lo, lo + HALF, wg[3, 0][:, lo : lo + HALF] if t == 3 else wg[t, lo])
-        wo_bf = placed([P, N, PACK], BF16, "wo_bf", 140)
-        wo_scales = keep.tile([P, N], U8, name="wo_scales", align_bytes=64)
-        nc.scalar.copy(wo_bf[:], wo_raw[:].rearrange("p t n -> p n t"))
+            root(t, lo, lo + HALF, keep)
+            weigh(nc.gpsimd, t, lo, lo + HALF, wg[t, 0][:, lo : lo + HALF] if t >= 2 else wg[t, lo])
 
         base_of = lambda lo: base_sb[lo // (T2 // 2)]
         GROUP = SHARED // 2 * CHUNK
-        low = [placed([P, 2, GROUP], F32, "low%d" % u, 53.5 + 6 * u) for u in range(2)]
-        high = placed([P, 2, SHARED * CHUNK], F32, "high", 65.5)
+        low = [placed([P, 2, GROUP], F32, "low%d" % u, 80 + 6 * u) for u in range(2)]
         zs = {}
         ones = []
         scatter(0, HALF, S)
@@ -217,11 +203,15 @@ def tile_list_kmer_locus_coverage_kernel(
                 MULT,
             )
             if lo + CHUNK == GROUP:
-                ones.append(placed([P, 1], F32, "ones%d" % u, 56 + 5 * u))
+                ones.append(placed([P, 1], F32, "ones%d" % u, 80 + 6 * u))
                 nc.gpsimd.memset(ones[u][:], 1.0)
-        scatter(2, HALF, S)
+        wo_bf = placed([P, N, PACK], BF16, "wo_bf", 140)
+        wo_scales = keep.tile([P, N], U8, name="wo_scales", align_bytes=64)
+        nc.scalar.copy(wo_bf[:], wo_raw[:].rearrange("p t n -> p n t"))
+        scatter(2, 0, S)
+        high = placed([P, 2, SHARED * CHUNK], F32, "high", 65.5)
         nc.scalar.copy(high[:, 0, :], pages[2][:, 0 : SHARED * CHUNK])
-        rest = placed([P, PACK, T2 - SHARED * CHUNK], F32, "rest", 46)
+        rest = placed([P, PACK, T2 - SHARED * CHUNK], F32, "rest", 53)
         for t in range(PACK - 1):
             nc.scalar.activation(rest[:, t, :], pages[t][:, SHARED * CHUNK : T2], ACT.Copy, bias=1.0)
         scatter(3, 0, S)

@@ -15,7 +15,6 @@ FP8X4 = mybir.dt.float8_e4m3fn_x4
 FP4X4 = mybir.dt.float4_e2m1fn_x4
 ACT = mybir.ActivationFunctionType
 MULT = mybir.AluOpType.mult
-ADD = mybir.AluOpType.add
 
 P = 128
 PACK = 4
@@ -197,9 +196,9 @@ def tile_list_kmer_locus_coverage_kernel(
             zs[c] = placed([P, CHUNK, PACK], BF16, "z%d" % c, 144 + 2 * c)
             blo = c * CHUNK % (T2 // 2)
             nc.gpsimd.tensor_tensor(
-                zs[c][:, :, 0:2],
-                low[u][:, :, lo : lo + CHUNK].rearrange("p t j -> p j t"),
-                base_of(c * CHUNK)[:, 0:2, blo : blo + CHUNK].rearrange("p t j -> p j t"),
+                zs[c][:, :, 0:2].rearrange("p (c i) t -> p c t i", i=2),
+                low[u][:, :, lo : lo + CHUNK].rearrange("p t (c i) -> p c t i", i=2),
+                base_of(c * CHUNK)[:, 0:2, blo : blo + CHUNK].rearrange("p t (c i) -> p c t i", i=2),
                 MULT,
             )
             if lo + CHUNK == GROUP:
@@ -210,7 +209,7 @@ def tile_list_kmer_locus_coverage_kernel(
         nc.scalar.copy(wo_bf[:], wo_raw[:].rearrange("p t n -> p n t"))
         scatter(2, 0, S)
         high = placed([P, 2, SHARED * CHUNK], F32, "high", 65.5)
-        nc.scalar.copy(high[:, 0, :], pages[2][:, 0 : SHARED * CHUNK])
+        nc.scalar.activation(high[:, 0, :], pages[2][:, 0 : SHARED * CHUNK], ACT.Copy, bias=1.0)
         rest = placed([P, PACK, T2 - SHARED * CHUNK], F32, "rest", 53)
         for t in range(PACK - 1):
             nc.scalar.activation(rest[:, t, :], pages[t][:, SHARED * CHUNK : T2], ACT.Copy, bias=1.0)
@@ -228,12 +227,10 @@ def tile_list_kmer_locus_coverage_kernel(
             lo = c * CHUNK + part * P
             blo = lo % (T2 // 2)
             if c < SHARED:
-                nc.vector.scalar_tensor_tensor(
-                    zs[c][:, part * P : (part + 1) * P, 2:4],
-                    high[:, :, lo : lo + P].rearrange("p t j -> p j t"),
-                    ones[lo // GROUP][:],
-                    base_of(lo)[:, 2:4, blo : blo + P].rearrange("p t j -> p j t"),
-                    ADD,
+                nc.vector.tensor_tensor(
+                    zs[c][:, part * P : (part + 1) * P, 2:4].rearrange("p (c i) t -> p c t i", i=2),
+                    high[:, :, lo : lo + P].rearrange("p t (c i) -> p c t i", i=2),
+                    base_of(lo)[:, 2:4, blo : blo + P].rearrange("p t (c i) -> p c t i", i=2),
                     MULT,
                 )
                 return
@@ -286,8 +283,8 @@ def tile_list_kmer_locus_coverage_kernel(
                     nc.scalar.copy(staged[:, tiles, :], accs[b][:])
                 nc.sync.dma_start(out_view[:, tiles, lo : lo + CHUNK], staged[:, tiles, :])
 
-        for lo, hi in ((0, P), (P, CHUNK), (CHUNK, 2 * CHUNK), (2 * CHUNK, 4 * CHUNK), (4 * CHUNK, SHARED * CHUNK)):
-            nc.scalar.copy(high[:, 1, lo:hi], pages[3][:, lo:hi])
+        for lo, hi in ((0, P), (P, CHUNK), (CHUNK, GROUP), (GROUP, SHARED * CHUNK)):
+            nc.scalar.activation(high[:, 1, lo:hi], pages[3][:, lo:hi], ACT.Identity, bias=ones[lo // GROUP][:])
         nc.scalar.activation(rest[:, 3, :], pages[3][:, SHARED * CHUNK : T2], ACT.Copy, bias=1.0)
         make_z(0, 0)
         make_z(0, 1)

@@ -22,7 +22,7 @@ PASSES = K // (P * PACK)
 HALF = 512
 FIRST = 256
 CHUNK = 256
-SHARED = 6
+SHARED = 5
 BANKS = 8
 KIB = 1024
 QUADRANTS = (0, 2, 1, 3)
@@ -49,7 +49,7 @@ def tile_list_kmer_locus_coverage_kernel(
         one = keep.tile([P, 1], F32, name="one")
         wkw_raw = keep.tile([P, PASSES * (H // 2)], I32, name="wkw_raw", align_bytes=64)
         wks_raw = placed([P, PASSES * (H // 4)], I32, "wks_raw", 71)
-        tab_planes = keep.tile([P, PASSES, S // 4], I32, name="tab_planes", align_bytes=64)
+        tab_planes = [keep.tile([P, PASSES, HALF // 4], I32, name="tab_planes0", align_bytes=64)]
         floor = keep.tile([P, 1], F32, name="floor")
 
         def load_words(a, lo, hi):
@@ -74,13 +74,17 @@ def tile_list_kmer_locus_coverage_kernel(
         nc.scalar.activation(floor[:], one[:], ACT.Sqrt, scale=2.0**-116)
         nc.gpsimd.memset(scale_rows[0:48, :], 0)
         nc.gpsimd.memset(scale_rows[96:128, :], 0)
-        nc.gpsimd.memset(tab_planes[:], 0)
+        nc.gpsimd.memset(tab_planes[0][:], 0)
 
         picked_rows = keep.tile([P, S], U8, name="picked_rows", align_bytes=64)
         nc.vector.tensor_copy(picked_rows[:], scale_rows[:].bitcast(U8).indirect(idx[:]))
 
-        for q in QUADRANTS:
-            nc.sync.dma_start(tab_planes[32 * q : 32 * q + 4], picked_rows[48 + 12 * q : 60 + 12 * q, :].bitcast(I32))
+        def move_scales(hf):
+            picked = picked_rows[:, hf * HALF : (hf + 1) * HALF].bitcast(I32)
+            for q in QUADRANTS:
+                nc.sync.dma_start(tab_planes[hf][32 * q : 32 * q + 4], picked[48 + 12 * q : 60 + 12 * q, :])
+
+        move_scales(0)
         pages = [placed([P, T2], F32, "page%d" % t, 92 + 8 * t) for t in range(PACK)]
         for t in range(PACK):
             nc.gpsimd.memset(pages[t][:], 0.0)
@@ -97,6 +101,8 @@ def tile_list_kmer_locus_coverage_kernel(
         nc.vector.tensor_copy(wkw[:], wkw_raw[:].bitcast(U16).rearrange("p (m t) -> p t m", t=PACK))
         wks = placed([P, PACK, PASSES * P], U8, "wks", 79)
         nc.vector.tensor_copy(wks[:], wks_raw[:].bitcast(U8).rearrange("p (m t) -> p t m", t=PACK))
+        tab_planes.append(placed([P, PASSES, HALF // 4], I32, "tab_planes1", 22))
+        nc.gpsimd.memset(tab_planes[1][:], 0)
         gather_words(1, 0, S)
         gather_words(2, 0, HALF)
         gather_words(2, HALF, S)
@@ -113,11 +119,13 @@ def tile_list_kmer_locus_coverage_kernel(
 
         load_wgs(0, 2, 0, FIRST, 16)
         load_wgs(0, 2, FIRST, HALF, 14)
-        load_wgs(0, 2, HALF, S, 18)
-        load_wgs(2, 1, 0, S, 45)
-        load_wgs(3, 1, 0, S, 49)
+        move_scales(1)
+        load_wgs(2, 1, 0, FIRST, 28)
+        load_wgs(0, 2, HALF, S, 29)
+        load_wgs(2, 1, FIRST, S, 50)
+        load_wgs(3, 1, 0, S, 53)
         base_by_plane = base.rearrange("(p t) j -> p t j", t=PACK)
-        base_sb = [placed([P, PACK, T2 // 2], F32, "base0", 29)]
+        base_sb = [placed([P, PACK, T2 // 2], F32, "base0", 34)]
         nc.sync.dma_start(base_sb[0][:], base_by_plane[:, :, 0 : T2 // 2])
         wo_raw = placed([P, PACK, N], F32, "wo_raw", 59)
         nc.sync.dma_start(wo_raw[:], wo.rearrange("(p t) n -> p t n", t=PACK))
@@ -136,7 +144,7 @@ def tile_list_kmer_locus_coverage_kernel(
                             lhsT=wkw[:, t, a * P : (a + 1) * P].bitcast(U8).bitcast(FP4X4),
                             lhsT_scale=wks[:, t, a * P : (a + 1) * P],
                             rhs=gathered[a][:, c : c + n].bitcast(FP8X4),
-                            rhs_scale=tab_planes[:, a, :].bitcast(U8)[:, c : c + n],
+                            rhs_scale=tab_planes[c // HALF][:, a, :].bitcast(U8)[:, c % HALF : c % HALF + n],
                             start=(a == 0 and c == lo),
                             stop=(a == PASSES - 1 and c + n == hi),
                         )
@@ -150,7 +158,7 @@ def tile_list_kmer_locus_coverage_kernel(
 
         def scatter_fused(t, lo, hi):
             nc.vector.tensor_tensor(
-                pages[t][:].indirect(idx2[:, lo // 16 : hi // 16]), hs[:, t, lo:hi], wg[t, lo], MULT
+                pages[t][:].indirect(idx2[:, lo // 16 : hi // 16]), hs[:, t, lo:hi], wg[t, 0][:, lo:hi], MULT
             )
 
         def weigh(engine, t, lo, hi, weights):
@@ -164,7 +172,7 @@ def tile_list_kmer_locus_coverage_kernel(
         root(0, P, FIRST, keep, "mag2")
         scatter_fused(0, 0, FIRST)
         root(1, 0, FIRST, keep)
-        first_products(((0, FIRST, HALF, 3), (1, FIRST, HALF, 4)))
+        first_products(((0, FIRST, HALF, 3), (1, FIRST, HALF, 4), (2, 0, FIRST, 5)))
         root(0, FIRST, HALF, keep, "mag2")
         weigh(nc.vector, 0, FIRST, HALF, wg[0, FIRST])
         scatter_fused(1, 0, FIRST)
@@ -172,24 +180,31 @@ def tile_list_kmer_locus_coverage_kernel(
         root(1, FIRST, HALF, keep)
         weigh(nc.gpsimd, 1, FIRST, HALF, wg[1, FIRST])
         scatter(1, FIRST, HALF)
+        root(2, 0, FIRST, keep)
+        weigh(nc.gpsimd, 2, 0, FIRST, wg[2, 0])
+        scatter(2, 0, FIRST)
         base_sb.append(placed([P, PACK, T2 // 2], F32, "base1", 0))
         nc.sync.dma_start(base_sb[1][:], base_by_plane[:, :, T2 // 2 : T2])
-        for t, lo, bank in ((0, HALF, 2), (1, HALF, 3), (2, 0, 4), (2, HALF, 2), (3, 0, 3), (3, HALF, 4)):
-            first_products(((t, lo, lo + HALF, bank),))
-            root(t, lo, lo + HALF, keep)
-            weigh(nc.gpsimd, t, lo, lo + HALF, wg[t, 0][:, lo : lo + HALF] if t >= 2 else wg[t, lo])
+        later = ((0, HALF, S, 2), (1, HALF, S, 3), (2, FIRST, HALF, 2), (2, HALF, S, 3), (3, 0, HALF, 2), (3, HALF, S, 3))
+        for t, lo, hi, bank in later:
+            first = (HALF, HALF, FIRST, 0)[t]
+            first_products(((t, lo, hi, bank),))
+            root(t, lo, hi, keep if t < 2 else ring)
+            weigh(nc.gpsimd, t, lo, hi, wg[t, first][:, lo - first : hi - first])
 
         base_of = lambda lo: base_sb[lo // (T2 // 2)]
-        GROUP = SHARED // 2 * CHUNK
-        low = [placed([P, 2, GROUP], F32, "low%d" % u, 80 + 6 * u) for u in range(2)]
+        GROUP = CHUNK
+        ends = (0, GROUP, SHARED * CHUNK)
+        low = [placed([P, 2, ends[u + 1] - ends[u]], F32, "low%d" % u, 80 + 2 * u) for u in range(2)]
         zs = {}
         ones = []
         scatter(0, HALF, S)
         for u in range(2):
-            nc.scalar.activation(low[u][:, 0, :], pages[0][:, u * GROUP : (u + 1) * GROUP], ACT.Copy, bias=1.0)
+            nc.scalar.activation(low[u][:, 0, :], pages[0][:, ends[u] : ends[u + 1]], ACT.Copy, bias=1.0)
         scatter(1, HALF, S)
         for c in range(SHARED):
-            u, lo = divmod(c * CHUNK, GROUP)
+            u = min(c * CHUNK // GROUP, 1)
+            lo = c * CHUNK - ends[u]
             nc.scalar.activation(
                 low[u][:, 1, lo : lo + CHUNK], pages[1][:, c * CHUNK : (c + 1) * CHUNK], ACT.Copy, bias=1.0
             )
@@ -201,13 +216,13 @@ def tile_list_kmer_locus_coverage_kernel(
                 base_of(c * CHUNK)[:, 0:2, blo : blo + CHUNK].rearrange("p t (c i) -> p c t i", i=2),
                 MULT,
             )
-            if lo + CHUNK == GROUP:
-                ones.append(placed([P, 1], F32, "ones%d" % u, 80 + 6 * u))
+            if (c + 1) * CHUNK in ends:
+                ones.append(placed([P, 1], F32, "ones%d" % u, 81.5 + 2 * u))
                 nc.gpsimd.memset(ones[u][:], 1.0)
-        wo_bf = placed([P, N, PACK], BF16, "wo_bf", 140)
+        wo_bf = placed([P, N, PACK], BF16, "wo_bf", 77)
         wo_scales = keep.tile([P, N], U8, name="wo_scales", align_bytes=64)
         nc.scalar.copy(wo_bf[:], wo_raw[:].rearrange("p t n -> p n t"))
-        scatter(2, 0, S)
+        scatter(2, FIRST, S)
         high = placed([P, 2, SHARED * CHUNK], F32, "high", 65.5)
         nc.scalar.activation(high[:, 0, :], pages[2][:, 0 : SHARED * CHUNK], ACT.Copy, bias=1.0)
         rest = placed([P, PACK, T2 - SHARED * CHUNK], F32, "rest", 53)
@@ -283,8 +298,8 @@ def tile_list_kmer_locus_coverage_kernel(
                     nc.scalar.copy(staged[:, tiles, :], accs[b][:])
                 nc.sync.dma_start(out_view[:, tiles, lo : lo + CHUNK], staged[:, tiles, :])
 
-        for lo, hi in ((0, P), (P, CHUNK), (CHUNK, GROUP), (GROUP, SHARED * CHUNK)):
-            nc.scalar.activation(high[:, 1, lo:hi], pages[3][:, lo:hi], ACT.Identity, bias=ones[lo // GROUP][:])
+        for lo, hi in ((0, P), (P, CHUNK), (CHUNK, 3 * CHUNK), (3 * CHUNK, SHARED * CHUNK)):
+            nc.scalar.activation(high[:, 1, lo:hi], pages[3][:, lo:hi], ACT.Identity, bias=ones[min(lo // GROUP, 1)][:])
         nc.scalar.activation(rest[:, 3, :], pages[3][:, SHARED * CHUNK : T2], ACT.Copy, bias=1.0)
         make_z(0, 0)
         make_z(0, 1)

@@ -21,11 +21,10 @@ PACK = 4
 PASSES = K // (P * PACK)
 HALF = 512
 FIRST = 256
-CHUNK = 256
-SHARED = 5
 BANKS = 8
 KIB = 1024
 QUADRANTS = (0, 2, 1, 3)
+EDGES = (0, 128, 384, 640, 896, 1152, 1408, 1664, 1920, 2048)
 
 
 def tile_list_kmer_locus_coverage_kernel(
@@ -44,16 +43,16 @@ def tile_list_kmer_locus_coverage_kernel(
 
         idx = keep.tile([P, S // 16], U16, name="idx")
         idx2 = keep.tile([P, S // 16], U16, name="idx2")
-        words = [placed([P, T], I32, "words%d" % a, 12 + 16 * a) for a in range(PASSES)]
-        scale_rows = placed([P, T // 4], I32, "scale_rows", 64)
+        words = [placed([P, T], I32, "words%d" % a, 16 * a) for a in range(PASSES)]
+        scale_rows = placed([P, T // 4], I32, "scale_rows", 52)
         one = keep.tile([P, 1], F32, name="one")
-        wkw_raw = keep.tile([P, PASSES * (H // 2)], I32, name="wkw_raw", align_bytes=64)
-        wks_raw = placed([P, PASSES * (H // 4)], I32, "wks_raw", 71)
-        tab_planes = [keep.tile([P, PASSES, HALF // 4], I32, name="tab_planes0", align_bytes=64)]
         floor = keep.tile([P, 1], F32, name="floor")
+        wkw_raw = keep.tile([P, PASSES * (H // 2)], I32, name="wkw_raw", align_bytes=64)
+        wks_raw = placed([P, PASSES * (H // 4)], I32, "wks_raw", 60)
+        tab_planes = [keep.tile([P, PASSES, HALF // 4], I32, name="tab_planes0", align_bytes=64)]
 
-        def load_words(a, lo, hi):
-            nc.sync.dma_start(words[a][:, lo:hi], tab_words[a].rearrange("p t i -> p (t i)").bitcast(I32)[:, lo:hi])
+        def load_words(a):
+            nc.sync.dma_start(words[a][:], tab_words[a].rearrange("p t i -> p (t i)").bitcast(I32))
 
         nc.gpsimd.memset(wks_raw[:], 0)
         nc.sync.dma_start(
@@ -66,10 +65,10 @@ def tile_list_kmer_locus_coverage_kernel(
                 wks_raw[32 * q : 32 * q + 4, :].rearrange("p (a c) -> p a c", a=PASSES),
                 wk_scales[:, 4 * q : 4 * q + 4, :].bitcast(I32).rearrange("a r c -> r a c"),
             )
-        load_words(0, 0, T)
+        load_words(0)
         nc.sync.dma_start(scale_rows[48:96, :], tab_scales.bitcast(I32).rearrange("a q c -> q a c"))
-        load_words(1, 0, T)
-        load_words(2, 0, T)
+        load_words(1)
+        load_words(2)
         nc.vector.memset(one[:], 1.0)
         nc.scalar.activation(floor[:], one[:], ACT.Sqrt, scale=2.0**-116)
         nc.gpsimd.memset(scale_rows[0:48, :], 0)
@@ -85,11 +84,11 @@ def tile_list_kmer_locus_coverage_kernel(
                 nc.sync.dma_start(tab_planes[hf][32 * q : 32 * q + 4], picked[48 + 12 * q : 60 + 12 * q, :])
 
         move_scales(0)
-        pages = [placed([P, T2], F32, "page%d" % t, 92 + 8 * t) for t in range(PACK)]
+        pages = [placed([P, T2], F32, "page%d" % t, 68 + 8 * t) for t in range(PACK)]
         for t in range(PACK):
             nc.gpsimd.memset(pages[t][:], 0.0)
 
-        gathered = [placed([P, S], U32, "gathered%d" % a, 67 + 4 * a) for a in range(PASSES)]
+        gathered = [placed([P, S], U32, "gathered%d" % a, (55, 60, 64)[a]) for a in range(PASSES)]
 
         def gather_words(a, lo, hi):
             nc.vector.tensor_copy(
@@ -97,14 +96,15 @@ def tile_list_kmer_locus_coverage_kernel(
             )
 
         gather_words(0, 0, S)
-        wkw = placed([P, PACK, PASSES * P], U16, "wkw", 140)
+        wkw = placed([P, PACK, PASSES * P], U16, "wkw", 148)
         nc.vector.tensor_copy(wkw[:], wkw_raw[:].bitcast(U16).rearrange("p (m t) -> p t m", t=PACK))
-        wks = placed([P, PACK, PASSES * P], U8, "wks", 79)
+        wks = placed([P, PACK, PASSES * P], U8, "wks", 151)
         nc.vector.tensor_copy(wks[:], wks_raw[:].bitcast(U8).rearrange("p (m t) -> p t m", t=PACK))
-        tab_planes.append(placed([P, PASSES, HALF // 4], I32, "tab_planes1", 22))
+        tab_planes.append(placed([P, PASSES, HALF // 4], I32, "tab_planes1", 4))
         nc.gpsimd.memset(tab_planes[1][:], 0)
         gather_words(1, 0, S)
-        gather_words(2, 0, HALF)
+        gather_words(2, 0, FIRST)
+        gather_words(2, FIRST, HALF)
         gather_words(2, HALF, S)
 
         wgs_by_plane = wgs.rearrange("(g t) j -> g t j", t=PACK)
@@ -117,202 +117,152 @@ def tile_list_kmer_locus_coverage_kernel(
             for u in range(planes):
                 wg[t + u, lo] = piece[:, u, :]
 
-        load_wgs(0, 2, 0, FIRST, 16)
-        load_wgs(0, 2, FIRST, HALF, 14)
+        load_wgs(0, 2, 0, FIRST, 0)
+        load_wgs(0, 2, FIRST, HALF, 2)
         move_scales(1)
-        load_wgs(2, 1, 0, FIRST, 28)
-        load_wgs(0, 2, HALF, S, 29)
-        load_wgs(2, 1, FIRST, S, 50)
-        load_wgs(3, 1, 0, S, 53)
+        load_wgs(0, 2, HALF, S, 16)
+        load_wgs(2, 1, 0, S, 20)
+        load_wgs(3, 1, 0, S, 24)
         base_by_plane = base.rearrange("(p t) j -> p t j", t=PACK)
-        base_sb = [placed([P, PACK, T2 // 2], F32, "base0", 34)]
-        nc.sync.dma_start(base_sb[0][:], base_by_plane[:, :, 0 : T2 // 2])
-        wo_raw = placed([P, PACK, N], F32, "wo_raw", 59)
+        base_low = placed([P, 2, T2], F32, "base_low", 28)
+        nc.sync.dma_start(base_low[:], base_by_plane[:, 0:2, :])
+        wo_raw = placed([P, PACK, N], F32, "wo_raw", 44)
         nc.sync.dma_start(wo_raw[:], wo.rearrange("(p t) n -> p t n", t=PACK))
 
+        hs = [placed([P, S], F32, "h%d" % t, 100 + 4 * t) for t in range(PACK)]
         sums = {}
 
-        def first_products(pieces):
-            for t, lo, hi, bank in pieces:
+        def passes(t, lo, hi, bank, first, last):
+            if first == 0:
                 sums[t, lo] = psum.tile([P, hi - lo], F32, name="acc%d_%d" % (t, lo), tag="bank%d" % bank)
-            for t, lo, hi, bank in pieces:
-                for a in range(PASSES):
-                    n = HALF if hi - lo == HALF else P
-                    for c in range(lo, hi, n):
-                        nc.tensor.matmul_mx(
-                            out=sums[t, lo][:, c - lo : c - lo + n],
-                            lhsT=wkw[:, t, a * P : (a + 1) * P].bitcast(U8).bitcast(FP4X4),
-                            lhsT_scale=wks[:, t, a * P : (a + 1) * P],
-                            rhs=gathered[a][:, c : c + n].bitcast(FP8X4),
-                            rhs_scale=tab_planes[c // HALF][:, a, :].bitcast(U8)[:, c % HALF : c % HALF + n],
-                            start=(a == 0 and c == lo),
-                            stop=(a == PASSES - 1 and c + n == hi),
-                        )
+            acc = sums[t, lo]
+            for a in range(first, last):
+                nc.tensor.matmul_mx(
+                    out=acc[:],
+                    lhsT=wkw[:, t, a * P : (a + 1) * P].bitcast(U8).bitcast(FP4X4),
+                    lhsT_scale=wks[:, t, a * P : (a + 1) * P],
+                    rhs=gathered[a][:, lo:hi].bitcast(FP8X4),
+                    rhs_scale=tab_planes[lo // HALF][:, a, :].bitcast(U8)[:, lo % HALF : lo % HALF + hi - lo],
+                    start=(a == 0),
+                    stop=(a == PASSES - 1),
+                )
 
-        hs = placed([P, PACK, S], F32, "hs", 124)
-
-        def root(t, lo, hi, pool, tag="mag"):
-            mag = pool.tile([P, hi - lo], F32, name=tag)
+        def root(t, lo, hi, slot):
+            mag = placed([P, hi - lo], F32, "mag%d_%d" % (t, lo), 116 + 2 * slot)
             nc.scalar.activation(mag[:], sums[t, lo][:], ACT.Abs)
-            nc.scalar.activation(hs[:, t, lo:hi], mag[:], ACT.Sqrt, bias=floor[:])
+            nc.scalar.activation(hs[t][:, lo:hi], mag[:], ACT.Sqrt, bias=floor[:])
 
-        def scatter_fused(t, lo, hi):
-            nc.vector.tensor_tensor(
-                pages[t][:].indirect(idx2[:, lo // 16 : hi // 16]), hs[:, t, lo:hi], wg[t, 0][:, lo:hi], MULT
-            )
-
-        def weigh(engine, t, lo, hi, weights):
-            engine.tensor_tensor(hs[:, t, lo:hi], hs[:, t, lo:hi], weights, MULT)
+        def weigh(engine, t, lo, hi, first):
+            engine.tensor_tensor(hs[t][:, lo:hi], hs[t][:, lo:hi], wg[t, first][:, lo - first : hi - first], MULT)
 
         def scatter(t, lo, hi):
-            nc.vector.tensor_copy(pages[t][:].indirect(idx2[:, lo // 16 : hi // 16]), hs[:, t, lo:hi])
+            nc.vector.tensor_copy(pages[t][:].indirect(idx2[:, lo // 16 : hi // 16]), hs[t][:, lo:hi])
 
-        first_products(((0, 0, P, 0), (0, P, FIRST, 1), (1, 0, FIRST, 2)))
-        root(0, 0, P, keep)
-        root(0, P, FIRST, keep, "mag2")
-        scatter_fused(0, 0, FIRST)
-        root(1, 0, FIRST, keep)
-        first_products(((0, FIRST, HALF, 3), (1, FIRST, HALF, 4), (2, 0, FIRST, 5)))
-        root(0, FIRST, HALF, keep, "mag2")
-        weigh(nc.vector, 0, FIRST, HALF, wg[0, FIRST])
-        scatter_fused(1, 0, FIRST)
-        scatter(0, FIRST, HALF)
-        root(1, FIRST, HALF, keep)
-        weigh(nc.gpsimd, 1, FIRST, HALF, wg[1, FIRST])
-        scatter(1, FIRST, HALF)
-        root(2, 0, FIRST, keep)
-        weigh(nc.gpsimd, 2, 0, FIRST, wg[2, 0])
-        scatter(2, 0, FIRST)
-        base_sb.append(placed([P, PACK, T2 // 2], F32, "base1", 0))
-        nc.sync.dma_start(base_sb[1][:], base_by_plane[:, :, T2 // 2 : T2])
-        later = ((0, HALF, S, 2), (1, HALF, S, 3), (2, FIRST, HALF, 2), (2, HALF, S, 3), (3, 0, HALF, 2), (3, HALF, S, 3))
-        for t, lo, hi, bank in later:
-            first = (HALF, HALF, FIRST, 0)[t]
-            first_products(((t, lo, hi, bank),))
-            root(t, lo, hi, keep if t < 2 else ring)
-            weigh(nc.gpsimd, t, lo, hi, wg[t, first][:, lo - first : hi - first])
-
-        base_of = lambda lo: base_sb[lo // (T2 // 2)]
-        GROUP = CHUNK
-        ends = (0, GROUP, SHARED * CHUNK)
-        low = [placed([P, 2, ends[u + 1] - ends[u]], F32, "low%d" % u, 80 + 2 * u) for u in range(2)]
-        zs = {}
-        ones = []
-        scatter(0, HALF, S)
         for u in range(2):
-            nc.scalar.activation(low[u][:, 0, :], pages[0][:, ends[u] : ends[u + 1]], ACT.Copy, bias=1.0)
-        scatter(1, HALF, S)
-        for c in range(SHARED):
-            u = min(c * CHUNK // GROUP, 1)
-            lo = c * CHUNK - ends[u]
-            nc.scalar.activation(
-                low[u][:, 1, lo : lo + CHUNK], pages[1][:, c * CHUNK : (c + 1) * CHUNK], ACT.Copy, bias=1.0
-            )
-            zs[c] = placed([P, CHUNK, PACK], BF16, "z%d" % c, 144 + 2 * c)
-            blo = c * CHUNK % (T2 // 2)
-            nc.gpsimd.tensor_tensor(
-                zs[c][:, :, 0:2].rearrange("p (c i) t -> p c t i", i=2),
-                low[u][:, :, lo : lo + CHUNK].rearrange("p t (c i) -> p c t i", i=2),
-                base_of(c * CHUNK)[:, 0:2, blo : blo + CHUNK].rearrange("p t (c i) -> p c t i", i=2),
+            passes(0, u * P, (u + 1) * P, u, 0, PASSES - 1)
+        for u in range(2):
+            passes(0, u * P, (u + 1) * P, u, PASSES - 1, PASSES)
+            root(0, u * P, (u + 1) * P, u)
+            weigh(nc.gpsimd, 0, u * P, (u + 1) * P, 0)
+        scatter(0, 0, FIRST)
+        pieces = ((1, 0, FIRST), (0, FIRST, HALF), (1, FIRST, HALF), (0, HALF, S), (1, HALF, S))
+        for u, (t, lo, hi) in enumerate(pieces):
+            passes(t, lo, hi, 2 + u, 0, PASSES)
+            root(t, lo, hi, max(u - 1, 0) % 2)
+            weigh(nc.gpsimd, t, lo, hi, lo)
+            scatter(t, lo, hi)
+        for t in (2, 3):
+            for hf in range(2):
+                passes(t, hf * HALF, (hf + 1) * HALF, (2 * t + hf + 3) % BANKS, 0, PASSES)
+                root(t, hf * HALF, (hf + 1) * HALF, hf)
+                weigh(nc.gpsimd, t, hf * HALF, (hf + 1) * HALF, 0)
+
+        chunks = len(EDGES) - 1
+        pairs = [placed([P, 2, EDGES[c + 1] - EDGES[c]], I32, "pairs%d" % c, 132 + EDGES[c] // P) for c in range(chunks)]
+
+        def lift(dst, t, lo, hi):
+            nc.scalar.activation(dst[:, t % 2, lo:hi], pages[t][:, lo:hi], ACT.Copy, bias=1.0)
+
+        def make_pairs(engine, c, u, lifted, rows, part=None):
+            lo, hi = EDGES[c], EDGES[c + 1]
+            if part is not None:
+                lo, hi = lo + part * P, lo + (part + 1) * P
+            engine.tensor_tensor(
+                pairs[c][:, u, lo - EDGES[c] : hi - EDGES[c]].bitcast(BF16).rearrange("p (c i t) -> p c t i", i=PACK, t=2),
+                lifted[:, :, lo:hi].rearrange("p t (c i) -> p c t i", i=PACK),
+                rows[:, :, lo:hi].rearrange("p t (c i) -> p c t i", i=PACK),
                 MULT,
             )
-            if (c + 1) * CHUNK in ends:
-                ones.append(placed([P, 1], F32, "ones%d" % u, 81.5 + 2 * u))
-                nc.gpsimd.memset(ones[u][:], 1.0)
-        wo_bf = placed([P, N, PACK], BF16, "wo_bf", 77)
+
+        low = placed([P, 2, T2], F32, "low", 116)
+        lift(low, 0, 0, T2)
+        base_high = placed([P, 2, T2], F32, "base_high", 60)
+        nc.sync.dma_start(base_high[:], base_by_plane[:, 2:4, :])
+        for lo, hi in ((0, EDGES[1]), (EDGES[1], EDGES[3]), (EDGES[3], T2)):
+            lift(low, 1, lo, hi)
+        for c in range(chunks):
+            make_pairs(nc.gpsimd, c, 0, low, base_low)
+        wo_bf = placed([P, N, PACK], BF16, "wo_bf", 76)
         wo_scales = keep.tile([P, N], U8, name="wo_scales", align_bytes=64)
         nc.scalar.copy(wo_bf[:], wo_raw[:].rearrange("p t n -> p n t"))
-        scatter(2, FIRST, S)
-        high = placed([P, 2, SHARED * CHUNK], F32, "high", 65.5)
-        nc.scalar.activation(high[:, 0, :], pages[2][:, 0 : SHARED * CHUNK], ACT.Copy, bias=1.0)
-        rest = placed([P, PACK, T2 - SHARED * CHUNK], F32, "rest", 53)
-        for t in range(PACK - 1):
-            nc.scalar.activation(rest[:, t, :], pages[t][:, SHARED * CHUNK : T2], ACT.Copy, bias=1.0)
+        scatter(2, 0, S)
+        high = placed([P, 2, T2], F32, "high", 44)
+        lift(high, 2, 0, T2)
         scatter(3, 0, S)
-        wo_codes = placed([P, N], U32, "wo_codes", 124)
+        wo_codes = placed([P, N], U32, "wo_codes", 112)
         nc.vector.quantize_mx(
             out=wo_codes[:].bitcast(FP8X4), scales=wo_scales[:], in_=wo_bf[:].rearrange("p n t -> p (n t)")
         )
+        for lo, hi in ((0, EDGES[1]), (EDGES[1], EDGES[2]), (EDGES[2], EDGES[4]), (EDGES[4], T2)):
+            lift(high, 3, lo, hi)
 
         out_view = out.rearrange("(m p) j -> p m j", p=P)
-        chunks = T2 // CHUNK
-        zq = {}
+        zs = {}
+        banks_used = [0]
 
-        def make_z(c, part):
-            lo = c * CHUNK + part * P
-            blo = lo % (T2 // 2)
-            if c < SHARED:
-                nc.vector.tensor_tensor(
-                    zs[c][:, part * P : (part + 1) * P, 2:4].rearrange("p (c i) t -> p c t i", i=2),
-                    high[:, :, lo : lo + P].rearrange("p t (c i) -> p c t i", i=2),
-                    base_of(lo)[:, 2:4, blo : blo + P].rearrange("p t (c i) -> p c t i", i=2),
-                    MULT,
-                )
-                return
-            if part == 0:
-                zs[c] = ring.tile([P, CHUNK, PACK], BF16, name="z", align_bytes=64)
-            rlo = lo - SHARED * CHUNK
-            nc.vector.tensor_tensor(
-                zs[c][:, part * P : (part + 1) * P, :].rearrange("p (c i) t -> p c t i", i=2),
-                rest[:, :, rlo : rlo + P].rearrange("p t (c i) -> p c t i", i=2),
-                base_of(lo)[:, :, blo : blo + P].rearrange("p t (c i) -> p c t i", i=2),
-                MULT,
+        def weave(c):
+            width = EDGES[c + 1] - EDGES[c]
+            zs[c] = ring.tile([P, width, 2], I32, name="z", align_bytes=64)
+            nc.vector.tensor_copy(
+                zs[c][:].rearrange("p (c i) u -> p c u i", i=2), pairs[c][:].rearrange("p u (c i) -> p c u i", i=2)
             )
 
-        def quantise_z(c, lo, hi):
-            if lo == 0:
-                codes = ring.tile([P, CHUNK], U32, name="z_codes", align_bytes=64)
-                scales = ring.tile([P, CHUNK], U8, name="z_scales", align_bytes=64)
-                zq[c] = (codes, scales)
-            codes, scales = zq[c]
+        def tracks(c):
+            lo, width = EDGES[c], EDGES[c + 1] - EDGES[c]
+            codes = ring.tile([P, width], U32, name="z_codes", align_bytes=64)
+            scales = ring.tile([P, width], U8, name="z_scales", align_bytes=64)
             nc.vector.quantize_mx(
-                out=codes[:, lo:hi].bitcast(FP8X4),
-                scales=scales[:, lo:hi],
-                in_=zs[c][:, lo:hi, :].rearrange("p j t -> p (j t)"),
+                out=codes[:].bitcast(FP8X4), scales=scales[:], in_=zs[c][:].rearrange("p j u -> p (j u)").bitcast(BF16)
             )
-
-        def second_product(c, group, n):
-            codes, scales = zq[c]
-            lo = c * CHUNK
-            staged = stage.tile([P, PACK, CHUNK], F32, name="staged", align_bytes=64)
-            accs = [
-                psum.tile([P, group, CHUNK], F32, name="track", tag="bank%d" % ((2 * c + b) % BANKS))
-                for b in range(PACK // group)
-            ]
-            for col in range(0, CHUNK, n):
-                for m in range(PACK):
+            group = PACK if c == 0 else 2
+            staged = stage.tile([P, PACK, width], F32, name="staged", align_bytes=64)
+            for b in range(PACK // group):
+                acc = psum.tile([P, group, width], F32, name="track", tag="bank%d" % (banks_used[0] % BANKS))
+                banks_used[0] = banks_used[0] + 1
+                for m in range(b * group, (b + 1) * group):
                     nc.tensor.matmul_mx(
-                        out=accs[m // group][:, m % group, col : col + n],
+                        out=acc[:, m % group, :],
                         lhsT=wo_codes[:, P * m : P * (m + 1)].bitcast(FP8X4),
                         lhsT_scale=wo_scales[:, P * m : P * (m + 1)],
-                        rhs=codes[:, col : col + n].bitcast(FP8X4),
-                        rhs_scale=scales[:, col : col + n],
+                        rhs=codes[:].bitcast(FP8X4),
+                        rhs_scale=scales[:],
                         start=True,
                         stop=True,
                     )
-            for b in range(PACK // group):
                 tiles = slice(b * group, (b + 1) * group)
-                if (group == 1 and b % 2 == 1) or (c == chunks - 2 and b == 1):
-                    nc.vector.tensor_copy(staged[:, tiles, :], accs[b][:])
+                if c >= chunks - 2 and b == 1:
+                    nc.vector.tensor_copy(staged[:, tiles, :], acc[:])
                 else:
-                    nc.scalar.copy(staged[:, tiles, :], accs[b][:])
-                nc.sync.dma_start(out_view[:, tiles, lo : lo + CHUNK], staged[:, tiles, :])
+                    nc.scalar.copy(staged[:, tiles, :], acc[:])
+                nc.sync.dma_start(out_view[:, tiles, lo : lo + width], staged[:, tiles, :])
 
-        for lo, hi in ((0, P), (P, CHUNK), (CHUNK, 3 * CHUNK), (3 * CHUNK, SHARED * CHUNK)):
-            nc.scalar.activation(high[:, 1, lo:hi], pages[3][:, lo:hi], ACT.Identity, bias=ones[min(lo // GROUP, 1)][:])
-        nc.scalar.activation(rest[:, 3, :], pages[3][:, SHARED * CHUNK : T2], ACT.Copy, bias=1.0)
-        make_z(0, 0)
-        make_z(0, 1)
-        quantise_z(0, 0, P)
-        quantise_z(0, P, CHUNK)
-        second_product(0, 2, P)
-        make_z(1, 0)
-        make_z(1, 1)
-        for c in range(1, chunks - 1):
-            make_z(c + 1, 0)
-            quantise_z(c, 0, CHUNK)
-            second_product(c, 2, CHUNK)
-            make_z(c + 1, 1)
-        quantise_z(chunks - 1, 0, P)
-        quantise_z(chunks - 1, P, CHUNK)
-        second_product(chunks - 1, 1, P)
+        make_pairs(nc.vector, 0, 1, high, base_high)
+        make_pairs(nc.vector, 1, 1, high, base_high, 0)
+        weave(0)
+        make_pairs(nc.vector, 1, 1, high, base_high, 1)
+        tracks(0)
+        for c in range(1, chunks):
+            weave(c)
+            if c + 1 < chunks:
+                make_pairs(nc.vector, c + 1, 1, high, base_high)
+            tracks(c)

@@ -24,7 +24,8 @@ FIRST = 256
 BANKS = 8
 KIB = 1024
 QUADRANTS = (0, 2, 1, 3)
-EDGES = (0, 128, 384, 640, 896, 1152, 1408, 1664, 1920, 2048)
+CHUNK = 256
+EDGES = tuple(range(0, T2 + 1, CHUNK))
 
 
 def tile_list_kmer_locus_coverage_kernel(
@@ -34,7 +35,7 @@ def tile_list_kmer_locus_coverage_kernel(
     with ExitStack() as ctx:
         keep = ctx.enter_context(tc.tile_pool(name="keep", bufs=1))
         mem = ctx.enter_context(tc.tile_pool(name="mem", bufs=1))
-        stage = ctx.enter_context(tc.tile_pool(name="stage", bufs=8))
+        stage = ctx.enter_context(tc.tile_pool(name="stage", bufs=1))
         ring = ctx.enter_context(tc.tile_pool(name="ring", bufs=3))
         psum = ctx.enter_context(tc.psum_pool(name="psum", bufs=1))
 
@@ -219,42 +220,51 @@ def tile_list_kmer_locus_coverage_kernel(
         out_view = out.rearrange("(m p) j -> p m j", p=P)
         zs = {}
         banks_used = [0]
+        staged = {}
 
         def weave(c):
-            width = EDGES[c + 1] - EDGES[c]
-            zs[c] = ring.tile([P, width, 2], I32, name="z", align_bytes=64)
+            zs[c] = ring.tile([P, CHUNK, 2], I32, name="z", align_bytes=64)
             nc.vector.tensor_copy(
                 zs[c][:].rearrange("p (c i) u -> p c u i", i=2), pairs[c][:].rearrange("p u (c i) -> p c u i", i=2)
             )
 
+        def span(c, b):
+            first = 3 - b
+            if c < first:
+                return c, c + 1
+            lo = c - (c - first) % 2
+            return lo, min(lo + 2, chunks)
+
         def tracks(c):
-            lo, width = EDGES[c], EDGES[c + 1] - EDGES[c]
-            codes = ring.tile([P, width], U32, name="z_codes", align_bytes=64)
-            scales = ring.tile([P, width], U8, name="z_scales", align_bytes=64)
+            codes = ring.tile([P, CHUNK], U32, name="z_codes", align_bytes=64)
+            scales = ring.tile([P, CHUNK], U8, name="z_scales", align_bytes=64)
             nc.vector.quantize_mx(
                 out=codes[:].bitcast(FP8X4), scales=scales[:], in_=zs[c][:].rearrange("p j u -> p (j u)").bitcast(BF16)
             )
-            group = PACK if c == 0 else 2
-            staged = stage.tile([P, PACK, width], F32, name="staged", align_bytes=64)
-            for b in range(PACK // group):
-                acc = psum.tile([P, group, width], F32, name="track", tag="bank%d" % (banks_used[0] % BANKS))
-                banks_used[0] = banks_used[0] + 1
-                for m in range(b * group, (b + 1) * group):
-                    nc.tensor.matmul_mx(
-                        out=acc[:, m % group, :],
-                        lhsT=wo_codes[:, P * m : P * (m + 1)].bitcast(FP8X4),
-                        lhsT_scale=wo_scales[:, P * m : P * (m + 1)],
-                        rhs=codes[:].bitcast(FP8X4),
-                        rhs_scale=scales[:],
-                        start=True,
-                        stop=True,
-                    )
-                tiles = slice(b * group, (b + 1) * group)
-                if c >= chunks - 2 and b == 1:
-                    nc.vector.tensor_copy(staged[:, tiles, :], acc[:])
-                else:
-                    nc.scalar.copy(staged[:, tiles, :], acc[:])
-                nc.sync.dma_start(out_view[:, tiles, lo : lo + width], staged[:, tiles, :])
+            group = 1 if c == 0 else 2
+            for b in ((1, 0) if c >= 3 and c % 2 == 1 else (0, 1)):
+                lo, hi = span(c, b)
+                if c == lo:
+                    staged[b] = stage.tile([P, 2, (hi - lo) * CHUNK], F32, name="staged%d_%d" % (c, b), align_bytes=64)
+                for first in range(2 * b, 2 * b + 2, group):
+                    acc = psum.tile([P, group, CHUNK], F32, name="track", tag="bank%d" % (banks_used[0] % BANKS))
+                    banks_used[0] = banks_used[0] + 1
+                    for m in range(first, first + group):
+                        nc.tensor.matmul_mx(
+                            out=acc[:, m - first, :],
+                            lhsT=wo_codes[:, P * m : P * (m + 1)].bitcast(FP8X4),
+                            lhsT_scale=wo_scales[:, P * m : P * (m + 1)],
+                            rhs=codes[:].bitcast(FP8X4),
+                            rhs_scale=scales[:],
+                            start=True,
+                            stop=True,
+                        )
+                    rows = slice(first - 2 * b, first - 2 * b + group)
+                    nc.scalar.copy(staged[b][:, rows, (c - lo) * CHUNK : (c - lo + 1) * CHUNK], acc[:])
+                    if c + 1 == hi:
+                        nc.sync.dma_start(
+                            out_view[:, first : first + group, lo * CHUNK : hi * CHUNK], staged[b][:, rows, :]
+                        )
 
         make_pairs(nc.vector, 0, 1, high, base_high)
         make_pairs(nc.vector, 1, 1, high, base_high, 0)

@@ -176,20 +176,17 @@ def tile_list_kmer_locus_coverage_kernel(
             for hf in range(2):
                 passes(t, hf * HALF, (hf + 1) * HALF, (2 * t + hf + 3) % BANKS, 0, PASSES)
                 root(t, hf * HALF, (hf + 1) * HALF, hf)
-                weigh(nc.gpsimd, t, hf * HALF, (hf + 1) * HALF, 0)
+            weigh(nc.gpsimd, t, 0, S, 0)
 
         chunks = len(EDGES) - 1
-        pairs = [placed([P, 2, EDGES[c + 1] - EDGES[c]], I32, "pairs%d" % c, 132 + EDGES[c] // P) for c in range(chunks)]
+        pairs = placed([P, 2, T2, 2], BF16, "pairs", 132)
 
         def lift(dst, t, lo, hi):
             nc.scalar.activation(dst[:, t % 2, lo:hi], pages[t][:, lo:hi], ACT.Copy, bias=1.0)
 
-        def make_pairs(engine, c, u, lifted, rows, part=None):
-            lo, hi = EDGES[c], EDGES[c + 1]
-            if part is not None:
-                lo, hi = lo + part * P, lo + (part + 1) * P
+        def make_pairs(engine, u, lifted, rows, lo, hi):
             engine.tensor_tensor(
-                pairs[c][:, u, lo - EDGES[c] : hi - EDGES[c]].bitcast(BF16).rearrange("p (c i t) -> p c t i", i=PACK, t=2),
+                pairs[:, u, lo:hi, :].rearrange("p (c i) t -> p c t i", i=PACK),
                 lifted[:, :, lo:hi].rearrange("p t (c i) -> p c t i", i=PACK),
                 rows[:, :, lo:hi].rearrange("p t (c i) -> p c t i", i=PACK),
                 MULT,
@@ -201,8 +198,8 @@ def tile_list_kmer_locus_coverage_kernel(
         nc.sync.dma_start(base_high[:], base_by_plane[:, 2:4, :])
         for lo, hi in ((0, EDGES[1]), (EDGES[1], EDGES[3]), (EDGES[3], T2)):
             lift(low, 1, lo, hi)
-        for c in range(chunks):
-            make_pairs(nc.gpsimd, c, 0, low, base_low)
+        for lo, hi in ((0, EDGES[1]), (EDGES[1], EDGES[3]), (EDGES[3], T2)):
+            make_pairs(nc.gpsimd, 0, low, base_low, lo, hi)
         wo_bf = placed([P, N, PACK], BF16, "wo_bf", 76)
         wo_scales = keep.tile([P, N], U8, name="wo_scales", align_bytes=64)
         nc.scalar.copy(wo_bf[:], wo_raw[:].rearrange("p t n -> p n t"))
@@ -223,9 +220,10 @@ def tile_list_kmer_locus_coverage_kernel(
         staged = {}
 
         def weave(c):
-            zs[c] = ring.tile([P, CHUNK, 2], I32, name="z", align_bytes=64)
+            zs[c] = ring.tile([P, CHUNK, 2, 2], BF16, name="z", align_bytes=64)
             nc.vector.tensor_copy(
-                zs[c][:].rearrange("p (c i) u -> p c u i", i=2), pairs[c][:].rearrange("p u (c i) -> p c u i", i=2)
+                zs[c][:].rearrange("p (c i) u t -> p c u i t", i=2),
+                pairs[:, :, EDGES[c] : EDGES[c + 1], :].rearrange("p u (c i) t -> p c u i t", i=2),
             )
 
         def span(c, b):
@@ -239,7 +237,7 @@ def tile_list_kmer_locus_coverage_kernel(
             codes = ring.tile([P, CHUNK], U32, name="z_codes", align_bytes=64)
             scales = ring.tile([P, CHUNK], U8, name="z_scales", align_bytes=64)
             nc.vector.quantize_mx(
-                out=codes[:].bitcast(FP8X4), scales=scales[:], in_=zs[c][:].rearrange("p j u -> p (j u)").bitcast(BF16)
+                out=codes[:].bitcast(FP8X4), scales=scales[:], in_=zs[c][:].rearrange("p j u t -> p (j u t)")
             )
             group = 1 if c == 0 else 2
             for b in ((1, 0) if c >= 3 and c % 2 == 1 else (0, 1)):
@@ -260,19 +258,23 @@ def tile_list_kmer_locus_coverage_kernel(
                             stop=True,
                         )
                     rows = slice(first - 2 * b, first - 2 * b + group)
-                    nc.scalar.copy(staged[b][:, rows, (c - lo) * CHUNK : (c - lo + 1) * CHUNK], acc[:])
+                    dst = staged[b][:, rows, (c - lo) * CHUNK : (c - lo + 1) * CHUNK]
+                    if c == chunks - 1 and b == 1:
+                        nc.vector.tensor_copy(dst, acc[:])
+                    else:
+                        nc.scalar.copy(dst, acc[:])
                     if c + 1 == hi:
                         nc.sync.dma_start(
                             out_view[:, first : first + group, lo * CHUNK : hi * CHUNK], staged[b][:, rows, :]
                         )
 
-        make_pairs(nc.vector, 0, 1, high, base_high)
-        make_pairs(nc.vector, 1, 1, high, base_high, 0)
+        make_pairs(nc.vector, 1, high, base_high, 0, CHUNK)
+        make_pairs(nc.vector, 1, high, base_high, CHUNK, CHUNK + P)
         weave(0)
-        make_pairs(nc.vector, 1, 1, high, base_high, 1)
+        make_pairs(nc.vector, 1, high, base_high, CHUNK + P, 2 * CHUNK)
         tracks(0)
         for c in range(1, chunks):
             weave(c)
             if c + 1 < chunks:
-                make_pairs(nc.vector, c + 1, 1, high, base_high)
+                make_pairs(nc.vector, 1, high, base_high, EDGES[c + 1], EDGES[c + 2])
             tracks(c)

@@ -148,10 +148,10 @@ def tile_list_kmer_locus_coverage_kernel(
                     stop=(a == PASSES - 1),
                 )
 
-        def root(t, lo, hi, slot):
+        def root(t, lo, hi, slot, dst=None):
             mag = placed([P, hi - lo], F32, "mag%d_%d" % (t, lo), 116 + 2 * slot)
             nc.scalar.activation(mag[:], sums[t, lo][:], ACT.Abs)
-            nc.scalar.activation(hs[t][:, lo:hi], mag[:], ACT.Sqrt, bias=floor[:])
+            nc.scalar.activation(hs[t][:, lo:hi] if dst is None else dst, mag[:], ACT.Sqrt, bias=floor[:])
 
         def weigh(engine, t, lo, hi, first):
             engine.tensor_tensor(hs[t][:, lo:hi], hs[t][:, lo:hi], wg[t, first][:, lo - first : hi - first], MULT)
@@ -159,23 +159,40 @@ def tile_list_kmer_locus_coverage_kernel(
         def scatter(t, lo, hi):
             nc.vector.tensor_copy(pages[t][:].indirect(idx2[:, lo // 16 : hi // 16]), hs[t][:, lo:hi])
 
+        first_roots = placed([P, FIRST], F32, "first_roots", 120)
         for u in range(2):
             passes(0, u * P, (u + 1) * P, u, 0, PASSES - 1)
         for u in range(2):
             passes(0, u * P, (u + 1) * P, u, PASSES - 1, PASSES)
-            root(0, u * P, (u + 1) * P, u)
-            weigh(nc.gpsimd, 0, u * P, (u + 1) * P, 0)
+            root(0, u * P, (u + 1) * P, u, first_roots[:, u * P : (u + 1) * P])
+        nc.vector.tensor_tensor(hs[0][:, 0:FIRST], first_roots[:], wg[0, 0], MULT)
         scatter(0, 0, FIRST)
-        pieces = ((1, 0, FIRST), (0, FIRST, HALF), (1, FIRST, HALF), (0, HALF, S), (1, HALF, S))
-        for u, (t, lo, hi) in enumerate(pieces):
-            passes(t, lo, hi, 2 + u, 0, PASSES)
-            root(t, lo, hi, max(u - 1, 0) % 2)
-            weigh(nc.gpsimd, t, lo, hi, lo)
-            scatter(t, lo, hi)
+        passes(1, 0, FIRST, 2, 0, PASSES)
+        root(1, 0, FIRST, 0)
+        second = placed([P, FIRST], F32, "second", 120)
+        nc.gpsimd.tensor_tensor(second[:], hs[1][:, 0:FIRST], wg[1, 0], MULT)
+        nc.vector.tensor_copy(pages[1][:].indirect(idx2[:, 0 : FIRST // 16]), second[:])
+        made = [0]
+
+        def respond(t, lo, hi):
+            passes(t, lo, hi, (3 + made[0]) % BANKS, 0, PASSES)
+            root(t, lo, hi, made[0] % 2)
+            made[0] = made[0] + 1
+
+        for t in range(2):
+            respond(t, FIRST, HALF)
+            weigh(nc.gpsimd, t, FIRST, HALF, FIRST)
+            scatter(t, FIRST, HALF)
+        for lo in (HALF, HALF + FIRST):
+            respond(0, lo, lo + FIRST)
+            weigh(nc.gpsimd, 0, lo, lo + FIRST, HALF)
+        scatter(0, HALF, S)
+        respond(1, HALF, S)
+        weigh(nc.gpsimd, 1, HALF, S, HALF)
+        scatter(1, HALF, S)
         for t in (2, 3):
-            for hf in range(2):
-                passes(t, hf * HALF, (hf + 1) * HALF, (2 * t + hf + 3) % BANKS, 0, PASSES)
-                root(t, hf * HALF, (hf + 1) * HALF, hf)
+            for lo in (0, HALF):
+                respond(t, lo, lo + HALF)
             weigh(nc.gpsimd, t, 0, S, 0)
 
         chunks = len(EDGES) - 1

@@ -76,8 +76,21 @@ def tile_list_kmer_locus_coverage_kernel(
         nc.gpsimd.memset(scale_rows[96:128, :], 0)
         nc.gpsimd.memset(tab_planes[0][:], 0)
 
+        gathered = {}
+
+        def gather_words(a, lo, hi):
+            nc.vector.tensor_copy(
+                gathered[a, lo // HALF][:, lo % HALF : lo % HALF + hi - lo],
+                words[a][:].bitcast(U32).indirect(idx[:, lo // 16 : hi // 16]),
+            )
+
+        gathered[0, 0] = placed([P, HALF], U32, "gathered0_0", 56)
+        gather_words(0, 0, HALF)
         picked_rows = keep.tile([P, S], U8, name="picked_rows", align_bytes=64)
-        nc.vector.tensor_copy(picked_rows[:], scale_rows[:].bitcast(U8).indirect(idx[:]))
+        for lo in (0, HALF):
+            nc.vector.tensor_copy(
+                picked_rows[:, lo : lo + HALF], scale_rows[:].bitcast(U8).indirect(idx[:, lo // 16 : (lo + HALF) // 16])
+            )
 
         def move_scales(hf):
             picked = picked_rows[:, hf * HALF : (hf + 1) * HALF].bitcast(I32)
@@ -89,21 +102,19 @@ def tile_list_kmer_locus_coverage_kernel(
         for t in range(PACK):
             nc.gpsimd.memset(pages[t][:], 0.0)
 
-        gathered = [placed([P, S], U32, "gathered%d" % a, (55, 60, 64)[a]) for a in range(PASSES)]
-
-        def gather_words(a, lo, hi):
-            nc.vector.tensor_copy(
-                gathered[a][:, lo:hi], words[a][:].bitcast(U32).indirect(idx[:, lo // 16 : hi // 16])
-            )
-
-        gather_words(0, 0, S)
+        gathered[0, 1] = placed([P, HALF], U32, "gathered0_1", 54)
+        gather_words(0, HALF, S)
         wkw = placed([P, PACK, PASSES * P], U16, "wkw", 148)
         nc.vector.tensor_copy(wkw[:], wkw_raw[:].bitcast(U16).rearrange("p (m t) -> p t m", t=PACK))
-        wks = placed([P, PACK, PASSES * P], U8, "wks", 151)
+        wks = placed([P, PACK, PASSES * P], U8, "wks", 6)
         nc.vector.tensor_copy(wks[:], wks_raw[:].bitcast(U8).rearrange("p (m t) -> p t m", t=PACK))
         tab_planes.append(placed([P, PASSES, HALF // 4], I32, "tab_planes1", 4))
         nc.gpsimd.memset(tab_planes[1][:], 0)
-        gather_words(1, 0, S)
+        for a in (1, 2):
+            both = placed([P, S], U32, "gathered%d" % a, 56 + 4 * a)
+            gathered[a, 0], gathered[a, 1] = both[:, 0:HALF], both[:, HALF:S]
+            if a == 1:
+                nc.vector.tensor_copy(both[:], words[a][:].bitcast(U32).indirect(idx[:]))
         gather_words(2, 0, FIRST)
         gather_words(2, FIRST, HALF)
         gather_words(2, HALF, S)
@@ -142,7 +153,7 @@ def tile_list_kmer_locus_coverage_kernel(
                     out=acc[:],
                     lhsT=wkw[:, t, a * P : (a + 1) * P].bitcast(U8).bitcast(FP4X4),
                     lhsT_scale=wks[:, t, a * P : (a + 1) * P],
-                    rhs=gathered[a][:, lo:hi].bitcast(FP8X4),
+                    rhs=gathered[a, lo // HALF][:, lo % HALF : lo % HALF + hi - lo].bitcast(FP8X4),
                     rhs_scale=tab_planes[lo // HALF][:, a, :].bitcast(U8)[:, lo % HALF : lo % HALF + hi - lo],
                     start=(a == 0),
                     stop=(a == PASSES - 1),

@@ -19,13 +19,19 @@ MULT = mybir.AluOpType.mult
 P = 128
 PACK = 4
 PASSES = K // (P * PACK)
+STRIPE = 16
 HALF = 512
 FIRST = 256
+CHUNK = 256
+CHUNKS = T2 // CHUNK
 BANKS = 8
 KIB = 1024
+LINE = 4
 QUADRANTS = (0, 2, 1, 3)
-CHUNK = 256
-EDGES = tuple(range(0, T2 + 1, CHUNK))
+SCALE_ROW0 = 48
+LOW_PIECES = ((0, CHUNK), (CHUNK, 3 * CHUNK), (3 * CHUNK, T2))
+HIGH_PIECES = ((0, CHUNK), (CHUNK, 2 * CHUNK), (2 * CHUNK, 4 * CHUNK), (4 * CHUNK, T2))
+LONG_ROWS_FROM = (2, 1)
 
 
 def tile_list_kmer_locus_coverage_kernel(
@@ -42,8 +48,8 @@ def tile_list_kmer_locus_coverage_kernel(
         def placed(shape, dtype, name, kib):
             return mem.tile(shape, dtype, name=name, offset=int(kib * KIB), align_bytes=64)
 
-        idx = keep.tile([P, S // 16], U16, name="idx")
-        idx2 = keep.tile([P, S // 16], U16, name="idx2")
+        idx = keep.tile([P, S // STRIPE], U16, name="idx")
+        idx2 = keep.tile([P, S // STRIPE], U16, name="idx2")
         words = [placed([P, T], I32, "words%d" % a, 16 * a) for a in range(PASSES)]
         scale_rows = placed([P, T // 4], I32, "scale_rows", 52)
         one = keep.tile([P, 1], F32, name="one")
@@ -67,21 +73,27 @@ def tile_list_kmer_locus_coverage_kernel(
                 wk_scales[:, 4 * q : 4 * q + 4, :].bitcast(I32).rearrange("a r c -> r a c"),
             )
         load_words(0)
-        nc.sync.dma_start(scale_rows[48:96, :], tab_scales.bitcast(I32).rearrange("a q c -> q a c"))
+        scale_end = SCALE_ROW0 + 16 * PASSES
+        nc.sync.dma_start(scale_rows[SCALE_ROW0:scale_end, :], tab_scales.bitcast(I32).rearrange("a q c -> q a c"))
         load_words(1)
         load_words(2)
         nc.vector.memset(one[:], 1.0)
         nc.scalar.activation(floor[:], one[:], ACT.Sqrt, scale=2.0**-116)
-        nc.gpsimd.memset(scale_rows[0:48, :], 0)
-        nc.gpsimd.memset(scale_rows[96:128, :], 0)
+        nc.gpsimd.memset(scale_rows[0:SCALE_ROW0, :], 0)
+        nc.gpsimd.memset(scale_rows[scale_end:P, :], 0)
         nc.gpsimd.memset(tab_planes[0][:], 0)
 
         gathered = {}
 
+        def entries(lst, lo, hi):
+            return lst[:, lo // STRIPE : hi // STRIPE]
+
+        def in_half(tile, lo, hi):
+            return tile[:, lo % HALF : lo % HALF + hi - lo]
+
         def gather_words(a, lo, hi):
             nc.vector.tensor_copy(
-                gathered[a, lo // HALF][:, lo % HALF : lo % HALF + hi - lo],
-                words[a][:].bitcast(U32).indirect(idx[:, lo // 16 : hi // 16]),
+                in_half(gathered[a, lo // HALF], lo, hi), words[a][:].bitcast(U32).indirect(entries(idx, lo, hi))
             )
 
         gathered[0, 0] = placed([P, HALF], U32, "gathered0_0", 56)
@@ -89,13 +101,15 @@ def tile_list_kmer_locus_coverage_kernel(
         picked_rows = keep.tile([P, S], U8, name="picked_rows", align_bytes=64)
         for lo in (0, HALF):
             nc.vector.tensor_copy(
-                picked_rows[:, lo : lo + HALF], scale_rows[:].bitcast(U8).indirect(idx[:, lo // 16 : (lo + HALF) // 16])
+                picked_rows[:, lo : lo + HALF], scale_rows[:].bitcast(U8).indirect(entries(idx, lo, lo + HALF))
             )
 
         def move_scales(hf):
             picked = picked_rows[:, hf * HALF : (hf + 1) * HALF].bitcast(I32)
+            rows = 4 * PASSES
             for q in QUADRANTS:
-                nc.sync.dma_start(tab_planes[hf][32 * q : 32 * q + 4], picked[48 + 12 * q : 60 + 12 * q, :])
+                lo = SCALE_ROW0 + rows * q
+                nc.sync.dma_start(tab_planes[hf][32 * q : 32 * q + 4], picked[lo : lo + rows, :])
 
         move_scales(0)
         pages = [placed([P, T2], F32, "page%d" % t, 68 + 8 * t) for t in range(PACK)]
@@ -147,28 +161,28 @@ def tile_list_kmer_locus_coverage_kernel(
         def passes(t, lo, hi, bank, first, last):
             if first == 0:
                 sums[t, lo] = psum.tile([P, hi - lo], F32, name="acc%d_%d" % (t, lo), tag="bank%d" % bank)
-            acc = sums[t, lo]
             for a in range(first, last):
                 nc.tensor.matmul_mx(
-                    out=acc[:],
+                    out=sums[t, lo][:],
                     lhsT=wkw[:, t, a * P : (a + 1) * P].bitcast(U8).bitcast(FP4X4),
                     lhsT_scale=wks[:, t, a * P : (a + 1) * P],
-                    rhs=gathered[a, lo // HALF][:, lo % HALF : lo % HALF + hi - lo].bitcast(FP8X4),
-                    rhs_scale=tab_planes[lo // HALF][:, a, :].bitcast(U8)[:, lo % HALF : lo % HALF + hi - lo],
+                    rhs=in_half(gathered[a, lo // HALF], lo, hi).bitcast(FP8X4),
+                    rhs_scale=in_half(tab_planes[lo // HALF][:, a, :].bitcast(U8), lo, hi),
                     start=(a == 0),
                     stop=(a == PASSES - 1),
                 )
 
-        def root(t, lo, hi, slot, dst=None):
+        def root(t, lo, hi, slot, dst):
             mag = placed([P, hi - lo], F32, "mag%d_%d" % (t, lo), 116 + 2 * slot)
             nc.scalar.activation(mag[:], sums[t, lo][:], ACT.Abs)
-            nc.scalar.activation(hs[t][:, lo:hi] if dst is None else dst, mag[:], ACT.Sqrt, bias=floor[:])
+            nc.scalar.activation(dst, mag[:], ACT.Sqrt, bias=floor[:])
 
-        def weigh(engine, t, lo, hi, first):
-            engine.tensor_tensor(hs[t][:, lo:hi], hs[t][:, lo:hi], wg[t, first][:, lo - first : hi - first], MULT)
+        def weigh(t, lo, hi, loaded_from):
+            weights = wg[t, loaded_from][:, lo - loaded_from : hi - loaded_from]
+            nc.gpsimd.tensor_tensor(hs[t][:, lo:hi], hs[t][:, lo:hi], weights, MULT)
 
-        def scatter(t, lo, hi):
-            nc.vector.tensor_copy(pages[t][:].indirect(idx2[:, lo // 16 : hi // 16]), hs[t][:, lo:hi])
+        def scatter(t, lo, hi, values):
+            nc.vector.tensor_copy(pages[t][:].indirect(entries(idx2, lo, hi)), values)
 
         first_roots = placed([P, FIRST], F32, "first_roots", 120)
         for u in range(2):
@@ -177,36 +191,35 @@ def tile_list_kmer_locus_coverage_kernel(
             passes(0, u * P, (u + 1) * P, u, PASSES - 1, PASSES)
             root(0, u * P, (u + 1) * P, u, first_roots[:, u * P : (u + 1) * P])
         nc.vector.tensor_tensor(hs[0][:, 0:FIRST], first_roots[:], wg[0, 0], MULT)
-        scatter(0, 0, FIRST)
+        scatter(0, 0, FIRST, hs[0][:, 0:FIRST])
         passes(1, 0, FIRST, 2, 0, PASSES)
-        root(1, 0, FIRST, 0)
+        root(1, 0, FIRST, 0, hs[1][:, 0:FIRST])
         second = placed([P, FIRST], F32, "second", 120)
         nc.gpsimd.tensor_tensor(second[:], hs[1][:, 0:FIRST], wg[1, 0], MULT)
-        nc.vector.tensor_copy(pages[1][:].indirect(idx2[:, 0 : FIRST // 16]), second[:])
-        made = [0]
+        scatter(1, 0, FIRST, second[:])
+        later = []
 
         def respond(t, lo, hi):
-            passes(t, lo, hi, (3 + made[0]) % BANKS, 0, PASSES)
-            root(t, lo, hi, made[0] % 2)
-            made[0] = made[0] + 1
+            passes(t, lo, hi, (3 + len(later)) % BANKS, 0, PASSES)
+            root(t, lo, hi, len(later) % 2, hs[t][:, lo:hi])
+            later.append((t, lo))
 
         for t in range(2):
             respond(t, FIRST, HALF)
-            weigh(nc.gpsimd, t, FIRST, HALF, FIRST)
-            scatter(t, FIRST, HALF)
+            weigh(t, FIRST, HALF, FIRST)
+            scatter(t, FIRST, HALF, hs[t][:, FIRST:HALF])
         for lo in (HALF, HALF + FIRST):
             respond(0, lo, lo + FIRST)
-            weigh(nc.gpsimd, 0, lo, lo + FIRST, HALF)
-        scatter(0, HALF, S)
+            weigh(0, lo, lo + FIRST, HALF)
+        scatter(0, HALF, S, hs[0][:, HALF:S])
         respond(1, HALF, S)
-        weigh(nc.gpsimd, 1, HALF, S, HALF)
-        scatter(1, HALF, S)
+        weigh(1, HALF, S, HALF)
+        scatter(1, HALF, S, hs[1][:, HALF:S])
         for t in (2, 3):
             for lo in (0, HALF):
                 respond(t, lo, lo + HALF)
-            weigh(nc.gpsimd, t, 0, S, 0)
+            weigh(t, 0, S, 0)
 
-        chunks = len(EDGES) - 1
         pairs = placed([P, 2, T2, 2], BF16, "pairs", 132)
 
         def lift(dst, t, lo, hi):
@@ -214,9 +227,9 @@ def tile_list_kmer_locus_coverage_kernel(
 
         def make_pairs(engine, u, lifted, rows, lo, hi):
             engine.tensor_tensor(
-                pairs[:, u, lo:hi, :].rearrange("p (c i) t -> p c t i", i=PACK),
-                lifted[:, :, lo:hi].rearrange("p t (c i) -> p c t i", i=PACK),
-                rows[:, :, lo:hi].rearrange("p t (c i) -> p c t i", i=PACK),
+                pairs[:, u, lo:hi, :].rearrange("p (c i) t -> p c t i", i=LINE),
+                lifted[:, :, lo:hi].rearrange("p t (c i) -> p c t i", i=LINE),
+                rows[:, :, lo:hi].rearrange("p t (c i) -> p c t i", i=LINE),
                 MULT,
             )
 
@@ -224,42 +237,44 @@ def tile_list_kmer_locus_coverage_kernel(
         lift(low, 0, 0, T2)
         base_high = placed([P, 2, T2], F32, "base_high", 60)
         nc.sync.dma_start(base_high[:], base_by_plane[:, 2:4, :])
-        for lo, hi in ((0, EDGES[1]), (EDGES[1], EDGES[3]), (EDGES[3], T2)):
+        for lo, hi in LOW_PIECES:
             lift(low, 1, lo, hi)
-        for lo, hi in ((0, EDGES[1]), (EDGES[1], EDGES[3]), (EDGES[3], T2)):
+        for lo, hi in LOW_PIECES:
             make_pairs(nc.gpsimd, 0, low, base_low, lo, hi)
         wo_bf = placed([P, N, PACK], BF16, "wo_bf", 76)
         wo_scales = keep.tile([P, N], U8, name="wo_scales", align_bytes=64)
         nc.scalar.copy(wo_bf[:], wo_raw[:].rearrange("p t n -> p n t"))
-        scatter(2, 0, S)
+        scatter(2, 0, S, hs[2][:, 0:S])
         high = placed([P, 2, T2], F32, "high", 44)
         lift(high, 2, 0, T2)
-        scatter(3, 0, S)
+        scatter(3, 0, S, hs[3][:, 0:S])
         wo_codes = placed([P, N], U32, "wo_codes", 112)
         nc.vector.quantize_mx(
             out=wo_codes[:].bitcast(FP8X4), scales=wo_scales[:], in_=wo_bf[:].rearrange("p n t -> p (n t)")
         )
-        for lo, hi in ((0, EDGES[1]), (EDGES[1], EDGES[2]), (EDGES[2], EDGES[4]), (EDGES[4], T2)):
+        for lo, hi in HIGH_PIECES:
             lift(high, 3, lo, hi)
 
         out_view = out.rearrange("(m p) j -> p m j", p=P)
         zs = {}
-        banks_used = [0]
+        banks = []
         staged = {}
+
+        def make_high_pairs(lo, hi):
+            make_pairs(nc.vector, 1, high, base_high, lo, hi)
 
         def weave(c):
             zs[c] = ring.tile([P, CHUNK, 2, 2], BF16, name="z", align_bytes=64)
             nc.vector.tensor_copy(
                 zs[c][:].rearrange("p (c i) u t -> p c u i t", i=2),
-                pairs[:, :, EDGES[c] : EDGES[c + 1], :].rearrange("p u (c i) t -> p c u i t", i=2),
+                pairs[:, :, c * CHUNK : (c + 1) * CHUNK, :].rearrange("p u (c i) t -> p c u i t", i=2),
             )
 
         def span(c, b):
-            first = 3 - b
-            if c < first:
+            if c < LONG_ROWS_FROM[b]:
                 return c, c + 1
-            lo = c - (c - first) % 2
-            return lo, min(lo + 2, chunks)
+            lo = c - (c - LONG_ROWS_FROM[b]) % 2
+            return lo, min(lo + 2, CHUNKS)
 
         def tracks(c):
             codes = ring.tile([P, CHUNK], U32, name="z_codes", align_bytes=64)
@@ -267,14 +282,15 @@ def tile_list_kmer_locus_coverage_kernel(
             nc.vector.quantize_mx(
                 out=codes[:].bitcast(FP8X4), scales=scales[:], in_=zs[c][:].rearrange("p j u t -> p (j u t)")
             )
-            group = 1 if c == 0 else 2
-            for b in ((1, 0) if c >= 3 and c % 2 == 1 else (0, 1)):
+            completes_long_store = span(c, 1) == (c - 1, c + 1)
+            for b in (1, 0) if completes_long_store else (0, 1):
                 lo, hi = span(c, b)
+                group = 1 if c == 0 or (lo, hi) == (c - 1, c + 1) else 2
                 if c == lo:
                     staged[b] = stage.tile([P, 2, (hi - lo) * CHUNK], F32, name="staged%d_%d" % (c, b), align_bytes=64)
                 for first in range(2 * b, 2 * b + 2, group):
-                    acc = psum.tile([P, group, CHUNK], F32, name="track", tag="bank%d" % (banks_used[0] % BANKS))
-                    banks_used[0] = banks_used[0] + 1
+                    acc = psum.tile([P, group, CHUNK], F32, name="track", tag="bank%d" % (len(banks) % BANKS))
+                    banks.append(acc)
                     for m in range(first, first + group):
                         nc.tensor.matmul_mx(
                             out=acc[:, m - first, :],
@@ -287,7 +303,7 @@ def tile_list_kmer_locus_coverage_kernel(
                         )
                     rows = slice(first - 2 * b, first - 2 * b + group)
                     dst = staged[b][:, rows, (c - lo) * CHUNK : (c - lo + 1) * CHUNK]
-                    if c == chunks - 1 and b == 1:
+                    if c == CHUNKS - 1 and b == 1:
                         nc.vector.tensor_copy(dst, acc[:])
                     else:
                         nc.scalar.copy(dst, acc[:])
@@ -296,13 +312,13 @@ def tile_list_kmer_locus_coverage_kernel(
                             out_view[:, first : first + group, lo * CHUNK : hi * CHUNK], staged[b][:, rows, :]
                         )
 
-        make_pairs(nc.vector, 1, high, base_high, 0, CHUNK)
-        make_pairs(nc.vector, 1, high, base_high, CHUNK, CHUNK + P)
+        make_high_pairs(0, CHUNK)
+        make_high_pairs(CHUNK, CHUNK + CHUNK // 2)
         weave(0)
-        make_pairs(nc.vector, 1, high, base_high, CHUNK + P, 2 * CHUNK)
+        make_high_pairs(CHUNK + CHUNK // 2, 2 * CHUNK)
         tracks(0)
-        for c in range(1, chunks):
+        for c in range(1, CHUNKS):
             weave(c)
-            if c + 1 < chunks:
-                make_pairs(nc.vector, 1, high, base_high, EDGES[c + 1], EDGES[c + 2])
+            if c + 1 < CHUNKS:
+                make_high_pairs((c + 1) * CHUNK, (c + 2) * CHUNK)
             tracks(c)

@@ -25,6 +25,7 @@ FIRST = 256
 CHUNK = 256
 CHUNKS = T2 // CHUNK
 BANKS = 8
+WARM_UPS = 4
 KIB = 1024
 LINE = 4
 QUADRANTS = (0, 2, 1, 3)
@@ -122,6 +123,17 @@ def tile_list_kmer_locus_coverage_kernel(
         nc.vector.tensor_copy(wkw[:], wkw_raw[:].bitcast(U16).rearrange("p (m t) -> p t m", t=PACK))
         wks = placed([P, PACK, PASSES * P], U8, "wks", 6)
         nc.vector.tensor_copy(wks[:], wks_raw[:].bitcast(U8).rearrange("p (m t) -> p t m", t=PACK))
+        unread = psum.tile([P, HALF], F32, name="unread", tag="bank%d" % (BANKS - 1))
+        for u in range(WARM_UPS):
+            nc.tensor.matmul_mx(
+                out=unread[:],
+                lhsT=wkw[:, 0, 0:P].bitcast(U8).bitcast(FP4X4),
+                lhsT_scale=wks[:, 0, 0:P],
+                rhs=gathered[0, 0][:].bitcast(FP8X4),
+                rhs_scale=picked_rows[:, 0:HALF],
+                start=True,
+                stop=True,
+            )
         tab_planes.append(placed([P, PASSES, HALF // 4], I32, "tab_planes1", 4))
         nc.gpsimd.memset(tab_planes[1][:], 0)
         for a in (1, 2):

@@ -55,8 +55,10 @@ def tile_list_kmer_locus_coverage_kernel(
         scale_rows = placed([P, T // 4], I32, "scale_rows", 52)
         one = keep.tile([P, 1], F32, name="one")
         floor = keep.tile([P, 1], F32, name="floor")
-        wkw_raw = keep.tile([P, PASSES * (H // 2)], I32, name="wkw_raw", align_bytes=64)
+        wkw_first = keep.tile([P, (PASSES - 1) * (H // 2)], I32, name="wkw_first", align_bytes=64)
+        wkw_last = keep.tile([P, H // 2], I32, name="wkw_last", align_bytes=64)
         wks_raw = placed([P, PASSES * (H // 4)], I32, "wks_raw", 60)
+        wks_rows = keep.tile([P, PASSES * (H // 4)], I32, name="wks_rows", align_bytes=64)
         tab_planes = [keep.tile([P, PASSES, HALF // 4], I32, name="tab_planes0", align_bytes=64)]
 
         def load_words(a):
@@ -64,20 +66,24 @@ def tile_list_kmer_locus_coverage_kernel(
 
         nc.gpsimd.memset(wks_raw[:], 0)
         nc.sync.dma_start(
-            wkw_raw[:].rearrange("p (a c) -> p a c", a=PASSES), wk_words.bitcast(I32).rearrange("a p c -> p a c")
+            wkw_first[:].rearrange("p (a c) -> p a c", a=PASSES - 1),
+            wk_words[0 : PASSES - 1].bitcast(I32).rearrange("a p c -> p a c"),
         )
-        nc.sync.dma_start(idx[:], offs)
-        nc.sync.dma_start(idx2[:], offs2)
         for q in QUADRANTS:
             nc.sync.dma_start(
-                wks_raw[32 * q : 32 * q + 4, :].rearrange("p (a c) -> p a c", a=PASSES),
+                wks_rows[32 * q : 32 * q + 4, :].rearrange("p (a c) -> p a c", a=PASSES),
                 wk_scales[:, 4 * q : 4 * q + 4, :].bitcast(I32).rearrange("a r c -> r a c"),
             )
+        nc.sync.dma_start(idx[:], offs)
         load_words(0)
+        for q in QUADRANTS:
+            nc.vector.tensor_copy(wks_raw[32 * q : 32 * q + 4, :], wks_rows[32 * q : 32 * q + 4, :])
         scale_end = SCALE_ROW0 + 16 * PASSES
         nc.sync.dma_start(scale_rows[SCALE_ROW0:scale_end, :], tab_scales.bitcast(I32).rearrange("a q c -> q a c"))
         load_words(1)
+        nc.sync.dma_start(idx2[:], offs2)
         load_words(2)
+        nc.sync.dma_start(wkw_last[:], wk_words[PASSES - 1].bitcast(I32))
         nc.vector.memset(one[:], 1.0)
         nc.scalar.activation(floor[:], one[:], ACT.Sqrt, scale=2.0**-116)
         nc.gpsimd.memset(scale_rows[0:SCALE_ROW0, :], 0)
@@ -119,28 +125,39 @@ def tile_list_kmer_locus_coverage_kernel(
 
         gathered[0, 1] = placed([P, HALF], U32, "gathered0_1", 54)
         gather_words(0, HALF, S)
-        wkw = placed([P, PACK, PASSES * P], U16, "wkw", 148)
-        nc.vector.tensor_copy(wkw[:], wkw_raw[:].bitcast(U16).rearrange("p (m t) -> p t m", t=PACK))
-        wks = placed([P, PACK, PASSES * P], U8, "wks", 6)
+        wkw0 = placed([P, PACK, (PASSES - 1) * P], U16, "wkw0", 148)
+        nc.vector.tensor_copy(wkw0[:], wkw_first[:].bitcast(U16).rearrange("p (m t) -> p t m", t=PACK))
+        wkw = {(t, a): wkw0[:, t, a * P : (a + 1) * P] for t in range(PACK) for a in range(PASSES - 1)}
+
+        def deal_rest(t, planes, kib):
+            dealt = placed([P, planes, P], U16, "wkw_last%d" % t, kib)
+            by_plane = wkw_last[:].bitcast(U16).rearrange("p (m t) -> p t m", t=PACK)
+            nc.scalar.copy(dealt[:], by_plane[:, t : t + planes, :])
+            for u in range(planes):
+                wkw[t + u, PASSES - 1] = dealt[:, u, :]
+
+        deal_rest(0, 1, 150)
+        deal_rest(1, 1, 150.25)
+        wks = placed([P, PACK, PASSES * P], U8, "wks", 151)
         nc.vector.tensor_copy(wks[:], wks_raw[:].bitcast(U8).rearrange("p (m t) -> p t m", t=PACK))
-        unread = psum.tile([P, HALF], F32, name="unread", tag="bank%d" % (BANKS - 1))
-        for u in range(WARM_UPS):
-            nc.tensor.matmul_mx(
-                out=unread[:],
-                lhsT=wkw[:, 0, 0:P].bitcast(U8).bitcast(FP4X4),
-                lhsT_scale=wks[:, 0, 0:P],
-                rhs=gathered[0, 0][:].bitcast(FP8X4),
-                rhs_scale=picked_rows[:, 0:HALF],
-                start=True,
-                stop=True,
-            )
         tab_planes.append(placed([P, PASSES, HALF // 4], I32, "tab_planes1", 4))
         nc.gpsimd.memset(tab_planes[1][:], 0)
         for a in (1, 2):
             both = placed([P, S], U32, "gathered%d" % a, 56 + 4 * a)
             gathered[a, 0], gathered[a, 1] = both[:, 0:HALF], both[:, HALF:S]
-            if a == 1:
-                nc.vector.tensor_copy(both[:], words[a][:].bitcast(U32).indirect(idx[:]))
+        gather_words(1, 0, HALF)
+        unread = psum.tile([P, HALF], F32, name="unread", tag="bank%d" % (BANKS - 1))
+        for u in range(WARM_UPS):
+            nc.tensor.matmul_mx(
+                out=unread[:],
+                lhsT=wkw[0, 0].bitcast(U8).bitcast(FP4X4),
+                lhsT_scale=wks[:, 0, 0:P],
+                rhs=gathered[1, 0].bitcast(FP8X4),
+                rhs_scale=picked_rows[:, 0:HALF],
+                start=True,
+                stop=True,
+            )
+        gather_words(1, HALF, S)
         gather_words(2, 0, FIRST)
         gather_words(2, FIRST, HALF)
         gather_words(2, HALF, S)
@@ -176,7 +193,7 @@ def tile_list_kmer_locus_coverage_kernel(
             for a in range(first, last):
                 nc.tensor.matmul_mx(
                     out=sums[t, lo][:],
-                    lhsT=wkw[:, t, a * P : (a + 1) * P].bitcast(U8).bitcast(FP4X4),
+                    lhsT=wkw[t, a].bitcast(U8).bitcast(FP4X4),
                     lhsT_scale=wks[:, t, a * P : (a + 1) * P],
                     rhs=in_half(gathered[a, lo // HALF], lo, hi).bitcast(FP8X4),
                     rhs_scale=in_half(tab_planes[lo // HALF][:, a, :].bitcast(U8), lo, hi),
@@ -184,8 +201,10 @@ def tile_list_kmer_locus_coverage_kernel(
                     stop=(a == PASSES - 1),
                 )
 
+        mag_places = [116, 118]
+
         def root(t, lo, hi, slot, dst):
-            mag = placed([P, hi - lo], F32, "mag%d_%d" % (t, lo), 116 + 2 * slot)
+            mag = placed([P, hi - lo], F32, "mag%d_%d" % (t, lo), mag_places[slot])
             nc.scalar.activation(mag[:], sums[t, lo][:], ACT.Abs)
             nc.scalar.activation(dst, mag[:], ACT.Sqrt, bias=floor[:])
 
@@ -220,6 +239,8 @@ def tile_list_kmer_locus_coverage_kernel(
             respond(t, FIRST, HALF)
             weigh(t, FIRST, HALF, FIRST)
             scatter(t, FIRST, HALF, hs[t][:, FIRST:HALF])
+        deal_rest(2, 2, mag_places[1])
+        mag_places[1] = 121
         for lo in (HALF, HALF + FIRST):
             respond(0, lo, lo + FIRST)
             weigh(0, lo, lo + FIRST, HALF)

@@ -55,18 +55,19 @@ def tile_list_kmer_locus_coverage_kernel(
         scale_rows = placed([P, T // 4], I32, "scale_rows", 52)
         one = keep.tile([P, 1], F32, name="one")
         floor = keep.tile([P, 1], F32, name="floor")
-        wkw_first = keep.tile([P, (PASSES - 1) * (H // 2)], I32, name="wkw_first", align_bytes=64)
+        wk_raw = placed([P, 18 * KIB // 4], I32, "wk_raw", 75)
+        wkw_first = wk_raw[:, 0 : (PASSES - 1) * (H // 2)]
         wkw_last = keep.tile([P, H // 2], I32, name="wkw_last", align_bytes=64)
-        wks_raw = placed([P, PASSES * (H // 4)], I32, "wks_raw", 60)
+        wks_raw = wk_raw[:, 18 * KIB // 4 - PASSES * (H // 4) :]
         wks_rows = keep.tile([P, PASSES * (H // 4)], I32, name="wks_rows", align_bytes=64)
         tab_planes = [keep.tile([P, PASSES, HALF // 4], I32, name="tab_planes0", align_bytes=64)]
 
         def load_words(a):
             nc.sync.dma_start(words[a][:], tab_words[a].rearrange("p t i -> p (t i)").bitcast(I32))
 
-        nc.gpsimd.memset(wks_raw[:], 0)
+        nc.gpsimd.memset(wks_raw, 0)
         nc.sync.dma_start(
-            wkw_first[:].rearrange("p (a c) -> p a c", a=PASSES - 1),
+            wkw_first.rearrange("p (a c) -> p a c", a=PASSES - 1),
             wk_words[0 : PASSES - 1].bitcast(I32).rearrange("a p c -> p a c"),
         )
         for q in QUADRANTS:
@@ -126,7 +127,7 @@ def tile_list_kmer_locus_coverage_kernel(
         gathered[0, 1] = placed([P, HALF], U32, "gathered0_1", 54)
         gather_words(0, HALF, S)
         wkw0 = placed([P, PACK, (PASSES - 1) * P], U16, "wkw0", 148)
-        nc.vector.tensor_copy(wkw0[:], wkw_first[:].bitcast(U16).rearrange("p (m t) -> p t m", t=PACK))
+        nc.vector.tensor_copy(wkw0[:], wkw_first.bitcast(U16).rearrange("p (m t) -> p t m", t=PACK))
         wkw = {(t, a): wkw0[:, t, a * P : (a + 1) * P] for t in range(PACK) for a in range(PASSES - 1)}
 
         def deal_rest(t, planes, kib):
@@ -139,7 +140,7 @@ def tile_list_kmer_locus_coverage_kernel(
         deal_rest(0, 1, 150)
         deal_rest(1, 1, 150.25)
         wks = placed([P, PACK, PASSES * P], U8, "wks", 151)
-        nc.vector.tensor_copy(wks[:], wks_raw[:].bitcast(U8).rearrange("p (m t) -> p t m", t=PACK))
+        nc.vector.tensor_copy(wks[:], wks_raw.bitcast(U8).rearrange("p (m t) -> p t m", t=PACK))
         tab_planes.append(placed([P, PASSES, HALF // 4], I32, "tab_planes1", 4))
         nc.gpsimd.memset(tab_planes[1][:], 0)
         for a in (1, 2):

@@ -243,12 +243,10 @@ def tile_list_kmer_locus_coverage_kernel(
         deal_rest(2, 2, mag_places[1])
         mag_places[1] = 121
         for lo in (HALF, HALF + FIRST):
-            respond(0, lo, lo + FIRST)
-            weigh(0, lo, lo + FIRST, HALF)
-        scatter(0, HALF, S, hs[0][:, HALF:S])
-        respond(1, HALF, S)
-        weigh(1, HALF, S, HALF)
-        scatter(1, HALF, S, hs[1][:, HALF:S])
+            for t in range(2):
+                respond(t, lo, lo + FIRST)
+                weigh(t, lo, lo + FIRST, HALF)
+                scatter(t, lo, lo + FIRST, hs[t][:, lo : lo + FIRST])
         for t in (2, 3):
             for lo in (0, HALF):
                 respond(t, lo, lo + HALF)
@@ -262,19 +260,26 @@ def tile_list_kmer_locus_coverage_kernel(
         def make_pairs(engine, u, lifted, rows, lo, hi):
             engine.tensor_tensor(
                 pairs[:, u, lo:hi, :].rearrange("p (c i) t -> p c t i", i=LINE),
-                lifted[:, :, lo:hi].rearrange("p t (c i) -> p c t i", i=LINE),
+                lifted.rearrange("p t (c i) -> p c t i", i=LINE),
                 rows[:, :, lo:hi].rearrange("p t (c i) -> p c t i", i=LINE),
                 MULT,
             )
 
-        low = placed([P, 2, T2], F32, "low", 116)
-        lift(low, 0, 0, T2)
+        low = {lo: placed([P, 2, hi - lo], F32, "low%d" % lo, 116 + lo * 8 // KIB) for lo, hi in LOW_PIECES}
+
+        def lift_low(t, lo, hi):
+            nc.scalar.activation(low[lo][:, t, :], pages[t][:, lo:hi], ACT.Copy, bias=1.0)
+
+        for lo, hi in LOW_PIECES[:2]:
+            lift_low(0, lo, hi)
+        for lo, hi in LOW_PIECES[:2]:
+            lift_low(1, lo, hi)
+        for t in range(2):
+            lift_low(t, *LOW_PIECES[2])
         base_high = placed([P, 2, T2], F32, "base_high", 60)
         nc.sync.dma_start(base_high[:], base_by_plane[:, 2:4, :])
         for lo, hi in LOW_PIECES:
-            lift(low, 1, lo, hi)
-        for lo, hi in LOW_PIECES:
-            make_pairs(nc.gpsimd, 0, low, base_low, lo, hi)
+            make_pairs(nc.gpsimd, 0, low[lo][:], base_low, lo, hi)
         wo_bf = placed([P, N, PACK], BF16, "wo_bf", 76)
         wo_scales = keep.tile([P, N], U8, name="wo_scales", align_bytes=64)
         nc.scalar.copy(wo_bf[:], wo_raw[:].rearrange("p t n -> p n t"))
@@ -282,7 +287,7 @@ def tile_list_kmer_locus_coverage_kernel(
         high = placed([P, 2, T2], F32, "high", 44)
         lift(high, 2, 0, T2)
         scatter(3, 0, S, hs[3][:, 0:S])
-        wo_codes = placed([P, N], U32, "wo_codes", 112)
+        wo_codes = placed([P, N], U32, "wo_codes", 122)
         nc.vector.quantize_mx(
             out=wo_codes[:].bitcast(FP8X4), scales=wo_scales[:], in_=wo_bf[:].rearrange("p n t -> p (n t)")
         )
@@ -295,7 +300,7 @@ def tile_list_kmer_locus_coverage_kernel(
         staged = {}
 
         def make_high_pairs(lo, hi):
-            make_pairs(nc.vector, 1, high, base_high, lo, hi)
+            make_pairs(nc.vector, 1, high[:, :, lo:hi], base_high, lo, hi)
 
         def weave(c):
             zs[c] = ring.tile([P, CHUNK, 2, 2], BF16, name="z", align_bytes=64)

@@ -25,6 +25,7 @@ FIRST = 256
 CHUNK = 256
 CHUNKS = T2 // CHUNK
 BANKS = 8
+FLOOR = 2.0**-58
 WARM_UPS = 4
 KIB = 1024
 LINE = 4
@@ -146,7 +147,11 @@ def tile_list_kmer_locus_coverage_kernel(
         for a in (1, 2):
             both = placed([P, S], U32, "gathered%d" % a, 56 + 4 * a)
             gathered[a, 0], gathered[a, 1] = both[:, 0:HALF], both[:, HALF:S]
-        gather_words(1, 0, HALF)
+            if a == 1:
+                for lo, hi in ((0, S - FIRST), (S - FIRST, S)):
+                    nc.vector.tensor_copy(
+                        both[:, lo:hi], words[a][:].bitcast(U32).indirect(entries(idx, lo, hi))
+                    )
         unread = psum.tile([P, HALF], F32, name="unread", tag="bank%d" % (BANKS - 1))
         for u in range(WARM_UPS):
             nc.tensor.matmul_mx(
@@ -158,7 +163,6 @@ def tile_list_kmer_locus_coverage_kernel(
                 start=True,
                 stop=True,
             )
-        gather_words(1, HALF, S)
         gather_words(2, 0, FIRST)
         gather_words(2, FIRST, HALF)
         gather_words(2, HALF, S)
@@ -204,10 +208,10 @@ def tile_list_kmer_locus_coverage_kernel(
 
         mag_places = [116, 118]
 
-        def root(t, lo, hi, slot, dst):
+        def root(t, lo, hi, slot, dst, bias=floor[:]):
             mag = placed([P, hi - lo], F32, "mag%d_%d" % (t, lo), mag_places[slot])
             nc.scalar.activation(mag[:], sums[t, lo][:], ACT.Abs)
-            nc.scalar.activation(dst, mag[:], ACT.Sqrt, bias=floor[:])
+            nc.scalar.activation(dst, mag[:], ACT.Sqrt, bias=bias)
 
         def weigh(t, lo, hi, loaded_from):
             weights = wg[t, loaded_from][:, lo - loaded_from : hi - loaded_from]
@@ -218,11 +222,10 @@ def tile_list_kmer_locus_coverage_kernel(
 
         first_roots = placed([P, FIRST], F32, "first_roots", 120)
         for u in range(2):
-            passes(0, u * P, (u + 1) * P, u, 0, PASSES - 1)
-        for u in range(2):
-            passes(0, u * P, (u + 1) * P, u, PASSES - 1, PASSES)
-            root(0, u * P, (u + 1) * P, u, first_roots[:, u * P : (u + 1) * P])
-        nc.vector.tensor_tensor(hs[0][:, 0:FIRST], first_roots[:], wg[0, 0], MULT)
+            half = slice(u * P, (u + 1) * P)
+            passes(0, half.start, half.stop, u, 0, PASSES)
+            root(0, half.start, half.stop, u, first_roots[:, half], FLOOR)
+            nc.vector.tensor_tensor(hs[0][:, half], first_roots[:, half], wg[0, 0][:, half], MULT)
         scatter(0, 0, FIRST, hs[0][:, 0:FIRST])
         passes(1, 0, FIRST, 2, 0, PASSES)
         root(1, 0, FIRST, 0, hs[1][:, 0:FIRST])

from contextlib import ExitStack

import concourse.mybir as mybir

K, T, S, H, T2, N = 1536, 4096, 1024, 512, 2048, 512
FLOPS = 2 * K * H * S + 2 * H * N * T2

F32 = mybir.dt.float32
BF16 = mybir.dt.bfloat16
I32 = mybir.dt.int32
U32 = mybir.dt.uint32
U16 = mybir.dt.uint16
U8 = mybir.dt.uint8
FP8X4 = mybir.dt.float8_e4m3fn_x4
FP4X4 = mybir.dt.float4_e2m1fn_x4
ACT = mybir.ActivationFunctionType
MULT = mybir.AluOpType.mult

P = 128
PACK = 4
PASSES = K // (P * PACK)
STRIPE = 16
HALF = 512
FIRST = 256
CHUNK = 256
CHUNKS = T2 // CHUNK
BANKS = 8
FLOOR = 2.0**-58
WARM_UPS = 4
KIB = 1024
LINE = 4
QUADRANTS = (0, 2, 1, 3)
SCALE_ROW0 = 48
LOW_PIECES = ((0, CHUNK), (CHUNK, 3 * CHUNK), (3 * CHUNK, T2))
HIGH_PIECES = ((0, CHUNK), (CHUNK, 2 * CHUNK), (2 * CHUNK, 4 * CHUNK), (4 * CHUNK, T2))
LONG_ROWS_FROM = (2, 1)


def tile_list_kmer_locus_coverage_kernel(
    tc, tab_words, tab_scales, offs, wk_words, wk_scales, offs2, wgs, base, wo, out
):
    nc = tc.nc
    with ExitStack() as ctx:
        keep = ctx.enter_context(tc.tile_pool(name="keep", bufs=1))
        mem = ctx.enter_context(tc.tile_pool(name="mem", bufs=1))
        stage = ctx.enter_context(tc.tile_pool(name="stage", bufs=1))
        ring = ctx.enter_context(tc.tile_pool(name="ring", bufs=3))
        psum = ctx.enter_context(tc.psum_pool(name="psum", bufs=1))

        def placed(shape, dtype, name, kib):
            return mem.tile(shape, dtype, name=name, offset=int(kib * KIB), align_bytes=64)

        idx = keep.tile([P, S // STRIPE], U16, name="idx")
        idx2 = keep.tile([P, S // STRIPE], U16, name="idx2")
        words = [placed([P, T], I32, "words%d" % a, 16 * a) for a in range(PASSES)]
        scale_rows = placed([P, T // 4], I32, "scale_rows", 52)
        one = keep.tile([P, 1], F32, name="one")
        floor = keep.tile([P, 1], F32, name="floor")
        wk_raw = placed([P, 18 * KIB // 4], I32, "wk_raw", 75)
        wkw_first = wk_raw[:, 0 : (PASSES - 1) * (H // 2)]
        wkw_last = keep.tile([P, H // 2], I32, name="wkw_last", align_bytes=64)
        wks_raw = wk_raw[:, 18 * KIB // 4 - PASSES * (H // 4) :]
        wks_rows = keep.tile([P, PASSES * (H // 4)], I32, name="wks_rows", align_bytes=64)
        tab_planes = [keep.tile([P, PASSES, HALF // 4], I32, name="tab_planes0", align_bytes=64)]

        def load_words(a):
            nc.sync.dma_start(words[a][:], tab_words[a].rearrange("p t i -> p (t i)").bitcast(I32))

        nc.gpsimd.memset(wks_raw, 0)
        nc.sync.dma_start(
            wkw_first.rearrange("p (a c) -> p a c", a=PASSES - 1),
            wk_words[0 : PASSES - 1].bitcast(I32).rearrange("a p c -> p a c"),
        )
        for q in QUADRANTS:
            nc.sync.dma_start(
                wks_rows[32 * q : 32 * q + 4, :].rearrange("p (a c) -> p a c", a=PASSES),
                wk_scales[:, 4 * q : 4 * q + 4, :].bitcast(I32).rearrange("a r c -> r a c"),
            )
        nc.sync.dma_start(idx[:], offs)
        load_words(0)
        for q in QUADRANTS:
            nc.vector.tensor_copy(wks_raw[32 * q : 32 * q + 4, :], wks_rows[32 * q : 32 * q + 4, :])
        scale_end = SCALE_ROW0 + 16 * PASSES
        nc.sync.dma_start(scale_rows[SCALE_ROW0:scale_end, :], tab_scales.bitcast(I32).rearrange("a q c -> q a c"))
        load_words(1)
        nc.sync.dma_start(idx2[:], offs2)
        load_words(2)
        nc.sync.dma_start(wkw_last[:], wk_words[PASSES - 1].bitcast(I32))
        nc.vector.memset(one[:], 1.0)
        nc.scalar.activation(floor[:], one[:], ACT.Sqrt, scale=2.0**-116)
        nc.gpsimd.memset(scale_rows[0:SCALE_ROW0, :], 0)
        nc.gpsimd.memset(scale_rows[scale_end:P, :], 0)
        nc.gpsimd.memset(tab_planes[0][:], 0)

        gathered = {}

        def entries(lst, lo, hi):
            return lst[:, lo // STRIPE : hi // STRIPE]

        def in_half(tile, lo, hi):
            return tile[:, lo % HALF : lo % HALF + hi - lo]

        def gather_words(a, lo, hi):
            nc.vector.tensor_copy(
                in_half(gathered[a, lo // HALF], lo, hi), words[a][:].bitcast(U32).indirect(entries(idx, lo, hi))
            )

        gathered[0, 0] = placed([P, HALF], U32, "gathered0_0", 56)
        gather_words(0, 0, HALF)
        picked_rows = keep.tile([P, S], U8, name="picked_rows", align_bytes=64)
        for lo in (0, HALF):
            nc.vector.tensor_copy(
                picked_rows[:, lo : lo + HALF], scale_rows[:].bitcast(U8).indirect(entries(idx, lo, lo + HALF))
            )

        def move_scales(hf):
            picked = picked_rows[:, hf * HALF : (hf + 1) * HALF].bitcast(I32)
            rows = 4 * PASSES
            for q in QUADRANTS:
                lo = SCALE_ROW0 + rows * q
                nc.sync.dma_start(tab_planes[hf][32 * q : 32 * q + 4], picked[lo : lo + rows, :])

        move_scales(0)
        pages = [placed([P, T2], F32, "page%d" % t, 68 + 8 * t) for t in range(PACK)]
        for t in range(PACK):
            nc.gpsimd.memset(pages[t][:], 0.0)

        gathered[0, 1] = placed([P, HALF], U32, "gathered0_1", 54)
        gather_words(0, HALF, S)
        wkw0 = placed([P, PACK, (PASSES - 1) * P], U16, "wkw0", 148)
        nc.vector.tensor_copy(wkw0[:], wkw_first.bitcast(U16).rearrange("p (m t) -> p t m", t=PACK))
        wkw = {(t, a): wkw0[:, t, a * P : (a + 1) * P] for t in range(PACK) for a in range(PASSES - 1)}

        def deal_rest(t, planes, kib):
            dealt = placed([P, planes, P], U16, "wkw_last%d" % t, kib)
            by_plane = wkw_last[:].bitcast(U16).rearrange("p (m t) -> p t m", t=PACK)
            nc.scalar.copy(dealt[:], by_plane[:, t : t + planes, :])
            for u in range(planes):
                wkw[t + u, PASSES - 1] = dealt[:, u, :]

        deal_rest(0, 1, 150)
        deal_rest(1, 1, 150.25)
        wks = placed([P, PACK, PASSES * P], U8, "wks", 151)
        nc.vector.tensor_copy(wks[:], wks_raw.bitcast(U8).rearrange("p (m t) -> p t m", t=PACK))
        tab_planes.append(placed([P, PASSES, HALF // 4], I32, "tab_planes1", 4))
        nc.gpsimd.memset(tab_planes[1][:], 0)
        for a in (1, 2):
            both = placed([P, S], U32, "gathered%d" % a, 56 + 4 * a)
            gathered[a, 0], gathered[a, 1] = both[:, 0:HALF], both[:, HALF:S]
            if a == 1:
                for lo, hi in ((0, S - FIRST), (S - FIRST, S)):
                    nc.vector.tensor_copy(
                        both[:, lo:hi], words[a][:].bitcast(U32).indirect(entries(idx, lo, hi))
                    )
        unread = psum.tile([P, HALF], F32, name="unread", tag="bank%d" % (BANKS - 1))
        for u in range(WARM_UPS):
            nc.tensor.matmul_mx(
                out=unread[:],
                lhsT=wkw[0, 0].bitcast(U8).bitcast(FP4X4),
                lhsT_scale=wks[:, 0, 0:P],
                rhs=gathered[1, 0].bitcast(FP8X4),
                rhs_scale=picked_rows[:, 0:HALF],
                start=True,
                stop=True,
            )
        gather_words(2, 0, FIRST)
        gather_words(2, FIRST, HALF)
        gather_words(2, HALF, S)

        wgs_by_plane = wgs.rearrange("(g t) j -> g t j", t=PACK)
        wg = {}

        def load_wgs(t, planes, lo, hi, kib):
            piece = placed([P, planes, hi - lo], F32, "wg%d_%d" % (t, lo), kib)
            for q in QUADRANTS:
                nc.sync.dma_start(piece[32 * q : 32 * q + 32], wgs_by_plane[:, t : t + planes, lo:hi])
            for u in range(planes):
                wg[t + u, lo] = piece[:, u, :]

        load_wgs(0, 2, 0, FIRST, 0)
        load_wgs(0, 2, FIRST, HALF, 2)
        move_scales(1)
        load_wgs(0, 2, HALF, S, 16)
        load_wgs(2, 1, 0, S, 20)
        load_wgs(3, 1, 0, S, 24)
        base_by_plane = base.rearrange("(p t) j -> p t j", t=PACK)
        base_low = placed([P, 2, T2], F32, "base_low", 28)
        nc.sync.dma_start(base_low[:], base_by_plane[:, 0:2, :])
        wo_raw = placed([P, PACK, N], F32, "wo_raw", 44)
        nc.sync.dma_start(wo_raw[:], wo.rearrange("(p t) n -> p t n", t=PACK))

        hs = [placed([P, S], F32, "h%d" % t, 100 + 4 * t) for t in range(PACK)]
        sums = {}

        def passes(t, lo, hi, bank, first, last):
            if first == 0:
                sums[t, lo] = psum.tile([P, hi - lo], F32, name="acc%d_%d" % (t, lo), tag="bank%d" % bank)
            for a in range(first, last):
                nc.tensor.matmul_mx(
                    out=sums[t, lo][:],
                    lhsT=wkw[t, a].bitcast(U8).bitcast(FP4X4),
                    lhsT_scale=wks[:, t, a * P : (a + 1) * P],
                    rhs=in_half(gathered[a, lo // HALF], lo, hi).bitcast(FP8X4),
                    rhs_scale=in_half(tab_planes[lo // HALF][:, a, :].bitcast(U8), lo, hi),
                    start=(a == 0),
                    stop=(a == PASSES - 1),
                )

        mag_places = [116, 118]

        def root(t, lo, hi, slot, dst, bias=floor[:]):
            mag = placed([P, hi - lo], F32, "mag%d_%d" % (t, lo), mag_places[slot])
            nc.scalar.activation(mag[:], sums[t, lo][:], ACT.Abs)
            nc.scalar.activation(dst, mag[:], ACT.Sqrt, bias=bias)

        def weigh(t, lo, hi, loaded_from):
            weights = wg[t, loaded_from][:, lo - loaded_from : hi - loaded_from]
            nc.gpsimd.tensor_tensor(hs[t][:, lo:hi], hs[t][:, lo:hi], weights, MULT)

        def scatter(t, lo, hi, values):
            nc.vector.tensor_copy(pages[t][:].indirect(entries(idx2, lo, hi)), values)

        first_roots = placed([P, FIRST], F32, "first_roots", 120)
        for u in range(2):
            half = slice(u * P, (u + 1) * P)
            passes(0, half.start, half.stop, u, 0, PASSES)
            root(0, half.start, half.stop, u, first_roots[:, half], FLOOR)
            nc.vector.tensor_tensor(hs[0][:, half], first_roots[:, half], wg[0, 0][:, half], MULT)
        scatter(0, 0, FIRST, hs[0][:, 0:FIRST])
        passes(1, 0, FIRST, 2, 0, PASSES)
        root(1, 0, FIRST, 0, hs[1][:, 0:FIRST])
        second = placed([P, FIRST], F32, "second", 120)
        nc.gpsimd.tensor_tensor(second[:], hs[1][:, 0:FIRST], wg[1, 0], MULT)
        scatter(1, 0, FIRST, second[:])
        later = []

        def respond(t, lo, hi):
            passes(t, lo, hi, (3 + len(later)) % BANKS, 0, PASSES)
            root(t, lo, hi, len(later) % 2, hs[t][:, lo:hi])
            later.append((t, lo))

        for t in range(2):
            respond(t, FIRST, HALF)
            weigh(t, FIRST, HALF, FIRST)
            scatter(t, FIRST, HALF, hs[t][:, FIRST:HALF])
        deal_rest(2, 2, mag_places[1])
        mag_places[1] = 121
        for lo in (HALF, HALF + FIRST):
            for t in range(2):
                respond(t, lo, lo + FIRST)
                weigh(t, lo, lo + FIRST, HALF)
                scatter(t, lo, lo + FIRST, hs[t][:, lo : lo + FIRST])
        for t in (2, 3):
            for lo in (0, HALF):
                respond(t, lo, lo + HALF)
            weigh(t, 0, S, 0)

        pairs = placed([P, 2, T2, 2], BF16, "pairs", 132)

        def lift(dst, t, lo, hi):
            nc.scalar.activation(dst[:, t % 2, lo:hi], pages[t][:, lo:hi], ACT.Copy, bias=1.0)

        def make_pairs(engine, u, lifted, rows, lo, hi):
            engine.tensor_tensor(
                pairs[:, u, lo:hi, :].rearrange("p (c i) t -> p c t i", i=LINE),
                lifted.rearrange("p t (c i) -> p c t i", i=LINE),
                rows[:, :, lo:hi].rearrange("p t (c i) -> p c t i", i=LINE),
                MULT,
            )

        low = {lo: placed([P, 2, hi - lo], F32, "low%d" % lo, 116 + lo * 8 // KIB) for lo, hi in LOW_PIECES}

        def lift_low(t, lo, hi):
            nc.scalar.activation(low[lo][:, t, :], pages[t][:, lo:hi], ACT.Copy, bias=1.0)

        for lo, hi in LOW_PIECES[:2]:
            lift_low(0, lo, hi)
        for lo, hi in LOW_PIECES[:2]:
            lift_low(1, lo, hi)
        for t in range(2):
            lift_low(t, *LOW_PIECES[2])
        base_high = placed([P, 2, T2], F32, "base_high", 60)
        nc.sync.dma_start(base_high[:], base_by_plane[:, 2:4, :])
        for lo, hi in LOW_PIECES:
            make_pairs(nc.gpsimd, 0, low[lo][:], base_low, lo, hi)
        wo_bf = placed([P, N, PACK], BF16, "wo_bf", 76)
        wo_scales = keep.tile([P, N], U8, name="wo_scales", align_bytes=64)
        nc.scalar.copy(wo_bf[:], wo_raw[:].rearrange("p t n -> p n t"))
        scatter(2, 0, S, hs[2][:, 0:S])
        high = placed([P, 2, T2], F32, "high", 44)
        lift(high, 2, 0, T2)
        scatter(3, 0, S, hs[3][:, 0:S])
        wo_codes = placed([P, N], U32, "wo_codes", 122)
        nc.vector.quantize_mx(
            out=wo_codes[:].bitcast(FP8X4), scales=wo_scales[:], in_=wo_bf[:].rearrange("p n t -> p (n t)")
        )
        for lo, hi in HIGH_PIECES:
            lift(high, 3, lo, hi)

        out_view = out.rearrange("(m p) j -> p m j", p=P)
        zs = {}
        banks = []
        staged = {}

        def make_high_pairs(lo, hi):
            make_pairs(nc.vector, 1, high[:, :, lo:hi], base_high, lo, hi)

        def weave(c):
            zs[c] = ring.tile([P, CHUNK, 2, 2], BF16, name="z", align_bytes=64)
            nc.vector.tensor_copy(
                zs[c][:].rearrange("p (c i) u t -> p c u i t", i=2),
                pairs[:, :, c * CHUNK : (c + 1) * CHUNK, :].rearrange("p u (c i) t -> p c u i t", i=2),
            )

        def span(c, b):
            if c < LONG_ROWS_FROM[b]:
                return c, c + 1
            lo = c - (c - LONG_ROWS_FROM[b]) % 2
            return lo, min(lo + 2, CHUNKS)

        def tracks(c):
            codes = ring.tile([P, CHUNK], U32, name="z_codes", align_bytes=64)
            scales = ring.tile([P, CHUNK], U8, name="z_scales", align_bytes=64)
            nc.vector.quantize_mx(
                out=codes[:].bitcast(FP8X4), scales=scales[:], in_=zs[c][:].rearrange("p j u t -> p (j u t)")
            )
            completes_long_store = span(c, 1) == (c - 1, c + 1)
            for b in (1, 0) if completes_long_store else (0, 1):
                lo, hi = span(c, b)
                group = 1 if c == 0 or (lo, hi) == (c - 1, c + 1) else 2
                if c == lo:
                    staged[b] = stage.tile([P, 2, (hi - lo) * CHUNK], F32, name="staged%d_%d" % (c, b), align_bytes=64)
                for first in range(2 * b, 2 * b + 2, group):
                    acc = psum.tile([P, group, CHUNK], F32, name="track", tag="bank%d" % (len(banks) % BANKS))
                    banks.append(acc)
                    for m in range(first, first + group):
                        nc.tensor.matmul_mx(
                            out=acc[:, m - first, :],
                            lhsT=wo_codes[:, P * m : P * (m + 1)].bitcast(FP8X4),
                            lhsT_scale=wo_scales[:, P * m : P * (m + 1)],
                            rhs=codes[:].bitcast(FP8X4),
                            rhs_scale=scales[:],
                            start=True,
                            stop=True,
                        )
                    rows = slice(first - 2 * b, first - 2 * b + group)
                    dst = staged[b][:, rows, (c - lo) * CHUNK : (c - lo + 1) * CHUNK]
                    if c == CHUNKS - 1 and b == 1:
                        nc.vector.tensor_copy(dst, acc[:])
                    else:
                        nc.scalar.copy(dst, acc[:])
                    if c + 1 == hi:
                        nc.sync.dma_start(
                            out_view[:, first : first + group, lo * CHUNK : hi * CHUNK], staged[b][:, rows, :]
                        )

        make_high_pairs(0, CHUNK)
        make_high_pairs(CHUNK, CHUNK + CHUNK // 2)
        weave(0)
        make_high_pairs(CHUNK + CHUNK // 2, 2 * CHUNK)
        tracks(0)
        for c in range(1, CHUNKS):
            weave(c)
            if c + 1 < CHUNKS:
                make_high_pairs((c + 1) * CHUNK, (c + 2) * CHUNK)
            tracks(c)
